import numpy as np
import ml_dtypes


def mxq(x, axis, fmt="e4m3"):
    dtype, down = {"e4m3": (ml_dtypes.float8_e4m3fn, 7), "e5m2": (ml_dtypes.float8_e5m2, 14)}[fmt]
    v = np.moveaxis(np.asarray(x, np.float32).astype(ml_dtypes.bfloat16).astype(np.float64), axis, -1)
    blocks = v.reshape(v.shape[:-1] + (-1, 32))
    amax = np.abs(blocks).max(-1, keepdims=True)
    byte = np.maximum(np.where(amax > 0, np.frexp(amax)[1] - 1 + 127, 0) - down, 1)
    scale = np.exp2(byte - 127.0)
    codes = (blocks / scale).astype(np.float32).astype(dtype).astype(np.float64)
    return np.moveaxis((codes * scale).reshape(v.shape), -1, axis)


WIDE = False


def mx_kscale(k):
    if not WIDE:
        return np.ones(k)
    levels = np.array([18, -18])
    if k % 512:
        return np.exp2(np.random.permutation(np.resize(levels, k // 32))).repeat(32)
    a = np.empty((k // 512, 16))
    for p in range(k // 512):
        a[p, :8] = np.random.permutation(np.resize(levels, 8))
        for g in range(8):
            far = levels[np.abs(levels - a[p, g]) >= 10]
            a[p, g + 8] = far[np.random.randint(len(far))]
    return np.exp2(a.ravel()).repeat(32)


def f64(x):
    return np.asarray(x).astype(np.float64)


def striped(idx):
    return np.tile(np.asarray(idx).reshape(-1, 16).T, (8, 1)).astype(np.uint16)


def unstriped(offs):
    return offs[:16].T.reshape(-1).astype(np.int64)

def planes(y):
    n, m = y.shape
    v = y.astype(np.float32).astype(ml_dtypes.bfloat16).astype(np.float64).reshape(n // 32, 32, m)
    top = np.abs(v).max(1)
    byte = np.clip(np.where(top > 0, np.frexp(top)[1] - 1 + 127 - 7, 1), 1, 254)
    codes = (v * np.exp2(127.0 - byte)[:, None, :]).reshape(n, m).astype(np.float32).astype(ml_dtypes.float8_e4m3fn).view(np.uint8)
    words = codes.reshape(n // 512, 128, 4, m).transpose(0, 1, 3, 2)
    return np.ascontiguousarray(words), np.ascontiguousarray(byte.astype(np.uint8).reshape(n // 512, 16, m))


def setup_inputs():
    n = np.random.standard_normal
    uni = np.random.uniform
    idx = np.random.permutation(2048)[:512]
    f_f = mx_kscale(512)
    f_r = mx_kscale(512)
    return {
        "W": (n((512, 512)) / np.sqrt(512) * f_f[None, :]).astype(np.float32),
        "xT": (n((512, 512)) * f_r[None, :]).astype(np.float32),
        "G": (n((512, 512)) / np.sqrt(512) / f_r[:, None]).astype(np.float32),
        "hT": (np.tanh(2.0 * n((512, 2048)))).astype(np.float32),
        "cf": (uni(0.75, 1.3, (512, 1)) / f_f[:, None]).astype(np.float32),
        "ts": np.tile(uni(0.75, 1.3, 2048), (128, 1)).astype(np.float32),
        "offs": striped(idx),
    }


def reference(W, xT, G, hT, cf, ts, offs):
    idx = unstriped(offs)
    h = f64(hT)[:, idx]
    ts_i = f64(ts)[:1][:, idx]
    dv = mxq(f64(xT), 1, "e4m3") @ mxq(f64(G), 0, "e5m2")
    dz = f64(cf) * ts_i * dv * (1.0 - np.square(h))
    de = mxq(f64(W), 1, "e4m3") @ mxq(dz, 0, "e5m2")
    out_0 = np.zeros((512, 2048))
    out_0[:, idx] = de
    return (out_0,) + planes(out_0)

@@ -1,0 +1,212 @@
+from contextlib import ExitStack
+
+import concourse.mybir as mybir
+from concourse.masks import make_identity
+
+F32 = mybir.dt.float32
+BF16 = mybir.dt.bfloat16
+I32 = mybir.dt.int32
+U32 = mybir.dt.uint32
+U16 = mybir.dt.uint16
+U8 = mybir.dt.uint8
+E4M3 = mybir.dt.float8_e4m3fn_x4
+E5M2 = mybir.dt.float8_e5m2_x4
+ALU = mybir.AluOpType
+ACT = mybir.ActivationFunctionType
+
+P = 128
+LANES = 4
+K = P * LANES
+SLOTS = 512
+ITEMS = 2048
+FLOPS = 2 * 2 * 512 * 512 * 512
+BYTES = 4 * (3 * 512 * 512 + 512 * ITEMS + 512 + ITEMS) + 2 * P * 32 + 4 * 512 * ITEMS + 512 * ITEMS + 16 * ITEMS
+
+VECTOR_SLOTS = 320
+CHUNK = 512
+
+
+def tile_attend_gtower_tnh_E_pl_kernel(tc, W, xT, G, hT, cf, ts, offs, out_0, out_1, out_2):
+    nc = tc.nc
+    with ExitStack() as ctx:
+        sb = ctx.enter_context(tc.tile_pool(name="sb", bufs=1))
+        turn = ctx.enter_context(tc.psum_pool(name="turn", bufs=4))
+        acc = ctx.enter_context(tc.psum_pool(name="acc", bufs=1))
+
+        offsets = sb.tile([P, SLOTS // 16], U16, name="offsets")
+        nc.sync.dma_start(offsets[:], offs)
+
+        ts_row = sb.tile([1, ITEMS], F32, name="ts_row")
+        nc.sync.dma_start(ts_row[:], ts[0:1, :])
+        ts_window = sb.tile([P, ITEMS], F32, name="ts_window")
+        nc.gpsimd.memset(ts_window[:], 0.0)
+        nc.vector.tensor_copy(ts_window[0:1, :], ts_row[:])
+        cf_lanes = sb.tile([P, LANES], F32, name="cf_lanes")
+        nc.scalar.dma_start(cf_lanes[:], cf.rearrange("(p t) o -> p (t o)", t=LANES))
+
+        x_rows = xT.rearrange("(m t) k -> m t k", t=LANES)
+        w_rows = W.rearrange("(m t) k -> m t k", t=LANES)
+        h_rows = hT.rearrange("(p t) n -> p t n", t=LANES)
+        out_rows = out_0.rearrange("(p t) n -> p t n", t=LANES)
+
+        x_raw = [sb.tile([P, 2, K], F32, name="x_raw%d" % u) for u in range(2)]
+        for u in range(2):
+            nc.sync.dma_start(x_raw[u][:], x_rows[:, 2 * u : 2 * u + 2, :])
+        g_raw = sb.tile([P, LANES, SLOTS], F32, name="g_raw")
+        nc.sync.dma_start(g_raw[:], G.rearrange("(p j) i -> p j i", j=LANES))
+        h_window = [sb.tile([P, ITEMS], F32, name="h_window%d" % t) for t in range(LANES)]
+        w_first = sb.tile([P, K], F32, name="w_first")
+        w_rest = sb.tile([P, LANES - 1, K], F32, name="w_rest")
+        for t in range(LANES):
+            if t == LANES - 1:
+                nc.sync.dma_start(w_first[:], w_rows[:, 0, :])
+            nc.sync.dma_start(h_window[t][:], h_rows[:, t, :])
+        nc.sync.dma_start(w_rest[:], w_rows[:, 1:LANES, :])
+
+        ident = sb.tile([P, P], F32, name="ident")
+        make_identity(nc, ident[:])
+
+        out_window = [sb.tile([P, ITEMS], F32, name="out_window%d" % t) for t in range(LANES)]
+
+        for t in range(LANES):
+            for n0 in range(0, ITEMS, 512):
+                nc.gpsimd.memset(out_window[t][:, n0 : n0 + 512], 0.0)
+
+        def turn_rows(rows, grouped):
+            bank = turn.tile([P, LANES, P], F32, name="bank")
+            for j in range(LANES):
+                nc.tensor.transpose(bank[:, j, :], rows[:, j:K:LANES], ident[:])
+            nc.scalar.copy(grouped, bank[:].rearrange("p j m -> p m j"))
+
+        def quantize(grouped, codes, scales, fmt):
+            nc.vector.quantize_mx(out=codes.bitcast(fmt), scales=scales, in_=grouped.rearrange("p c j -> p (c j)"))
+
+        x_grouped = sb.tile([P, K, LANES], BF16, name="x_grouped", align_bytes=64)
+        x_words = x_grouped[:].rearrange("p c j -> p (c j)").bitcast(F32).rearrange("p (t m u) -> p t m u", t=LANES, u=2)
+        for v in range(2):
+            x_pairs = sb.tile([P, 2, 2, P, 2], BF16, name="x_pairs%d" % v)
+            nc.vector.tensor_copy(
+                x_pairs[:].rearrange("m t u p e -> m t p u e"),
+                x_raw[v][:].rearrange("m t (p u e) -> m t p u e", u=2, e=2),
+            )
+            pair_words = x_pairs[:].rearrange("m t u p e -> m (t u p e)").bitcast(F32)
+            x_bank = turn.tile([P, LANES, P], F32, name="bank")
+            for w in range(LANES):
+                nc.tensor.transpose(x_bank[:, w, :], pair_words[:, w * P : (w + 1) * P], ident[:])
+            nc.scalar.copy(x_words[:, 2 * v : 2 * v + 2, :, :], x_bank[:].rearrange("p (t u) m -> p t m u", u=2))
+
+        ts_listed = sb.tile([P, SLOTS], F32, name="ts_listed")
+        nc.vector.tensor_copy(ts_listed[:], ts_window[:].indirect(offsets[:]))
+        ts_bank = turn.tile([P, LANES, P], F32, name="bank")
+        for b in range(SLOTS // P):
+            nc.tensor.transpose(ts_bank[:, b, :], ts_listed[:, b * P : (b + 1) * P], ident[:])
+        ts_columns = sb.tile([P, SLOTS // P], F32, name="ts_columns")
+        nc.scalar.copy(ts_columns[:], ts_bank[:, :, 0])
+        spread_bank = turn.tile([P, LANES, P], F32, name="bank")
+        for b in range(SLOTS // P):
+            nc.tensor.transpose(spread_bank[:, b, :], ts_columns[:, b : b + 1].to_broadcast([P, P]), ident[:])
+        minus_ts = sb.tile([P, SLOTS], F32, name="minus_ts")
+        nc.scalar.activation(minus_ts[:], spread_bank[:].rearrange("p b n -> p (b n)"), ACT.Copy, scale=-1.0)
+
+        x_codes = sb.tile([P, K], U32, name="x_codes", align_bytes=64)
+        x_scales = sb.tile([P, K], U8, name="x_scales", align_bytes=64)
+        g_grouped = sb.tile([P, SLOTS, LANES], BF16, name="g_grouped", align_bytes=64)
+        g_by_slot = g_raw[:].rearrange("p j i -> p i j")
+        nc.vector.tensor_copy(g_grouped[:, :VECTOR_SLOTS, :], g_by_slot[:, :VECTOR_SLOTS, :])
+        nc.scalar.copy(g_grouped[:, VECTOR_SLOTS:, :], g_by_slot[:, VECTOR_SLOTS:, :])
+        g_codes = sb.tile([P, SLOTS], U32, name="g_codes", align_bytes=64)
+        g_scales = sb.tile([P, SLOTS], U8, name="g_scales", align_bytes=64)
+        quantize(g_grouped[:], g_codes[:], g_scales[:], E5M2)
+        quantize(x_grouped[:], x_codes[:], x_scales[:], E4M3)
+
+        def product(codes, scales, moving_codes, moving_scales, t):
+            sums = acc.tile([P, SLOTS], F32, name="sums%d" % t)
+            nc.tensor.matmul_mx(
+                out=sums[:],
+                lhsT=codes.bitcast(E4M3),
+                lhsT_scale=scales,
+                rhs=moving_codes[:].bitcast(E5M2),
+                rhs_scale=moving_scales[:],
+                start=True,
+                stop=True,
+            )
+            return sums
+
+        dv = {
+            t: product(x_codes[:, t * P : (t + 1) * P], x_scales[:, t * P : (t + 1) * P], g_codes, g_scales, t)
+            for t in range(LANES)
+        }
+
+        dz_lanes = sb.tile([P, LANES, SLOTS], BF16, name="dz_lanes", align_bytes=64)
+        last = LANES - 1
+        for t in range(LANES):
+            h = sb.tile([P, SLOTS], F32, name="h%d" % t, align_bytes=64)
+            nc.vector.tensor_copy(h[:], h_window[t][:].indirect(offsets[:]))
+            h_squared = sb.tile([P, SLOTS], F32, name="h_squared%d" % t, align_bytes=64)
+            nc.scalar.activation(h_squared[:], h[:], ACT.Square)
+            factor = sb.tile([P, SLOTS], F32, name="factor%d" % t)
+            nc.vector.scalar_tensor_tensor(factor[:], dv[t][:], cf_lanes[:, t : t + 1], minus_ts[:], ALU.mult, ALU.mult)
+            nc.vector.scalar_tensor_tensor(dz_lanes[:, t, :], h_squared[:], 1.0, factor[:], ALU.subtract, ALU.mult)
+
+        dz_grouped = sb.tile([P, SLOTS, LANES], BF16, name="dz_grouped", align_bytes=64)
+        dz_by_slot = dz_lanes[:].rearrange("p t i -> p i t")
+        nc.vector.tensor_copy(dz_grouped[:, :VECTOR_SLOTS, :], dz_by_slot[:, :VECTOR_SLOTS, :])
+        nc.scalar.copy(dz_grouped[:, VECTOR_SLOTS:, :], dz_by_slot[:, VECTOR_SLOTS:, :])
+        dz_codes = sb.tile([P, SLOTS], U32, name="dz_codes", align_bytes=64)
+        dz_scales = sb.tile([P, SLOTS], U8, name="dz_scales", align_bytes=64)
+        quantize(dz_grouped[:], dz_codes[:], dz_scales[:], E5M2)
+
+        chunks = ITEMS // CHUNK
+        w_tags = ("w_grouped0", "h3", "h_squared2", "h_squared3")
+        for t in range(LANES):
+            w_grouped = sb.tile([P, P, LANES], BF16, name="w_grouped%d" % t, tag=w_tags[t], align_bytes=64)
+            turn_rows(w_first[:] if t == 0 else w_rest[:, t - 1, :], w_grouped[:])
+            w_codes = sb.tile([P, P], U32, name="w_codes%d" % t, align_bytes=64)
+            w_scales = sb.tile([P, P], U8, name="w_scales%d" % t, align_bytes=64)
+            quantize(w_grouped[:], w_codes[:], w_scales[:], E4M3)
+            de_sums = product(w_codes[:], w_scales[:], dz_codes, dz_scales, t)
+            de = sb.tile([P, SLOTS], F32, name="de%d" % t)
+            nc.scalar.copy(de[:], de_sums[:])
+            nc.vector.tensor_copy(out_window[t][:].indirect(offsets[:]), de[:])
+            nc.sync.dma_start(out_rows[:, t, :], out_window[t][:])
+
+        pair_tags = ("dz_codes", "dz_scales", "w_codes3", "w_scales3")
+        pairs = [
+            sb.tile([P, 2, CHUNK, 2], BF16, name="pairs%d" % c, tag=pair_tags[c], align_bytes=64) for c in range(chunks)
+        ]
+
+        def round_lane(copy, t, c):
+            copy(pairs[c][:, t // 2, :, t % 2], out_window[t][:, c * CHUNK : (c + 1) * CHUNK])
+
+        for t in range(LANES):
+            for c in range(0 if t < 2 else 1, chunks):
+                round_lane(nc.scalar.copy, t, c)
+
+        y_scales = sb.tile([P, ITEMS], U8, name="y_scales", align_bytes=64)
+        words = out_1[0].rearrange("p n t -> p (n t)").bitcast(I32)
+        y_grouped = [sb.tile([P, CHUNK, LANES], BF16, name="y_grouped%d" % c, align_bytes=64) for c in range(chunks)]
+
+        def weave(copy, dtype, c):
+            copy(
+                y_grouped[c][:].rearrange("p n t -> p (n t)").bitcast(dtype).rearrange("p (n u) -> p n u", u=2),
+                pairs[c][:].rearrange("p u n e -> p (u n e)").bitcast(dtype).rearrange("p (u n) -> p n u", u=2),
+            )
+
+        def finish(c):
+            cols = slice(c * CHUNK, (c + 1) * CHUNK)
+            y_codes = sb.tile([P, CHUNK], U32, name="y_codes%d" % c, align_bytes=64)
+            quantize(y_grouped[c][:], y_codes[:], y_scales[:, cols], E4M3)
+            nc.sync.dma_start(words[:, cols], y_codes[:].bitcast(I32))
+
+        round_lane(nc.vector.tensor_copy, 2, 0)
+        round_lane(nc.vector.tensor_copy, 3, 0)
+        for c in range(chunks):
+            if c < chunks - 1:
+                weave(nc.vector.tensor_copy, I32, c)
+            else:
+                weave(nc.scalar.copy, U32, c)
+            finish(c)
+        scale_rows = out_2[0].bitcast(I32)
+        for q in range(4):
+            queue = nc.sync if q % 2 == 0 else nc.scalar
+            queue.dma_start(scale_rows[4 * q : 4 * q + 4, :], y_scales[32 * q : 32 * q + 4, :].bitcast(I32))

@@ -39,7 +39,7 @@ def tile_attend_gtower_tnh_E_pl_kernel(tc, W, xT, G, hT, cf, ts, offs, out_0, ou
         ts_row = sb.tile([1, ITEMS], F32, name="ts_row")
         nc.sync.dma_start(ts_row[:], ts[0:1, :])
         ts_window = sb.tile([P, ITEMS], F32, name="ts_window")
-        nc.gpsimd.memset(ts_window[:], 0.0)
+        nc.vector.memset(ts_window[:], 0.0)
         nc.vector.tensor_copy(ts_window[0:1, :], ts_row[:])
         cf_lanes = sb.tile([P, LANES], F32, name="cf_lanes")
         nc.scalar.dma_start(cf_lanes[:], cf.rearrange("(p t) o -> p (t o)", t=LANES))
@@ -55,45 +55,37 @@ def tile_attend_gtower_tnh_E_pl_kernel(tc, W, xT, G, hT, cf, ts, offs, out_0, ou
         g_raw = sb.tile([P, LANES, SLOTS], F32, name="g_raw")
         nc.sync.dma_start(g_raw[:], G.rearrange("(p j) i -> p j i", j=LANES))
         h_window = [sb.tile([P, ITEMS], F32, name="h_window%d" % t) for t in range(LANES)]
-        w_first = sb.tile([P, K], F32, name="w_first")
-        w_rest = sb.tile([P, LANES - 1, K], F32, name="w_rest")
+        w_raw = sb.tile([P, LANES, K], F32, name="w_raw")
+        nc.sync.dma_start(w_raw[:], w_rows)
         for t in range(LANES):
-            if t == LANES - 1:
-                nc.sync.dma_start(w_first[:], w_rows[:, 0, :])
             nc.sync.dma_start(h_window[t][:], h_rows[:, t, :])
-        nc.sync.dma_start(w_rest[:], w_rows[:, 1:LANES, :])
 
         ident = sb.tile([P, P], F32, name="ident")
         make_identity(nc, ident[:])
 
-        out_window = [sb.tile([P, ITEMS], F32, name="out_window%d" % t) for t in range(LANES)]
-
-        for t in range(LANES):
-            for n0 in range(0, ITEMS, 512):
-                nc.gpsimd.memset(out_window[t][:, n0 : n0 + 512], 0.0)
-
-        def turn_rows(rows, grouped):
-            bank = turn.tile([P, LANES, P], F32, name="bank")
-            for j in range(LANES):
-                nc.tensor.transpose(bank[:, j, :], rows[:, j:K:LANES], ident[:])
-            nc.scalar.copy(grouped, bank[:].rearrange("p j m -> p m j"))
-
         def quantize(grouped, codes, scales, fmt):
             nc.vector.quantize_mx(out=codes.bitcast(fmt), scales=scales, in_=grouped.rearrange("p c j -> p (c j)"))
 
-        x_grouped = sb.tile([P, K, LANES], BF16, name="x_grouped", align_bytes=64)
-        x_words = x_grouped[:].rearrange("p c j -> p (c j)").bitcast(F32).rearrange("p (t m u) -> p t m u", t=LANES, u=2)
-        for v in range(2):
-            x_pairs = sb.tile([P, 2, 2, P, 2], BF16, name="x_pairs%d" % v)
-            nc.vector.tensor_copy(
-                x_pairs[:].rearrange("m t u p e -> m t p u e"),
-                x_raw[v][:].rearrange("m t (p u e) -> m t p u e", u=2, e=2),
-            )
-            pair_words = x_pairs[:].rearrange("m t u p e -> m (t u p e)").bitcast(F32)
-            x_bank = turn.tile([P, LANES, P], F32, name="bank")
-            for w in range(LANES):
-                nc.tensor.transpose(x_bank[:, w, :], pair_words[:, w * P : (w + 1) * P], ident[:])
-            nc.scalar.copy(x_words[:, 2 * v : 2 * v + 2, :, :], x_bank[:].rearrange("p (t u) m -> p t m u", u=2))
+        def turn_matrix(halves, label):
+            grouped = sb.tile([P, K, LANES], BF16, name=label + "_grouped", align_bytes=64)
+            grouped_words = grouped[:].rearrange("p c j -> p (c j)").bitcast(F32)
+            grouped_words = grouped_words.rearrange("p (t m u) -> p t m u", t=LANES, u=2)
+            for v, half in enumerate(halves):
+                rounded = sb.tile([P, 2, 2, P, 2], BF16, name="%s_rounded%d" % (label, v))
+                nc.vector.tensor_copy(
+                    rounded[:].rearrange("m t u p e -> m t p u e"),
+                    half.rearrange("m t (p u e) -> m t p u e", u=2, e=2),
+                )
+                rounded_words = rounded[:].rearrange("m t u p e -> m (t u p e)").bitcast(F32)
+                bank = turn.tile([P, LANES, P], F32, name="bank")
+                for w in range(LANES):
+                    nc.tensor.transpose(bank[:, w, :], rounded_words[:, w * P : (w + 1) * P], ident[:])
+                nc.scalar.copy(
+                    grouped_words[:, 2 * v : 2 * v + 2, :, :], bank[:].rearrange("p (t u) m -> p t m u", u=2)
+                )
+            return grouped
+
+        x_grouped = turn_matrix([x_raw[0][:], x_raw[1][:]], "x")
 
         ts_listed = sb.tile([P, SLOTS], F32, name="ts_listed")
         nc.vector.tensor_copy(ts_listed[:], ts_window[:].indirect(offsets[:]))
@@ -137,6 +129,18 @@ def tile_attend_gtower_tnh_E_pl_kernel(tc, W, xT, G, hT, cf, ts, offs, out_0, ou
             for t in range(LANES)
         }
 
+        w_grouped = turn_matrix([w_raw[:, 0:2, :], w_raw[:, 2:4, :]], "w")
+        w_codes = sb.tile([P, K], U32, name="w_codes", align_bytes=64)
+        w_scales = sb.tile([P, K], U8, name="w_scales", align_bytes=64)
+
+        window_tags = ("g_grouped", "g_codes", "g_scales", "x_codes")
+        out_window = [
+            sb.tile([P, ITEMS], F32, name="out_window%d" % t, tag=window_tags[t], align_bytes=64) for t in range(LANES)
+        ]
+        for t in range(LANES):
+            for n0 in range(0, ITEMS, CHUNK):
+                nc.gpsimd.memset(out_window[t][:, n0 : n0 + CHUNK], 0.0)
+
         dz_lanes = sb.tile([P, LANES, SLOTS], BF16, name="dz_lanes", align_bytes=64)
         last = LANES - 1
         for t in range(LANES):
@@ -148,6 +152,8 @@ def tile_attend_gtower_tnh_E_pl_kernel(tc, W, xT, G, hT, cf, ts, offs, out_0, ou
             nc.vector.scalar_tensor_tensor(factor[:], dv[t][:], cf_lanes[:, t : t + 1], minus_ts[:], ALU.mult, ALU.mult)
             nc.vector.scalar_tensor_tensor(dz_lanes[:, t, :], h_squared[:], 1.0, factor[:], ALU.subtract, ALU.mult)
 
+        quantize(w_grouped[:], w_codes[:], w_scales[:], E4M3)
+
         dz_grouped = sb.tile([P, SLOTS, LANES], BF16, name="dz_grouped", align_bytes=64)
         dz_by_slot = dz_lanes[:].rearrange("p t i -> p i t")
         nc.vector.tensor_copy(dz_grouped[:, :VECTOR_SLOTS, :], dz_by_slot[:, :VECTOR_SLOTS, :])
@@ -157,20 +163,14 @@ def tile_attend_gtower_tnh_E_pl_kernel(tc, W, xT, G, hT, cf, ts, offs, out_0, ou
         quantize(dz_grouped[:], dz_codes[:], dz_scales[:], E5M2)
 
         chunks = ITEMS // CHUNK
-        w_tags = ("w_grouped0", "h3", "h_squared2", "h_squared3")
         for t in range(LANES):
-            w_grouped = sb.tile([P, P, LANES], BF16, name="w_grouped%d" % t, tag=w_tags[t], align_bytes=64)
-            turn_rows(w_first[:] if t == 0 else w_rest[:, t - 1, :], w_grouped[:])
-            w_codes = sb.tile([P, P], U32, name="w_codes%d" % t, align_bytes=64)
-            w_scales = sb.tile([P, P], U8, name="w_scales%d" % t, align_bytes=64)
-            quantize(w_grouped[:], w_codes[:], w_scales[:], E4M3)
-            de_sums = product(w_codes[:], w_scales[:], dz_codes, dz_scales, t)
+            de_sums = product(w_codes[:, t * P : (t + 1) * P], w_scales[:, t * P : (t + 1) * P], dz_codes, dz_scales, t)
             de = sb.tile([P, SLOTS], F32, name="de%d" % t)
             nc.scalar.copy(de[:], de_sums[:])
             nc.vector.tensor_copy(out_window[t][:].indirect(offsets[:]), de[:])
             nc.sync.dma_start(out_rows[:, t, :], out_window[t][:])
 
-        pair_tags = ("dz_codes", "dz_scales", "w_codes3", "w_scales3")
+        pair_tags = ("dz_codes", "dz_scales", "w_codes", "w_scales")
         pairs = [
             sb.tile([P, 2, CHUNK, 2], BF16, name="pairs%d" % c, tag=pair_tags[c], align_bytes=64) for c in range(chunks)
         ]

@@ -24,6 +24,7 @@ BYTES = 4 * (3 * 512 * 512 + 512 * ITEMS + 512 + ITEMS) + 2 * P * 32 + 4 * 512 *
 
 VECTOR_SLOTS = 320
 CHUNK = 512
+HALF = SLOTS // 2
 
 
 def tile_attend_gtower_tnh_E_pl_kernel(tc, W, xT, G, hT, cf, ts, offs, out_0, out_1, out_2):
@@ -40,6 +41,8 @@ def tile_attend_gtower_tnh_E_pl_kernel(tc, W, xT, G, hT, cf, ts, offs, out_0, ou
         nc.sync.dma_start(ts_row[:], ts[0:1, :])
         ts_window = sb.tile([P, ITEMS], F32, name="ts_window")
         nc.vector.memset(ts_window[:], 0.0)
+        out_window = [sb.tile([P, ITEMS], F32, name="out_window0")]
+        nc.vector.memset(out_window[0][:], 0.0)
         nc.vector.tensor_copy(ts_window[0:1, :], ts_row[:])
         cf_lanes = sb.tile([P, LANES], F32, name="cf_lanes")
         nc.scalar.dma_start(cf_lanes[:], cf.rearrange("(p t) o -> p (t o)", t=LANES))
@@ -56,8 +59,9 @@ def tile_attend_gtower_tnh_E_pl_kernel(tc, W, xT, G, hT, cf, ts, offs, out_0, ou
         nc.sync.dma_start(g_raw[:], G.rearrange("(p j) i -> p j i", j=LANES))
         h_window = [sb.tile([P, ITEMS], F32, name="h_window%d" % t) for t in range(LANES)]
         w_raw = sb.tile([P, LANES, K], F32, name="w_raw")
-        nc.sync.dma_start(w_raw[:], w_rows)
         for t in range(LANES):
+            if t == 2:
+                nc.sync.dma_start(w_raw[:], w_rows)
             nc.sync.dma_start(h_window[t][:], h_rows[:, t, :])
 
         ident = sb.tile([P, P], F32, name="ident")
@@ -93,12 +97,7 @@ def tile_attend_gtower_tnh_E_pl_kernel(tc, W, xT, G, hT, cf, ts, offs, out_0, ou
         for b in range(SLOTS // P):
             nc.tensor.transpose(ts_bank[:, b, :], ts_listed[:, b * P : (b + 1) * P], ident[:])
         ts_columns = sb.tile([P, SLOTS // P], F32, name="ts_columns")
-        nc.scalar.copy(ts_columns[:], ts_bank[:, :, 0])
-        spread_bank = turn.tile([P, LANES, P], F32, name="bank")
-        for b in range(SLOTS // P):
-            nc.tensor.transpose(spread_bank[:, b, :], ts_columns[:, b : b + 1].to_broadcast([P, P]), ident[:])
-        minus_ts = sb.tile([P, SLOTS], F32, name="minus_ts")
-        nc.scalar.activation(minus_ts[:], spread_bank[:].rearrange("p b n -> p (b n)"), ACT.Copy, scale=-1.0)
+        nc.scalar.activation(ts_columns[:], ts_bank[:, :, 0], ACT.Copy, scale=-1.0)
 
         x_codes = sb.tile([P, K], U32, name="x_codes", align_bytes=64)
         x_scales = sb.tile([P, K], U8, name="x_scales", align_bytes=64)
@@ -111,60 +110,77 @@ def tile_attend_gtower_tnh_E_pl_kernel(tc, W, xT, G, hT, cf, ts, offs, out_0, ou
         quantize(g_grouped[:], g_codes[:], g_scales[:], E5M2)
         quantize(x_grouped[:], x_codes[:], x_scales[:], E4M3)
 
-        def product(codes, scales, moving_codes, moving_scales, t):
-            sums = acc.tile([P, SLOTS], F32, name="sums%d" % t)
+        blocks = SLOTS // P
+        dv_by_slot = []
+        for b in range(blocks):
+            slots = slice(b * P, (b + 1) * P)
+            slot_sums = turn.tile([P, K], F32, name="bank")
             nc.tensor.matmul_mx(
-                out=sums[:],
-                lhsT=codes.bitcast(E4M3),
-                lhsT_scale=scales,
-                rhs=moving_codes[:].bitcast(E5M2),
-                rhs_scale=moving_scales[:],
+                out=slot_sums[:],
+                lhsT=g_codes[:, slots].bitcast(E5M2),
+                lhsT_scale=g_scales[:, slots],
+                rhs=x_codes[:].bitcast(E4M3),
+                rhs_scale=x_scales[:],
                 start=True,
                 stop=True,
             )
-            return sums
+            scaled = sb.tile([P, K], F32, name="scaled%d" % b)
+            nc.scalar.activation(scaled[:], slot_sums[:], ACT.Copy, scale=ts_columns[:, b : b + 1])
+            dv_by_slot.append(scaled)
 
-        dv = {
-            t: product(x_codes[:, t * P : (t + 1) * P], x_scales[:, t * P : (t + 1) * P], g_codes, g_scales, t)
-            for t in range(LANES)
-        }
+        for tag in ("g_grouped", "g_codes"):
+            window = sb.tile([P, ITEMS], F32, name="window_on_" + tag, tag=tag, align_bytes=64)
+            for n0 in range(0, ITEMS, CHUNK):
+                nc.gpsimd.memset(window[:, n0 : n0 + CHUNK], 0.0)
+            out_window.append(window)
+
+        dz_lanes = [sb.tile([P, LANES, HALF], BF16, name="dz_lanes%d" % v, align_bytes=64) for v in range(2)]
+        for t in range(LANES):
+            turned = acc.tile([P, blocks, P], F32, name="sums%d" % t)
+            for b in range(blocks):
+                nc.tensor.transpose(turned[:, b, :], dv_by_slot[b][:, t * P : (t + 1) * P], ident[:])
+            factor = sb.tile([P, SLOTS], F32, name="factor%d" % t)
+            nc.scalar.activation(
+                factor[:], turned[:].rearrange("p b n -> p (b n)"), ACT.Copy, scale=cf_lanes[:, t : t + 1]
+            )
+            for v in range(2):
+                slots = slice(v * HALF, (v + 1) * HALF)
+                h = sb.tile([P, HALF], F32, name="h%d_%d" % (t, v))
+                nc.vector.tensor_copy(h[:], h_window[t][:].indirect(offsets[:, v * HALF // 16 : (v + 1) * HALF // 16]))
+                h_squared = sb.tile([P, HALF], F32, name="h_squared%d_%d" % (t, v))
+                nc.scalar.activation(h_squared[:], h[:], ACT.Square)
+                nc.vector.scalar_tensor_tensor(
+                    dz_lanes[v][:, t, :], h_squared[:], 1.0, factor[:, slots], ALU.subtract, ALU.mult
+                )
 
         w_grouped = turn_matrix([w_raw[:, 0:2, :], w_raw[:, 2:4, :]], "w")
         w_codes = sb.tile([P, K], U32, name="w_codes", align_bytes=64)
         w_scales = sb.tile([P, K], U8, name="w_scales", align_bytes=64)
-
-        window_tags = ("g_grouped", "g_codes", "g_scales", "x_codes")
-        out_window = [
-            sb.tile([P, ITEMS], F32, name="out_window%d" % t, tag=window_tags[t], align_bytes=64) for t in range(LANES)
-        ]
-        for t in range(LANES):
-            for n0 in range(0, ITEMS, CHUNK):
-                nc.gpsimd.memset(out_window[t][:, n0 : n0 + CHUNK], 0.0)
-
-        dz_lanes = sb.tile([P, LANES, SLOTS], BF16, name="dz_lanes", align_bytes=64)
-        last = LANES - 1
-        for t in range(LANES):
-            h = sb.tile([P, SLOTS], F32, name="h%d" % t, align_bytes=64)
-            nc.vector.tensor_copy(h[:], h_window[t][:].indirect(offsets[:]))
-            h_squared = sb.tile([P, SLOTS], F32, name="h_squared%d" % t, align_bytes=64)
-            nc.scalar.activation(h_squared[:], h[:], ACT.Square)
-            factor = sb.tile([P, SLOTS], F32, name="factor%d" % t)
-            nc.vector.scalar_tensor_tensor(factor[:], dv[t][:], cf_lanes[:, t : t + 1], minus_ts[:], ALU.mult, ALU.mult)
-            nc.vector.scalar_tensor_tensor(dz_lanes[:, t, :], h_squared[:], 1.0, factor[:], ALU.subtract, ALU.mult)
-
         quantize(w_grouped[:], w_codes[:], w_scales[:], E4M3)
 
         dz_grouped = sb.tile([P, SLOTS, LANES], BF16, name="dz_grouped", align_bytes=64)
-        dz_by_slot = dz_lanes[:].rearrange("p t i -> p i t")
-        nc.vector.tensor_copy(dz_grouped[:, :VECTOR_SLOTS, :], dz_by_slot[:, :VECTOR_SLOTS, :])
-        nc.scalar.copy(dz_grouped[:, VECTOR_SLOTS:, :], dz_by_slot[:, VECTOR_SLOTS:, :])
+        nc.scalar.copy(dz_grouped[:, :HALF, :], dz_lanes[0][:].rearrange("p t i -> p i t"))
+        nc.vector.tensor_copy(dz_grouped[:, HALF:, :], dz_lanes[1][:].rearrange("p t i -> p i t"))
         dz_codes = sb.tile([P, SLOTS], U32, name="dz_codes", align_bytes=64)
         dz_scales = sb.tile([P, SLOTS], U8, name="dz_scales", align_bytes=64)
         quantize(dz_grouped[:], dz_codes[:], dz_scales[:], E5M2)
+        last_window = sb.tile([P, ITEMS], F32, name="last_window", tag="dz_grouped", align_bytes=64)
+        nc.vector.memset(last_window[:], 0.0)
+        out_window.append(last_window)
 
         chunks = ITEMS // CHUNK
         for t in range(LANES):
-            de_sums = product(w_codes[:, t * P : (t + 1) * P], w_scales[:, t * P : (t + 1) * P], dz_codes, dz_scales, t)
+            rows = slice(t * P, (t + 1) * P)
+            de_sums = acc.tile([P, SLOTS], F32, name="sums%d" % t)
+            nc.tensor.matmul_mx(
+                out=de_sums[:],
+                lhsT=w_codes[:, rows].bitcast(E4M3),
+                lhsT_scale=w_scales[:, rows],
+                rhs=dz_codes[:].bitcast(E5M2),
+                rhs_scale=dz_scales[:],
+                start=True,
+                stop=True,
+            )
             de = sb.tile([P, SLOTS], F32, name="de%d" % t)
             nc.scalar.copy(de[:], de_sums[:])
             nc.vector.tensor_copy(out_window[t][:].indirect(offsets[:]), de[:])
@@ -182,7 +198,7 @@ def tile_attend_gtower_tnh_E_pl_kernel(tc, W, xT, G, hT, cf, ts, offs, out_0, ou
             for c in range(0 if t < 2 else 1, chunks):
                 round_lane(nc.scalar.copy, t, c)
 
-        y_scales = sb.tile([P, ITEMS], U8, name="y_scales", align_bytes=64)
+        y_scales = sb.tile([P, CHUNK], U8, name="y_scales", align_bytes=64)
         words = out_1[0].rearrange("p n t -> p (n t)").bitcast(I32)
         y_grouped = [sb.tile([P, CHUNK, LANES], BF16, name="y_grouped%d" % c, align_bytes=64) for c in range(chunks)]
 
@@ -195,7 +211,7 @@ def tile_attend_gtower_tnh_E_pl_kernel(tc, W, xT, G, hT, cf, ts, offs, out_0, ou
         def finish(c):
             cols = slice(c * CHUNK, (c + 1) * CHUNK)
             y_codes = sb.tile([P, CHUNK], U32, name="y_codes%d" % c, align_bytes=64)
-            quantize(y_grouped[c][:], y_codes[:], y_scales[:, cols], E4M3)
+            quantize(y_grouped[c][:], y_codes[:], y_scales[4 * c : P, :], E4M3)
             nc.sync.dma_start(words[:, cols], y_codes[:].bitcast(I32))
 
         round_lane(nc.vector.tensor_copy, 2, 0)
@@ -206,7 +222,7 @@ def tile_attend_gtower_tnh_E_pl_kernel(tc, W, xT, G, hT, cf, ts, offs, out_0, ou
             else:
                 weave(nc.scalar.copy, U32, c)
             finish(c)
-        scale_rows = out_2[0].bitcast(I32)
+        scale_rows = out_2[0].bitcast(I32).rearrange("r (c n) -> c r n", c=chunks)
         for q in range(4):
             queue = nc.sync if q % 2 == 0 else nc.scalar
-            queue.dma_start(scale_rows[4 * q : 4 * q + 4, :], y_scales[32 * q : 32 * q + 4, :].bitcast(I32))
+            queue.dma_start(scale_rows[:, 4 * q : 4 * q + 4, :], y_scales[32 * q : 32 * q + 16, :].bitcast(I32))

@@ -19,12 +19,16 @@ LANES = 4
 K = P * LANES
 SLOTS = 512
 ITEMS = 2048
-FLOPS = 2 * 2 * 512 * 512 * 512
-BYTES = 4 * (3 * 512 * 512 + 512 * ITEMS + 512 + ITEMS) + 2 * P * 32 + 4 * 512 * ITEMS + 512 * ITEMS + 16 * ITEMS
+QUADRANTS = 4
+FLOPS = 2 * 2 * K * K * SLOTS
+BYTES = 4 * (3 * K * K + K * ITEMS + K + ITEMS) + 2 * P * SLOTS // 16 + 4 * K * ITEMS + K * ITEMS + 16 * ITEMS
 
+BLOCKS = SLOTS // P
+HALF = SLOTS // 2
 VECTOR_SLOTS = 320
 CHUNK = 512
-HALF = SLOTS // 2
+CHUNKS = ITEMS // CHUNK
+W_BEFORE_LANE = 2
 
 
 def tile_attend_gtower_tnh_E_pl_kernel(tc, W, xT, G, hT, cf, ts, offs, out_0, out_1, out_2):
@@ -52,15 +56,15 @@ def tile_attend_gtower_tnh_E_pl_kernel(tc, W, xT, G, hT, cf, ts, offs, out_0, ou
         h_rows = hT.rearrange("(p t) n -> p t n", t=LANES)
         out_rows = out_0.rearrange("(p t) n -> p t n", t=LANES)
 
-        x_raw = [sb.tile([P, 2, K], F32, name="x_raw%d" % u) for u in range(2)]
-        for u in range(2):
-            nc.sync.dma_start(x_raw[u][:], x_rows[:, 2 * u : 2 * u + 2, :])
+        x_raw = [sb.tile([P, 2, K], F32, name="x_raw%d" % v) for v in range(2)]
+        for v in range(2):
+            nc.sync.dma_start(x_raw[v][:], x_rows[:, 2 * v : 2 * v + 2, :])
         g_raw = sb.tile([P, LANES, SLOTS], F32, name="g_raw")
         nc.sync.dma_start(g_raw[:], G.rearrange("(p j) i -> p j i", j=LANES))
         h_window = [sb.tile([P, ITEMS], F32, name="h_window%d" % t) for t in range(LANES)]
         w_raw = sb.tile([P, LANES, K], F32, name="w_raw")
         for t in range(LANES):
-            if t == 2:
+            if t == W_BEFORE_LANE:
                 nc.sync.dma_start(w_raw[:], w_rows)
             nc.sync.dma_start(h_window[t][:], h_rows[:, t, :])
 
@@ -72,20 +76,20 @@ def tile_attend_gtower_tnh_E_pl_kernel(tc, W, xT, G, hT, cf, ts, offs, out_0, ou
 
         def turn_matrix(halves, label):
             grouped = sb.tile([P, K, LANES], BF16, name=label + "_grouped", align_bytes=64)
-            grouped_words = grouped[:].rearrange("p c j -> p (c j)").bitcast(F32)
-            grouped_words = grouped_words.rearrange("p (t m u) -> p t m u", t=LANES, u=2)
+            grouped_pairs = grouped[:].rearrange("p c j -> p (c j)").bitcast(F32)
+            grouped_pairs = grouped_pairs.rearrange("p (t m u) -> p t m u", t=LANES, u=2)
             for v, half in enumerate(halves):
                 rounded = sb.tile([P, 2, 2, P, 2], BF16, name="%s_rounded%d" % (label, v))
                 nc.vector.tensor_copy(
                     rounded[:].rearrange("m t u p e -> m t p u e"),
                     half.rearrange("m t (p u e) -> m t p u e", u=2, e=2),
                 )
-                rounded_words = rounded[:].rearrange("m t u p e -> m (t u p e)").bitcast(F32)
+                rounded_pairs = rounded[:].rearrange("m t u p e -> m (t u p e)").bitcast(F32)
                 bank = turn.tile([P, LANES, P], F32, name="bank")
-                for w in range(LANES):
-                    nc.tensor.transpose(bank[:, w, :], rounded_words[:, w * P : (w + 1) * P], ident[:])
+                for run in range(LANES):
+                    nc.tensor.transpose(bank[:, run, :], rounded_pairs[:, run * P : (run + 1) * P], ident[:])
                 nc.scalar.copy(
-                    grouped_words[:, 2 * v : 2 * v + 2, :, :], bank[:].rearrange("p (t u) m -> p t m u", u=2)
+                    grouped_pairs[:, 2 * v : 2 * v + 2, :, :], bank[:].rearrange("p (t u) m -> p t m u", u=2)
                 )
             return grouped
 
@@ -94,10 +98,10 @@ def tile_attend_gtower_tnh_E_pl_kernel(tc, W, xT, G, hT, cf, ts, offs, out_0, ou
         ts_listed = sb.tile([P, SLOTS], F32, name="ts_listed")
         nc.vector.tensor_copy(ts_listed[:], ts_window[:].indirect(offsets[:]))
         ts_bank = turn.tile([P, LANES, P], F32, name="bank")
-        for b in range(SLOTS // P):
+        for b in range(BLOCKS):
             nc.tensor.transpose(ts_bank[:, b, :], ts_listed[:, b * P : (b + 1) * P], ident[:])
-        ts_columns = sb.tile([P, SLOTS // P], F32, name="ts_columns")
-        nc.scalar.activation(ts_columns[:], ts_bank[:, :, 0], ACT.Copy, scale=-1.0)
+        minus_ts = sb.tile([P, BLOCKS], F32, name="minus_ts")
+        nc.scalar.activation(minus_ts[:], ts_bank[:, :, 0], ACT.Copy, scale=-1.0)
 
         x_codes = sb.tile([P, K], U32, name="x_codes", align_bytes=64)
         x_scales = sb.tile([P, K], U8, name="x_scales", align_bytes=64)
@@ -110,53 +114,55 @@ def tile_attend_gtower_tnh_E_pl_kernel(tc, W, xT, G, hT, cf, ts, offs, out_0, ou
         quantize(g_grouped[:], g_codes[:], g_scales[:], E5M2)
         quantize(x_grouped[:], x_codes[:], x_scales[:], E4M3)
 
-        blocks = SLOTS // P
         dv_by_slot = []
-        for b in range(blocks):
-            slots = slice(b * P, (b + 1) * P)
+        for b in range(BLOCKS):
+            block = slice(b * P, (b + 1) * P)
             slot_sums = turn.tile([P, K], F32, name="bank")
             nc.tensor.matmul_mx(
                 out=slot_sums[:],
-                lhsT=g_codes[:, slots].bitcast(E5M2),
-                lhsT_scale=g_scales[:, slots],
+                lhsT=g_codes[:, block].bitcast(E5M2),
+                lhsT_scale=g_scales[:, block],
                 rhs=x_codes[:].bitcast(E4M3),
                 rhs_scale=x_scales[:],
                 start=True,
                 stop=True,
             )
             scaled = sb.tile([P, K], F32, name="scaled%d" % b)
-            nc.scalar.activation(scaled[:], slot_sums[:], ACT.Copy, scale=ts_columns[:, b : b + 1])
+            nc.scalar.activation(scaled[:], slot_sums[:], ACT.Copy, scale=minus_ts[:, b : b + 1])
             dv_by_slot.append(scaled)
-
-        for tag in ("g_grouped", "g_codes"):
-            window = sb.tile([P, ITEMS], F32, name="window_on_" + tag, tag=tag, align_bytes=64)
-            for n0 in range(0, ITEMS, CHUNK):
-                nc.gpsimd.memset(window[:, n0 : n0 + CHUNK], 0.0)
-            out_window.append(window)
 
         dz_lanes = [sb.tile([P, LANES, HALF], BF16, name="dz_lanes%d" % v, align_bytes=64) for v in range(2)]
         for t in range(LANES):
-            turned = acc.tile([P, blocks, P], F32, name="sums%d" % t)
-            for b in range(blocks):
+            turned = acc.tile([P, BLOCKS, P], F32, name="sums%d" % t)
+            for b in range(BLOCKS):
                 nc.tensor.transpose(turned[:, b, :], dv_by_slot[b][:, t * P : (t + 1) * P], ident[:])
             factor = sb.tile([P, SLOTS], F32, name="factor%d" % t)
             nc.scalar.activation(
                 factor[:], turned[:].rearrange("p b n -> p (b n)"), ACT.Copy, scale=cf_lanes[:, t : t + 1]
             )
             for v in range(2):
-                slots = slice(v * HALF, (v + 1) * HALF)
                 h = sb.tile([P, HALF], F32, name="h%d_%d" % (t, v))
                 nc.vector.tensor_copy(h[:], h_window[t][:].indirect(offsets[:, v * HALF // 16 : (v + 1) * HALF // 16]))
                 h_squared = sb.tile([P, HALF], F32, name="h_squared%d_%d" % (t, v))
                 nc.scalar.activation(h_squared[:], h[:], ACT.Square)
                 nc.vector.scalar_tensor_tensor(
-                    dz_lanes[v][:, t, :], h_squared[:], 1.0, factor[:, slots], ALU.subtract, ALU.mult
+                    dz_lanes[v][:, t, :],
+                    h_squared[:],
+                    1.0,
+                    factor[:, v * HALF : (v + 1) * HALF],
+                    ALU.subtract,
+                    ALU.mult,
                 )
 
         w_grouped = turn_matrix([w_raw[:, 0:2, :], w_raw[:, 2:4, :]], "w")
         w_codes = sb.tile([P, K], U32, name="w_codes", align_bytes=64)
         w_scales = sb.tile([P, K], U8, name="w_scales", align_bytes=64)
         quantize(w_grouped[:], w_codes[:], w_scales[:], E4M3)
+
+        for tag in ("g_grouped", "g_codes"):
+            window = sb.tile([P, ITEMS], F32, name="window_on_" + tag, tag=tag, align_bytes=64)
+            nc.vector.memset(window[:], 0.0)
+            out_window.append(window)
 
         dz_grouped = sb.tile([P, SLOTS, LANES], BF16, name="dz_grouped", align_bytes=64)
         nc.scalar.copy(dz_grouped[:, :HALF, :], dz_lanes[0][:].rearrange("p t i -> p i t"))
@@ -168,7 +174,6 @@ def tile_attend_gtower_tnh_E_pl_kernel(tc, W, xT, G, hT, cf, ts, offs, out_0, ou
         nc.vector.memset(last_window[:], 0.0)
         out_window.append(last_window)
 
-        chunks = ITEMS // CHUNK
         for t in range(LANES):
             rows = slice(t * P, (t + 1) * P)
             de_sums = acc.tile([P, SLOTS], F32, name="sums%d" % t)
@@ -188,19 +193,19 @@ def tile_attend_gtower_tnh_E_pl_kernel(tc, W, xT, G, hT, cf, ts, offs, out_0, ou
 
         pair_tags = ("dz_codes", "dz_scales", "w_codes", "w_scales")
         pairs = [
-            sb.tile([P, 2, CHUNK, 2], BF16, name="pairs%d" % c, tag=pair_tags[c], align_bytes=64) for c in range(chunks)
+            sb.tile([P, 2, CHUNK, 2], BF16, name="pairs%d" % c, tag=pair_tags[c], align_bytes=64) for c in range(CHUNKS)
         ]
 
         def round_lane(copy, t, c):
             copy(pairs[c][:, t // 2, :, t % 2], out_window[t][:, c * CHUNK : (c + 1) * CHUNK])
 
         for t in range(LANES):
-            for c in range(0 if t < 2 else 1, chunks):
+            for c in range(0 if t < 2 else 1, CHUNKS):
                 round_lane(nc.scalar.copy, t, c)
 
         y_scales = sb.tile([P, CHUNK], U8, name="y_scales", align_bytes=64)
         words = out_1[0].rearrange("p n t -> p (n t)").bitcast(I32)
-        y_grouped = [sb.tile([P, CHUNK, LANES], BF16, name="y_grouped%d" % c, align_bytes=64) for c in range(chunks)]
+        y_grouped = [sb.tile([P, CHUNK, LANES], BF16, name="y_grouped%d" % c, align_bytes=64) for c in range(CHUNKS)]
 
         def weave(copy, dtype, c):
             copy(
@@ -208,21 +213,18 @@ def tile_attend_gtower_tnh_E_pl_kernel(tc, W, xT, G, hT, cf, ts, offs, out_0, ou
                 pairs[c][:].rearrange("p u n e -> p (u n e)").bitcast(dtype).rearrange("p (u n) -> p n u", u=2),
             )
 
-        def finish(c):
-            cols = slice(c * CHUNK, (c + 1) * CHUNK)
-            y_codes = sb.tile([P, CHUNK], U32, name="y_codes%d" % c, align_bytes=64)
-            quantize(y_grouped[c][:], y_codes[:], y_scales[4 * c : P, :], E4M3)
-            nc.sync.dma_start(words[:, cols], y_codes[:].bitcast(I32))
-
         round_lane(nc.vector.tensor_copy, 2, 0)
         round_lane(nc.vector.tensor_copy, 3, 0)
-        for c in range(chunks):
-            if c < chunks - 1:
+        for c in range(CHUNKS):
+            if c < CHUNKS - 1:
                 weave(nc.vector.tensor_copy, I32, c)
             else:
                 weave(nc.scalar.copy, U32, c)
-            finish(c)
-        scale_rows = out_2[0].bitcast(I32).rearrange("r (c n) -> c r n", c=chunks)
-        for q in range(4):
+            y_codes = sb.tile([P, CHUNK], U32, name="y_codes%d" % c, align_bytes=64)
+            quantize(y_grouped[c][:], y_codes[:], y_scales[4 * c : P, :], E4M3)
+            nc.sync.dma_start(words[:, c * CHUNK : (c + 1) * CHUNK], y_codes[:].bitcast(I32))
+
+        scale_rows = out_2[0].bitcast(I32).rearrange("r (c n) -> c r n", c=CHUNKS)
+        for q in range(QUADRANTS):
             queue = nc.sync if q % 2 == 0 else nc.scalar
             queue.dma_start(scale_rows[:, 4 * q : 4 * q + 4, :], y_scales[32 * q : 32 * q + 16, :].bitcast(I32))

@@ -26,9 +26,9 @@ BYTES = 4 * (3 * K * K + K * ITEMS + K + ITEMS) + 2 * P * SLOTS // 16 + 4 * K * 
 BLOCKS = SLOTS // P
 HALF = SLOTS // 2
 VECTOR_SLOTS = 320
+SCALAR_SLOTS = 192
 CHUNK = 512
 CHUNKS = ITEMS // CHUNK
-W_BEFORE_LANE = 2
 
 
 def tile_attend_gtower_tnh_E_pl_kernel(tc, W, xT, G, hT, cf, ts, offs, out_0, out_1, out_2):
@@ -40,14 +40,16 @@ def tile_attend_gtower_tnh_E_pl_kernel(tc, W, xT, G, hT, cf, ts, offs, out_0, ou
 
         offsets = sb.tile([P, SLOTS // 16], U16, name="offsets")
         nc.sync.dma_start(offsets[:], offs)
+        halves_of_list = [offsets[:, v * HALF // 16 : (v + 1) * HALF // 16] for v in range(2)]
 
         ts_row = sb.tile([1, ITEMS], F32, name="ts_row")
         nc.sync.dma_start(ts_row[:], ts[0:1, :])
         ts_window = sb.tile([P, ITEMS], F32, name="ts_window")
         nc.vector.memset(ts_window[:], 0.0)
-        out_window = [sb.tile([P, ITEMS], F32, name="out_window0")]
-        nc.vector.memset(out_window[0][:], 0.0)
-        nc.vector.tensor_copy(ts_window[0:1, :], ts_row[:])
+        out_window = [sb.tile([P, ITEMS], F32, name="out_window%d" % t) for t in range(2)]
+        for window in out_window:
+            nc.vector.memset(window[:], 0.0)
+        nc.scalar.copy(ts_window[0:1, :], ts_row[:])
         cf_lanes = sb.tile([P, LANES], F32, name="cf_lanes")
         nc.scalar.dma_start(cf_lanes[:], cf.rearrange("(p t) o -> p (t o)", t=LANES))
 
@@ -62,11 +64,13 @@ def tile_attend_gtower_tnh_E_pl_kernel(tc, W, xT, G, hT, cf, ts, offs, out_0, ou
         g_raw = sb.tile([P, LANES, SLOTS], F32, name="g_raw")
         nc.sync.dma_start(g_raw[:], G.rearrange("(p j) i -> p j i", j=LANES))
         h_window = [sb.tile([P, ITEMS], F32, name="h_window%d" % t) for t in range(LANES)]
-        w_raw = sb.tile([P, LANES, K], F32, name="w_raw")
-        for t in range(LANES):
-            if t == W_BEFORE_LANE:
-                nc.sync.dma_start(w_raw[:], w_rows)
+        w_first = sb.tile([P, 1, K], F32, name="w_first")
+        w_rest = sb.tile([P, LANES - 1, K], F32, name="w_rest")
+        nc.sync.dma_start(h_window[0][:], h_rows[:, 0, :])
+        nc.sync.dma_start(w_first[:], w_rows[:, 0:1, :])
+        for t in range(1, LANES):
             nc.sync.dma_start(h_window[t][:], h_rows[:, t, :])
+        nc.sync.dma_start(w_rest[:], w_rows[:, 1:LANES, :])
 
         ident = sb.tile([P, P], F32, name="ident")
         make_identity(nc, ident[:])
@@ -74,26 +78,27 @@ def tile_attend_gtower_tnh_E_pl_kernel(tc, W, xT, G, hT, cf, ts, offs, out_0, ou
         def quantize(grouped, codes, scales, fmt):
             nc.vector.quantize_mx(out=codes.bitcast(fmt), scales=scales, in_=grouped.rearrange("p c j -> p (c j)"))
 
-        def turn_matrix(halves, label):
-            grouped = sb.tile([P, K, LANES], BF16, name=label + "_grouped", align_bytes=64)
-            grouped_pairs = grouped[:].rearrange("p c j -> p (c j)").bitcast(F32)
-            grouped_pairs = grouped_pairs.rearrange("p (t m u) -> p t m u", t=LANES, u=2)
-            for v, half in enumerate(halves):
-                rounded = sb.tile([P, 2, 2, P, 2], BF16, name="%s_rounded%d" % (label, v))
-                nc.vector.tensor_copy(
-                    rounded[:].rearrange("m t u p e -> m t p u e"),
-                    half.rearrange("m t (p u e) -> m t p u e", u=2, e=2),
-                )
-                rounded_pairs = rounded[:].rearrange("m t u p e -> m (t u p e)").bitcast(F32)
-                bank = turn.tile([P, LANES, P], F32, name="bank")
-                for run in range(LANES):
-                    nc.tensor.transpose(bank[:, run, :], rounded_pairs[:, run * P : (run + 1) * P], ident[:])
-                nc.scalar.copy(
-                    grouped_pairs[:, 2 * v : 2 * v + 2, :, :], bank[:].rearrange("p (t u) m -> p t m u", u=2)
-                )
-            return grouped
+        def round_rows(rounded, raw):
+            nc.vector.tensor_copy(
+                rounded.rearrange("m t u p e -> m t p u e"), raw.rearrange("m t (p u e) -> m t p u e", u=2, e=2)
+            )
 
-        x_grouped = turn_matrix([x_raw[0][:], x_raw[1][:]], "x")
+        def turn_rows(grouped, rounded, lanes):
+            rounded_pairs = rounded.rearrange("m t u p e -> m (t u p e)").bitcast(F32)
+            grouped_pairs = grouped.rearrange("p c j -> p (c j)").bitcast(F32)
+            bank = turn.tile([P, LANES, P], F32, name="bank")
+            for run in range(2 * lanes):
+                nc.tensor.transpose(bank[:, run, :], rounded_pairs[:, run * P : (run + 1) * P], ident[:])
+            nc.scalar.copy(
+                grouped_pairs.rearrange("p (t m u) -> p t m u", t=lanes, u=2),
+                bank[:, 0 : 2 * lanes, :].rearrange("p (t u) m -> p t m u", u=2),
+            )
+
+        x_grouped = sb.tile([P, K, LANES], BF16, name="x_grouped", align_bytes=64)
+        for v in range(2):
+            x_rounded = sb.tile([P, 2, 2, P, 2], BF16, name="x_rounded%d" % v)
+            round_rows(x_rounded[:], x_raw[v][:])
+            turn_rows(x_grouped[:, 2 * v * P : 2 * (v + 1) * P, :], x_rounded[:], 2)
 
         ts_listed = sb.tile([P, SLOTS], F32, name="ts_listed")
         nc.vector.tensor_copy(ts_listed[:], ts_window[:].indirect(offsets[:]))
@@ -105,6 +110,7 @@ def tile_attend_gtower_tnh_E_pl_kernel(tc, W, xT, G, hT, cf, ts, offs, out_0, ou
 
         x_codes = sb.tile([P, K], U32, name="x_codes", align_bytes=64)
         x_scales = sb.tile([P, K], U8, name="x_scales", align_bytes=64)
+        quantize(x_grouped[:], x_codes[:], x_scales[:], E4M3)
         g_grouped = sb.tile([P, SLOTS, LANES], BF16, name="g_grouped", align_bytes=64)
         g_by_slot = g_raw[:].rearrange("p j i -> p i j")
         nc.vector.tensor_copy(g_grouped[:, :VECTOR_SLOTS, :], g_by_slot[:, :VECTOR_SLOTS, :])
@@ -112,7 +118,6 @@ def tile_attend_gtower_tnh_E_pl_kernel(tc, W, xT, G, hT, cf, ts, offs, out_0, ou
         g_codes = sb.tile([P, SLOTS], U32, name="g_codes", align_bytes=64)
         g_scales = sb.tile([P, SLOTS], U8, name="g_scales", align_bytes=64)
         quantize(g_grouped[:], g_codes[:], g_scales[:], E5M2)
-        quantize(x_grouped[:], x_codes[:], x_scales[:], E4M3)
 
         dv_by_slot = []
         for b in range(BLOCKS):
@@ -128,9 +133,14 @@ def tile_attend_gtower_tnh_E_pl_kernel(tc, W, xT, G, hT, cf, ts, offs, out_0, ou
                 stop=True,
             )
             scaled = sb.tile([P, K], F32, name="scaled%d" % b)
-            nc.scalar.activation(scaled[:], slot_sums[:], ACT.Copy, scale=minus_ts[:, b : b + 1])
+            if b % 2 == 0:
+                nc.scalar.activation(scaled[:], slot_sums[:], ACT.Copy, scale=minus_ts[:, b : b + 1])
+            else:
+                nc.vector.tensor_scalar_mul(scaled[:], slot_sums[:], minus_ts[:, b : b + 1])
             dv_by_slot.append(scaled)
 
+        w_codes = sb.tile([P, K], U32, name="w_codes", align_bytes=64)
+        w_scales = sb.tile([P, K], U8, name="w_scales", align_bytes=64)
         dz_lanes = [sb.tile([P, LANES, HALF], BF16, name="dz_lanes%d" % v, align_bytes=64) for v in range(2)]
         for t in range(LANES):
             turned = acc.tile([P, BLOCKS, P], F32, name="sums%d" % t)
@@ -140,41 +150,41 @@ def tile_attend_gtower_tnh_E_pl_kernel(tc, W, xT, G, hT, cf, ts, offs, out_0, ou
             nc.scalar.activation(
                 factor[:], turned[:].rearrange("p b n -> p (b n)"), ACT.Copy, scale=cf_lanes[:, t : t + 1]
             )
-            for v in range(2):
-                h = sb.tile([P, HALF], F32, name="h%d_%d" % (t, v))
-                nc.vector.tensor_copy(h[:], h_window[t][:].indirect(offsets[:, v * HALF // 16 : (v + 1) * HALF // 16]))
-                h_squared = sb.tile([P, HALF], F32, name="h_squared%d_%d" % (t, v))
+            squares = []
+            if t < LANES - 1:
+                h = sb.tile([P, SLOTS], F32, name="h%d" % t)
+                nc.vector.tensor_copy(h[:], h_window[t][:].indirect(offsets[:]))
+                h_squared = sb.tile([P, SLOTS], F32, name="h_squared%d" % t)
                 nc.scalar.activation(h_squared[:], h[:], ACT.Square)
+                squares = [h_squared[:, :HALF], h_squared[:, HALF:]]
+            else:
+                for v in range(2):
+                    h = sb.tile([P, HALF], F32, name="h_last%d" % v)
+                    nc.vector.tensor_copy(h[:], h_window[t][:].indirect(halves_of_list[v]))
+                    h_squared = sb.tile([P, HALF], F32, name="h_last_squared%d" % v)
+                    nc.scalar.activation(h_squared[:], h[:], ACT.Square)
+                    squares.append(h_squared[:])
+            for v in range(2):
                 nc.vector.scalar_tensor_tensor(
-                    dz_lanes[v][:, t, :],
-                    h_squared[:],
-                    1.0,
-                    factor[:, v * HALF : (v + 1) * HALF],
-                    ALU.subtract,
-                    ALU.mult,
+                    dz_lanes[v][:, t, :], squares[v], 1.0, factor[:, v * HALF : (v + 1) * HALF], ALU.subtract, ALU.mult
                 )
-
-        w_grouped = turn_matrix([w_raw[:, 0:2, :], w_raw[:, 2:4, :]], "w")
-        w_codes = sb.tile([P, K], U32, name="w_codes", align_bytes=64)
-        w_scales = sb.tile([P, K], U8, name="w_scales", align_bytes=64)
-        quantize(w_grouped[:], w_codes[:], w_scales[:], E4M3)
-
-        for tag in ("g_grouped", "g_codes"):
-            window = sb.tile([P, ITEMS], F32, name="window_on_" + tag, tag=tag, align_bytes=64)
-            nc.vector.memset(window[:], 0.0)
-            out_window.append(window)
+            if t == 1:
+                first_rounded = sb.tile([P, 1, 2, P, 2], BF16, name="first_rounded")
+                round_rows(first_rounded[:], w_first[:])
+                first_grouped = sb.tile([P, P, LANES], BF16, name="first_grouped", align_bytes=64)
+                turn_rows(first_grouped[:], first_rounded[:], 1)
+                quantize(first_grouped[:], w_codes[:, :P], w_scales[:, :P], E4M3)
 
         dz_grouped = sb.tile([P, SLOTS, LANES], BF16, name="dz_grouped", align_bytes=64)
-        nc.scalar.copy(dz_grouped[:, :HALF, :], dz_lanes[0][:].rearrange("p t i -> p i t"))
-        nc.vector.tensor_copy(dz_grouped[:, HALF:, :], dz_lanes[1][:].rearrange("p t i -> p i t"))
+        dz_by_slot = [lanes[:].rearrange("p t i -> p i t") for lanes in dz_lanes]
+        nc.scalar.copy(dz_grouped[:, :SCALAR_SLOTS, :], dz_by_slot[0][:, :SCALAR_SLOTS, :])
+        nc.vector.tensor_copy(dz_grouped[:, SCALAR_SLOTS:HALF, :], dz_by_slot[0][:, SCALAR_SLOTS:, :])
+        nc.vector.tensor_copy(dz_grouped[:, HALF:, :], dz_by_slot[1])
         dz_codes = sb.tile([P, SLOTS], U32, name="dz_codes", align_bytes=64)
         dz_scales = sb.tile([P, SLOTS], U8, name="dz_scales", align_bytes=64)
         quantize(dz_grouped[:], dz_codes[:], dz_scales[:], E5M2)
-        last_window = sb.tile([P, ITEMS], F32, name="last_window", tag="dz_grouped", align_bytes=64)
-        nc.vector.memset(last_window[:], 0.0)
-        out_window.append(last_window)
 
-        for t in range(LANES):
+        def second_product(t):
             rows = slice(t * P, (t + 1) * P)
             de_sums = acc.tile([P, SLOTS], F32, name="sums%d" % t)
             nc.tensor.matmul_mx(
@@ -186,6 +196,32 @@ def tile_attend_gtower_tnh_E_pl_kernel(tc, W, xT, G, hT, cf, ts, offs, out_0, ou
                 start=True,
                 stop=True,
             )
+            return de_sums
+
+        first_sums = second_product(0)
+        de_first = sb.tile([P, HALF], F32, name="de_first")
+        nc.scalar.copy(de_first[:], first_sums[:, :HALF])
+        rest_rounded = sb.tile([P, LANES - 1, 2, P, 2], BF16, name="rest_rounded", tag="dz_grouped", align_bytes=64)
+        round_rows(rest_rounded[:, 0:1], w_rest[:, 0:1, :])
+        round_rows(rest_rounded[:, 1:3], w_rest[:, 1:3, :])
+        nc.vector.tensor_copy(out_window[0][:].indirect(halves_of_list[0]), de_first[:])
+        rest_grouped = sb.tile([P, K - P, LANES], BF16, name="rest_grouped", align_bytes=64)
+        turn_rows(rest_grouped[:, :P, :], rest_rounded[:, 0:1], 1)
+        turn_rows(rest_grouped[:, P:, :], rest_rounded[:, 1:3], 2)
+        quantize(rest_grouped[:, :P, :], w_codes[:, P : 2 * P], w_scales[:, P : 2 * P], E4M3)
+        quantize(rest_grouped[:, P:, :], w_codes[:, 2 * P :], w_scales[:, 2 * P :], E4M3)
+        de_second = sb.tile([P, HALF], F32, name="de_second", tag="dz_grouped", align_bytes=64)
+        nc.scalar.copy(de_second[:], first_sums[:, HALF:])
+        nc.vector.tensor_copy(out_window[0][:].indirect(halves_of_list[1]), de_second[:])
+        nc.sync.dma_start(out_rows[:, 0, :], out_window[0][:])
+
+        for tag in ("rest_grouped", "dz_grouped"):
+            window = sb.tile([P, ITEMS], F32, name="window_on_" + tag, tag=tag, align_bytes=64)
+            nc.gpsimd.memset(window[:], 0.0)
+            out_window.append(window)
+
+        for t in range(1, LANES):
+            de_sums = second_product(t)
             de = sb.tile([P, SLOTS], F32, name="de%d" % t)
             nc.scalar.copy(de[:], de_sums[:])
             nc.vector.tensor_copy(out_window[t][:].indirect(offsets[:]), de[:])

@@ -217,7 +217,7 @@ def tile_attend_gtower_tnh_E_pl_kernel(tc, W, xT, G, hT, cf, ts, offs, out_0, ou
 
         for tag in ("rest_grouped", "dz_grouped"):
             window = sb.tile([P, ITEMS], F32, name="window_on_" + tag, tag=tag, align_bytes=64)
-            nc.gpsimd.memset(window[:], 0.0)
+            nc.vector.memset(window[:], 0.0)
             out_window.append(window)
 
         for t in range(1, LANES):

@@ -46,9 +46,8 @@ def tile_attend_gtower_tnh_E_pl_kernel(tc, W, xT, G, hT, cf, ts, offs, out_0, ou
         nc.sync.dma_start(ts_row[:], ts[0:1, :])
         ts_window = sb.tile([P, ITEMS], F32, name="ts_window")
         nc.vector.memset(ts_window[:], 0.0)
-        out_window = [sb.tile([P, ITEMS], F32, name="out_window%d" % t) for t in range(2)]
-        for window in out_window:
-            nc.vector.memset(window[:], 0.0)
+        out_window = [sb.tile([P, ITEMS], F32, name="out_window0")]
+        nc.vector.memset(out_window[0][:], 0.0)
         nc.scalar.copy(ts_window[0:1, :], ts_row[:])
         cf_lanes = sb.tile([P, LANES], F32, name="cf_lanes")
         nc.scalar.dma_start(cf_lanes[:], cf.rearrange("(p t) o -> p (t o)", t=LANES))
@@ -66,9 +65,8 @@ def tile_attend_gtower_tnh_E_pl_kernel(tc, W, xT, G, hT, cf, ts, offs, out_0, ou
         h_window = [sb.tile([P, ITEMS], F32, name="h_window%d" % t) for t in range(LANES)]
         w_first = sb.tile([P, 1, K], F32, name="w_first")
         w_rest = sb.tile([P, LANES - 1, K], F32, name="w_rest")
-        nc.sync.dma_start(h_window[0][:], h_rows[:, 0, :])
         nc.sync.dma_start(w_first[:], w_rows[:, 0:1, :])
-        for t in range(1, LANES):
+        for t in range(LANES):
             nc.sync.dma_start(h_window[t][:], h_rows[:, t, :])
         nc.sync.dma_start(w_rest[:], w_rows[:, 1:LANES, :])
 
@@ -78,10 +76,8 @@ def tile_attend_gtower_tnh_E_pl_kernel(tc, W, xT, G, hT, cf, ts, offs, out_0, ou
         def quantize(grouped, codes, scales, fmt):
             nc.vector.quantize_mx(out=codes.bitcast(fmt), scales=scales, in_=grouped.rearrange("p c j -> p (c j)"))
 
-        def round_rows(rounded, raw):
-            nc.vector.tensor_copy(
-                rounded.rearrange("m t u p e -> m t p u e"), raw.rearrange("m t (p u e) -> m t p u e", u=2, e=2)
-            )
+        def round_rows(copy, rounded, raw):
+            copy(rounded.rearrange("m t u p e -> m t p u e"), raw.rearrange("m t (p u e) -> m t p u e", u=2, e=2))
 
         def turn_rows(grouped, rounded, lanes):
             rounded_pairs = rounded.rearrange("m t u p e -> m (t u p e)").bitcast(F32)
@@ -97,7 +93,7 @@ def tile_attend_gtower_tnh_E_pl_kernel(tc, W, xT, G, hT, cf, ts, offs, out_0, ou
         x_grouped = sb.tile([P, K, LANES], BF16, name="x_grouped", align_bytes=64)
         for v in range(2):
             x_rounded = sb.tile([P, 2, 2, P, 2], BF16, name="x_rounded%d" % v)
-            round_rows(x_rounded[:], x_raw[v][:])
+            round_rows(nc.vector.tensor_copy, x_rounded[:], x_raw[v][:])
             turn_rows(x_grouped[:, 2 * v * P : 2 * (v + 1) * P, :], x_rounded[:], 2)
 
         ts_listed = sb.tile([P, SLOTS], F32, name="ts_listed")
@@ -113,11 +109,25 @@ def tile_attend_gtower_tnh_E_pl_kernel(tc, W, xT, G, hT, cf, ts, offs, out_0, ou
         quantize(x_grouped[:], x_codes[:], x_scales[:], E4M3)
         g_grouped = sb.tile([P, SLOTS, LANES], BF16, name="g_grouped", align_bytes=64)
         g_by_slot = g_raw[:].rearrange("p j i -> p i j")
-        nc.vector.tensor_copy(g_grouped[:, :VECTOR_SLOTS, :], g_by_slot[:, :VECTOR_SLOTS, :])
+        nc.vector.tensor_copy(g_grouped[:, :HALF, :], g_by_slot[:, :HALF, :])
+        nc.vector.tensor_copy(g_grouped[:, HALF:VECTOR_SLOTS, :], g_by_slot[:, HALF:VECTOR_SLOTS, :])
         nc.scalar.copy(g_grouped[:, VECTOR_SLOTS:, :], g_by_slot[:, VECTOR_SLOTS:, :])
         g_codes = sb.tile([P, SLOTS], U32, name="g_codes", align_bytes=64)
         g_scales = sb.tile([P, SLOTS], U8, name="g_scales", align_bytes=64)
-        quantize(g_grouped[:], g_codes[:], g_scales[:], E5M2)
+        for v in range(2):
+            half = slice(v * HALF, (v + 1) * HALF)
+            quantize(g_grouped[:, half, :], g_codes[:, half], g_scales[:, half], E5M2)
+        second_window = sb.tile([P, ITEMS], F32, name="second_window", tag="g_grouped", align_bytes=64)
+        nc.gpsimd.memset(second_window[:], 0.0)
+        out_window.append(second_window)
+
+        w_codes = sb.tile([P, K], U32, name="w_codes", align_bytes=64)
+        w_scales = sb.tile([P, K], U8, name="w_scales", align_bytes=64)
+        first_rounded = sb.tile([P, 1, 2, P, 2], BF16, name="first_rounded")
+        round_rows(nc.scalar.copy, first_rounded[:], w_first[:])
+        first_grouped = sb.tile([P, P, LANES], BF16, name="first_grouped", align_bytes=64)
+        turn_rows(first_grouped[:], first_rounded[:], 1)
+        quantize(first_grouped[:], w_codes[:, :P], w_scales[:, :P], E4M3)
 
         dv_by_slot = []
         for b in range(BLOCKS):
@@ -133,15 +143,24 @@ def tile_attend_gtower_tnh_E_pl_kernel(tc, W, xT, G, hT, cf, ts, offs, out_0, ou
                 stop=True,
             )
             scaled = sb.tile([P, K], F32, name="scaled%d" % b)
-            if b % 2 == 0:
+            if b < BLOCKS - 1:
                 nc.scalar.activation(scaled[:], slot_sums[:], ACT.Copy, scale=minus_ts[:, b : b + 1])
             else:
                 nc.vector.tensor_scalar_mul(scaled[:], slot_sums[:], minus_ts[:, b : b + 1])
             dv_by_slot.append(scaled)
 
-        w_codes = sb.tile([P, K], U32, name="w_codes", align_bytes=64)
-        w_scales = sb.tile([P, K], U8, name="w_scales", align_bytes=64)
-        dz_lanes = [sb.tile([P, LANES, HALF], BF16, name="dz_lanes%d" % v, align_bytes=64) for v in range(2)]
+        factors = []
+        squares = []
+
+        def gather_and_square(t, part, offsets_part, width, h_tag, square_tag):
+            h = sb.tile([P, width], F32, name="h%d_%d" % (t, part), tag=h_tag, align_bytes=64)
+            nc.vector.tensor_copy(h[:], h_window[t][:].indirect(offsets_part))
+            h_squared = sb.tile([P, width], F32, name="h_squared%d_%d" % (t, part), tag=square_tag)
+            nc.scalar.activation(h_squared[:], h[:], ACT.Square)
+            squares.append(h_squared)
+
+        h_tags = ("h0", "g_codes", "h2")
+        square_tags = ("minus_ts", "scaled0", "h_squared2")
         for t in range(LANES):
             turned = acc.tile([P, BLOCKS, P], F32, name="sums%d" % t)
             for b in range(BLOCKS):
@@ -150,39 +169,47 @@ def tile_attend_gtower_tnh_E_pl_kernel(tc, W, xT, G, hT, cf, ts, offs, out_0, ou
             nc.scalar.activation(
                 factor[:], turned[:].rearrange("p b n -> p (b n)"), ACT.Copy, scale=cf_lanes[:, t : t + 1]
             )
-            squares = []
+            factors.append(factor)
             if t < LANES - 1:
-                h = sb.tile([P, SLOTS], F32, name="h%d" % t)
-                nc.vector.tensor_copy(h[:], h_window[t][:].indirect(offsets[:]))
-                h_squared = sb.tile([P, SLOTS], F32, name="h_squared%d" % t)
-                nc.scalar.activation(h_squared[:], h[:], ACT.Square)
-                squares = [h_squared[:, :HALF], h_squared[:, HALF:]]
-            else:
-                for v in range(2):
-                    h = sb.tile([P, HALF], F32, name="h_last%d" % v)
-                    nc.vector.tensor_copy(h[:], h_window[t][:].indirect(halves_of_list[v]))
-                    h_squared = sb.tile([P, HALF], F32, name="h_last_squared%d" % v)
-                    nc.scalar.activation(h_squared[:], h[:], ACT.Square)
-                    squares.append(h_squared[:])
-            for v in range(2):
-                nc.vector.scalar_tensor_tensor(
-                    dz_lanes[v][:, t, :], squares[v], 1.0, factor[:, v * HALF : (v + 1) * HALF], ALU.subtract, ALU.mult
-                )
-            if t == 1:
-                first_rounded = sb.tile([P, 1, 2, P, 2], BF16, name="first_rounded")
-                round_rows(first_rounded[:], w_first[:])
-                first_grouped = sb.tile([P, P, LANES], BF16, name="first_grouped", align_bytes=64)
-                turn_rows(first_grouped[:], first_rounded[:], 1)
-                quantize(first_grouped[:], w_codes[:, :P], w_scales[:, :P], E4M3)
+                gather_and_square(t, 0, offsets[:], SLOTS, h_tags[t], square_tags[t])
+
+        dz_lanes = sb.tile([P, 2, LANES, HALF], BF16, name="dz_lanes", tag="h_window2")
+
+        def whole_lane(t):
+            nc.vector.scalar_tensor_tensor(
+                dz_lanes[:, :, t, :],
+                squares[t][:].rearrange("p (v i) -> p v i", v=2),
+                1.0,
+                factors[t][:].rearrange("p (v i) -> p v i", v=2),
+                ALU.subtract,
+                ALU.mult,
+            )
+
+        whole_lane(0)
+        whole_lane(1)
+        for v in range(2):
+            gather_and_square(LANES - 1, v, halves_of_list[v], HALF, "h_last%d" % v, "h_last_squared%d" % v)
+        whole_lane(2)
+        for v in range(2):
+            nc.vector.scalar_tensor_tensor(
+                dz_lanes[:, v, LANES - 1, :],
+                squares[LANES - 1 + v][:],
+                1.0,
+                factors[LANES - 1][:, v * HALF : (v + 1) * HALF],
+                ALU.subtract,
+                ALU.mult,
+            )
 
         dz_grouped = sb.tile([P, SLOTS, LANES], BF16, name="dz_grouped", align_bytes=64)
-        dz_by_slot = [lanes[:].rearrange("p t i -> p i t") for lanes in dz_lanes]
+        dz_by_slot = [dz_lanes[:, v].rearrange("p t i -> p i t") for v in range(2)]
         nc.scalar.copy(dz_grouped[:, :SCALAR_SLOTS, :], dz_by_slot[0][:, :SCALAR_SLOTS, :])
         nc.vector.tensor_copy(dz_grouped[:, SCALAR_SLOTS:HALF, :], dz_by_slot[0][:, SCALAR_SLOTS:, :])
         nc.vector.tensor_copy(dz_grouped[:, HALF:, :], dz_by_slot[1])
         dz_codes = sb.tile([P, SLOTS], U32, name="dz_codes", align_bytes=64)
         dz_scales = sb.tile([P, SLOTS], U8, name="dz_scales", align_bytes=64)
-        quantize(dz_grouped[:], dz_codes[:], dz_scales[:], E5M2)
+        for v in range(2):
+            half = slice(v * HALF, (v + 1) * HALF)
+            quantize(dz_grouped[:, half, :], dz_codes[:, half], dz_scales[:, half], E5M2)
 
         def second_product(t):
             rows = slice(t * P, (t + 1) * P)
@@ -202,8 +229,8 @@ def tile_attend_gtower_tnh_E_pl_kernel(tc, W, xT, G, hT, cf, ts, offs, out_0, ou
         de_first = sb.tile([P, HALF], F32, name="de_first")
         nc.scalar.copy(de_first[:], first_sums[:, :HALF])
         rest_rounded = sb.tile([P, LANES - 1, 2, P, 2], BF16, name="rest_rounded", tag="dz_grouped", align_bytes=64)
-        round_rows(rest_rounded[:, 0:1], w_rest[:, 0:1, :])
-        round_rows(rest_rounded[:, 1:3], w_rest[:, 1:3, :])
+        round_rows(nc.vector.tensor_copy, rest_rounded[:, 0:1], w_rest[:, 0:1, :])
+        round_rows(nc.vector.tensor_copy, rest_rounded[:, 1:3], w_rest[:, 1:3, :])
         nc.vector.tensor_copy(out_window[0][:].indirect(halves_of_list[0]), de_first[:])
         rest_grouped = sb.tile([P, K - P, LANES], BF16, name="rest_grouped", align_bytes=64)
         turn_rows(rest_grouped[:, :P, :], rest_rounded[:, 0:1], 1)
@@ -217,7 +244,7 @@ def tile_attend_gtower_tnh_E_pl_kernel(tc, W, xT, G, hT, cf, ts, offs, out_0, ou
 
         for tag in ("rest_grouped", "dz_grouped"):
             window = sb.tile([P, ITEMS], F32, name="window_on_" + tag, tag=tag, align_bytes=64)
-            nc.vector.memset(window[:], 0.0)
+            nc.gpsimd.memset(window[:], 0.0)
             out_window.append(window)
 
         for t in range(1, LANES):
@@ -237,7 +264,7 @@ def tile_attend_gtower_tnh_E_pl_kernel(tc, W, xT, G, hT, cf, ts, offs, out_0, ou
 
         for t in range(LANES):
             for c in range(0 if t < 2 else 1, CHUNKS):
-                round_lane(nc.scalar.copy, t, c)
+                round_lane(nc.gpsimd.tensor_copy if t < 2 and c == CHUNKS - 1 else nc.scalar.copy, t, c)
 
         y_scales = sb.tile([P, CHUNK], U8, name="y_scales", align_bytes=64)
         words = out_1[0].rearrange("p n t -> p (n t)").bitcast(I32)
@@ -251,11 +278,12 @@ def tile_attend_gtower_tnh_E_pl_kernel(tc, W, xT, G, hT, cf, ts, offs, out_0, ou
 
         round_lane(nc.vector.tensor_copy, 2, 0)
         round_lane(nc.vector.tensor_copy, 3, 0)
+        weave(nc.vector.tensor_copy, I32, 0)
         for c in range(CHUNKS):
-            if c < CHUNKS - 1:
-                weave(nc.vector.tensor_copy, I32, c)
-            else:
-                weave(nc.scalar.copy, U32, c)
+            if c < CHUNKS - 2:
+                weave(nc.vector.tensor_copy, I32, c + 1)
+            elif c == CHUNKS - 2:
+                weave(nc.scalar.copy, U32, c + 1)
             y_codes = sb.tile([P, CHUNK], U32, name="y_codes%d" % c, align_bytes=64)
             quantize(y_grouped[c][:], y_codes[:], y_scales[4 * c : P, :], E4M3)
             nc.sync.dma_start(words[:, c * CHUNK : (c + 1) * CHUNK], y_codes[:].bitcast(I32))

@@ -46,7 +46,7 @@ def tile_attend_gtower_tnh_E_pl_kernel(tc, W, xT, G, hT, cf, ts, offs, out_0, ou
         nc.sync.dma_start(ts_row[:], ts[0:1, :])
         ts_window = sb.tile([P, ITEMS], F32, name="ts_window")
         nc.vector.memset(ts_window[:], 0.0)
-        out_window = [sb.tile([P, ITEMS], F32, name="out_window0")]
+        out_window = {0: sb.tile([P, ITEMS], F32, name="out_window0")}
         nc.vector.memset(out_window[0][:], 0.0)
         nc.scalar.copy(ts_window[0:1, :], ts_row[:])
         cf_lanes = sb.tile([P, LANES], F32, name="cf_lanes")
@@ -119,7 +119,7 @@ def tile_attend_gtower_tnh_E_pl_kernel(tc, W, xT, G, hT, cf, ts, offs, out_0, ou
             quantize(g_grouped[:, half, :], g_codes[:, half], g_scales[:, half], E5M2)
         second_window = sb.tile([P, ITEMS], F32, name="second_window", tag="g_grouped", align_bytes=64)
         nc.gpsimd.memset(second_window[:], 0.0)
-        out_window.append(second_window)
+        out_window.update({2: second_window})
 
         w_codes = sb.tile([P, K], U32, name="w_codes", align_bytes=64)
         w_scales = sb.tile([P, K], U8, name="w_scales", align_bytes=64)
@@ -242,15 +242,16 @@ def tile_attend_gtower_tnh_E_pl_kernel(tc, W, xT, G, hT, cf, ts, offs, out_0, ou
         nc.vector.tensor_copy(out_window[0][:].indirect(halves_of_list[1]), de_second[:])
         nc.sync.dma_start(out_rows[:, 0, :], out_window[0][:])
 
-        for tag in ("rest_grouped", "dz_grouped"):
+        for t, tag in ((1, "rest_grouped"), (3, "dz_grouped")):
             window = sb.tile([P, ITEMS], F32, name="window_on_" + tag, tag=tag, align_bytes=64)
             nc.gpsimd.memset(window[:], 0.0)
-            out_window.append(window)
+            out_window.update({t: window})
 
-        for t in range(1, LANES):
-            de_sums = second_product(t)
-            de = sb.tile([P, SLOTS], F32, name="de%d" % t)
-            nc.scalar.copy(de[:], de_sums[:])
+        sums = {t: second_product(t) for t in (2, 1, 3)}
+
+        def scatter_lane(t, tag):
+            de = sb.tile([P, SLOTS], F32, name="de%d" % t, tag=tag)
+            nc.scalar.copy(de[:], sums[t][:])
             nc.vector.tensor_copy(out_window[t][:].indirect(offsets[:]), de[:])
             nc.sync.dma_start(out_rows[:, t, :], out_window[t][:])
 
@@ -262,31 +263,48 @@ def tile_attend_gtower_tnh_E_pl_kernel(tc, W, xT, G, hT, cf, ts, offs, out_0, ou
         def round_lane(copy, t, c):
             copy(pairs[c][:, t // 2, :, t % 2], out_window[t][:, c * CHUNK : (c + 1) * CHUNK])
 
-        for t in range(LANES):
-            for c in range(0 if t < 2 else 1, CHUNKS):
-                round_lane(nc.gpsimd.tensor_copy if t < 2 and c == CHUNKS - 1 else nc.scalar.copy, t, c)
+        def round_low_lane(t):
+            for c in range(CHUNKS):
+                round_lane(nc.gpsimd.tensor_copy if c == CHUNKS - 1 else nc.scalar.copy, t, c)
+
+        scatter_lane(2, "de2")
+        scatter_lane(1, "de1")
+        round_low_lane(0)
+        round_lane(nc.scalar.copy, 2, 0)
+        scatter_lane(3, "de2")
+        for c in range(1, CHUNKS):
+            round_lane(nc.scalar.copy, 2, c)
+        round_low_lane(1)
+        round_lane(nc.vector.tensor_copy, 3, 0)
+        for c in range(1, CHUNKS):
+            round_lane(nc.scalar.copy, 3, c)
 
         y_scales = sb.tile([P, CHUNK], U8, name="y_scales", align_bytes=64)
         words = out_1[0].rearrange("p n t -> p (n t)").bitcast(I32)
         y_grouped = [sb.tile([P, CHUNK, LANES], BF16, name="y_grouped%d" % c, align_bytes=64) for c in range(CHUNKS)]
+        y_codes = [sb.tile([P, CHUNK], U32, name="y_codes%d" % c, align_bytes=64) for c in range(CHUNKS)]
 
-        def weave(copy, dtype, c):
-            copy(
-                y_grouped[c][:].rearrange("p n t -> p (n t)").bitcast(dtype).rearrange("p (n u) -> p n u", u=2),
-                pairs[c][:].rearrange("p u n e -> p (u n e)").bitcast(dtype).rearrange("p (u n) -> p n u", u=2),
-            )
+        def weave(copy, dtype, c, columns):
+            woven = y_grouped[c][:].rearrange("p n t -> p (n t)").bitcast(dtype).rearrange("p (n u) -> p n u", u=2)
+            apart = pairs[c][:].rearrange("p u n e -> p (u n e)").bitcast(dtype).rearrange("p (u n) -> p n u", u=2)
+            copy(woven[:, columns, :], apart[:, columns, :])
 
-        round_lane(nc.vector.tensor_copy, 2, 0)
-        round_lane(nc.vector.tensor_copy, 3, 0)
-        weave(nc.vector.tensor_copy, I32, 0)
-        for c in range(CHUNKS):
-            if c < CHUNKS - 2:
-                weave(nc.vector.tensor_copy, I32, c + 1)
-            elif c == CHUNKS - 2:
-                weave(nc.scalar.copy, U32, c + 1)
-            y_codes = sb.tile([P, CHUNK], U32, name="y_codes%d" % c, align_bytes=64)
-            quantize(y_grouped[c][:], y_codes[:], y_scales[4 * c : P, :], E4M3)
-            nc.sync.dma_start(words[:, c * CHUNK : (c + 1) * CHUNK], y_codes[:].bitcast(I32))
+        def finish(c, columns):
+            quantize(y_grouped[c][:, columns, :], y_codes[c][:, columns], y_scales[4 * c : P, columns], E4M3)
+            nc.sync.dma_start(words[:, c * CHUNK : (c + 1) * CHUNK][:, columns], y_codes[c][:, columns].bitcast(I32))
+
+        whole, low, high = slice(0, CHUNK), slice(0, CHUNK // 2), slice(CHUNK // 2, CHUNK)
+        weave(nc.vector.tensor_copy, I32, 0, whole)
+        weave(nc.vector.tensor_copy, I32, 1, whole)
+        finish(0, whole)
+        weave(nc.vector.tensor_copy, I32, 2, low)
+        weave(nc.scalar.copy, U32, 2, high)
+        weave(nc.scalar.copy, U32, 3, low)
+        weave(nc.scalar.copy, U32, 3, high)
+        finish(1, whole)
+        finish(2, whole)
+        finish(3, low)
+        finish(3, high)
 
         scale_rows = out_2[0].bitcast(I32).rearrange("r (c n) -> c r n", c=CHUNKS)
         for q in range(QUADRANTS):

@@ -26,7 +26,7 @@ BYTES = 4 * (3 * K * K + K * ITEMS + K + ITEMS) + 2 * P * SLOTS // 16 + 4 * K * 
 BLOCKS = SLOTS // P
 HALF = SLOTS // 2
 VECTOR_SLOTS = 320
-SCALAR_SLOTS = 192
+SCATTER_ORDER = (0, 2, 1, 3)
 CHUNK = 512
 CHUNKS = ITEMS // CHUNK
 
@@ -39,11 +39,15 @@ def tile_attend_gtower_tnh_E_pl_kernel(tc, W, xT, G, hT, cf, ts, offs, out_0, ou
         acc = ctx.enter_context(tc.psum_pool(name="acc", bufs=1))
 
         offsets = sb.tile([P, SLOTS // 16], U16, name="offsets")
-        nc.sync.dma_start(offsets[:], offs)
+        x_rows = xT.rearrange("(m t) k -> m t k", t=LANES)
+        x_raw = [sb.tile([P, 2, K], F32, name="x_raw%d" % v) for v in range(2)]
         halves_of_list = [offsets[:, v * HALF // 16 : (v + 1) * HALF // 16] for v in range(2)]
 
         ts_row = sb.tile([1, ITEMS], F32, name="ts_row")
         nc.sync.dma_start(ts_row[:], ts[0:1, :])
+        nc.sync.dma_start(x_raw[0][:], x_rows[:, 0:2, :])
+        nc.sync.dma_start(offsets[:], offs)
+        nc.sync.dma_start(x_raw[1][:], x_rows[:, 2:4, :])
         ts_window = sb.tile([P, ITEMS], F32, name="ts_window")
         nc.vector.memset(ts_window[:], 0.0)
         out_window = {0: sb.tile([P, ITEMS], F32, name="out_window0")}
@@ -52,23 +56,20 @@ def tile_attend_gtower_tnh_E_pl_kernel(tc, W, xT, G, hT, cf, ts, offs, out_0, ou
         cf_lanes = sb.tile([P, LANES], F32, name="cf_lanes")
         nc.scalar.dma_start(cf_lanes[:], cf.rearrange("(p t) o -> p (t o)", t=LANES))
 
-        x_rows = xT.rearrange("(m t) k -> m t k", t=LANES)
         w_rows = W.rearrange("(m t) k -> m t k", t=LANES)
         h_rows = hT.rearrange("(p t) n -> p t n", t=LANES)
         out_rows = out_0.rearrange("(p t) n -> p t n", t=LANES)
 
-        x_raw = [sb.tile([P, 2, K], F32, name="x_raw%d" % v) for v in range(2)]
-        for v in range(2):
-            nc.sync.dma_start(x_raw[v][:], x_rows[:, 2 * v : 2 * v + 2, :])
         g_raw = sb.tile([P, LANES, SLOTS], F32, name="g_raw")
         nc.sync.dma_start(g_raw[:], G.rearrange("(p j) i -> p j i", j=LANES))
-        h_window = [sb.tile([P, ITEMS], F32, name="h_window%d" % t) for t in range(LANES)]
-        w_first = sb.tile([P, 1, K], F32, name="w_first")
-        w_rest = sb.tile([P, LANES - 1, K], F32, name="w_rest")
-        nc.sync.dma_start(w_first[:], w_rows[:, 0:1, :])
+        h_window = [sb.tile([P, ITEMS], F32, name="h_window%d" % t, align_bytes=64) for t in range(LANES)]
         for t in range(LANES):
             nc.sync.dma_start(h_window[t][:], h_rows[:, t, :])
-        nc.sync.dma_start(w_rest[:], w_rows[:, 1:LANES, :])
+        w_parts = [w_rows[:, 0:1, :], w_rows[:, 2:3, :], w_rows[:, 1:LANES:2, :]]
+        w_raw = []
+        for n, part in enumerate(w_parts):
+            w_raw.append(sb.tile([P, part.shape[1], K], F32, name="w_raw%d" % n))
+            nc.sync.dma_start(w_raw[n][:], part)
 
         ident = sb.tile([P, P], F32, name="ident")
         make_identity(nc, ident[:])
@@ -123,11 +124,6 @@ def tile_attend_gtower_tnh_E_pl_kernel(tc, W, xT, G, hT, cf, ts, offs, out_0, ou
 
         w_codes = sb.tile([P, K], U32, name="w_codes", align_bytes=64)
         w_scales = sb.tile([P, K], U8, name="w_scales", align_bytes=64)
-        first_rounded = sb.tile([P, 1, 2, P, 2], BF16, name="first_rounded")
-        round_rows(nc.scalar.copy, first_rounded[:], w_first[:])
-        first_grouped = sb.tile([P, P, LANES], BF16, name="first_grouped", align_bytes=64)
-        turn_rows(first_grouped[:], first_rounded[:], 1)
-        quantize(first_grouped[:], w_codes[:, :P], w_scales[:, :P], E4M3)
 
         dv_by_slot = []
         for b in range(BLOCKS):
@@ -149,6 +145,9 @@ def tile_attend_gtower_tnh_E_pl_kernel(tc, W, xT, G, hT, cf, ts, offs, out_0, ou
                 nc.vector.tensor_scalar_mul(scaled[:], slot_sums[:], minus_ts[:, b : b + 1])
             dv_by_slot.append(scaled)
 
+        last_window = sb.tile([P, ITEMS], F32, name="last_window", tag="x_codes", align_bytes=64)
+        nc.gpsimd.memset(last_window[:], 0.0)
+        out_window.update({3: last_window})
         factors = []
         squares = []
 
@@ -173,46 +172,59 @@ def tile_attend_gtower_tnh_E_pl_kernel(tc, W, xT, G, hT, cf, ts, offs, out_0, ou
             if t < LANES - 1:
                 gather_and_square(t, 0, offsets[:], SLOTS, h_tags[t], square_tags[t])
 
-        dz_lanes = sb.tile([P, 2, LANES, HALF], BF16, name="dz_lanes", tag="h_window2")
-
-        def whole_lane(t):
-            nc.vector.scalar_tensor_tensor(
-                dz_lanes[:, :, t, :],
-                squares[t][:].rearrange("p (v i) -> p v i", v=2),
-                1.0,
-                factors[t][:].rearrange("p (v i) -> p v i", v=2),
-                ALU.subtract,
-                ALU.mult,
-            )
-
-        whole_lane(0)
-        whole_lane(1)
-        for v in range(2):
-            gather_and_square(LANES - 1, v, halves_of_list[v], HALF, "h_last%d" % v, "h_last_squared%d" % v)
-        whole_lane(2)
-        for v in range(2):
-            nc.vector.scalar_tensor_tensor(
-                dz_lanes[:, v, LANES - 1, :],
-                squares[LANES - 1 + v][:],
-                1.0,
-                factors[LANES - 1][:, v * HALF : (v + 1) * HALF],
-                ALU.subtract,
-                ALU.mult,
-            )
-
+        dz_low = sb.tile([P, 2, SLOTS], BF16, name="dz_low", tag="h_window2", align_bytes=64)
+        for t in range(2):
+            nc.vector.scalar_tensor_tensor(dz_low[:, t, :], squares[t][:], 1.0, factors[t][:], ALU.subtract, ALU.mult)
         dz_grouped = sb.tile([P, SLOTS, LANES], BF16, name="dz_grouped", align_bytes=64)
-        dz_by_slot = [dz_lanes[:, v].rearrange("p t i -> p i t") for v in range(2)]
-        nc.scalar.copy(dz_grouped[:, :SCALAR_SLOTS, :], dz_by_slot[0][:, :SCALAR_SLOTS, :])
-        nc.vector.tensor_copy(dz_grouped[:, SCALAR_SLOTS:HALF, :], dz_by_slot[0][:, SCALAR_SLOTS:, :])
-        nc.vector.tensor_copy(dz_grouped[:, HALF:, :], dz_by_slot[1])
+        nc.vector.tensor_copy(dz_grouped[:, :, 0:2], dz_low[:].rearrange("p t i -> p i t"))
+
+        w_codes_parts = (slice(0, P), slice(P, 2 * P), slice(2 * P, K))
+        w_grouped = []
+
+        def turn_w(n):
+            lanes = w_raw[n].shape[1]
+            rounded = sb.tile([P, lanes, 2, P, 2], BF16, name="w_rounded%d" % n)
+            round_rows(nc.scalar.copy, rounded[:], w_raw[n][:])
+            grouped = sb.tile([P, lanes * P, LANES], BF16, name="w_grouped%d" % n, align_bytes=64)
+            turn_rows(grouped[:], rounded[:], lanes)
+            w_grouped.append(grouped)
+
+        def quantize_w(n):
+            quantize(w_grouped[n][:], w_codes[:, w_codes_parts[n]], w_scales[:, w_codes_parts[n]], E4M3)
+
+        last_tags = ("h_window2", "h_last1")
+        for v in range(2):
+            gather_and_square(LANES - 1, v, halves_of_list[v], HALF, last_tags[v], "h_last_squared%d" % v)
+        turn_w(0)
+        dz_high = sb.tile([P, 2, 2, HALF], BF16, name="dz_high", tag="h_window3", align_bytes=64)
+        nc.vector.scalar_tensor_tensor(
+            dz_high[:, :, 0, :],
+            squares[2][:].rearrange("p (v i) -> p v i", v=2),
+            1.0,
+            factors[2][:].rearrange("p (v i) -> p v i", v=2),
+            ALU.subtract,
+            ALU.mult,
+        )
+        for v in range(2):
+            half = slice(v * HALF, (v + 1) * HALF)
+            nc.vector.scalar_tensor_tensor(
+                dz_high[:, v, 1, :], squares[LANES - 1 + v][:], 1.0, factors[LANES - 1][:, half], ALU.subtract, ALU.mult
+            )
+        for v in range(2):
+            half = slice(v * HALF, (v + 1) * HALF)
+            nc.vector.tensor_copy(dz_grouped[:, half, 2:LANES], dz_high[:, v].rearrange("p t i -> p i t"))
         dz_codes = sb.tile([P, SLOTS], U32, name="dz_codes", align_bytes=64)
         dz_scales = sb.tile([P, SLOTS], U8, name="dz_scales", align_bytes=64)
         for v in range(2):
             half = slice(v * HALF, (v + 1) * HALF)
             quantize(dz_grouped[:, half, :], dz_codes[:, half], dz_scales[:, half], E5M2)
+        quantize_w(0)
+        turn_w(1)
+        quantize_w(1)
 
         def second_product(t):
-            rows = slice(t * P, (t + 1) * P)
+            place = SCATTER_ORDER.index(t)
+            rows = slice(place * P, (place + 1) * P)
             de_sums = acc.tile([P, SLOTS], F32, name="sums%d" % t)
             nc.tensor.matmul_mx(
                 out=de_sums[:],
@@ -225,35 +237,21 @@ def tile_attend_gtower_tnh_E_pl_kernel(tc, W, xT, G, hT, cf, ts, offs, out_0, ou
             )
             return de_sums
 
-        first_sums = second_product(0)
-        de_first = sb.tile([P, HALF], F32, name="de_first")
-        nc.scalar.copy(de_first[:], first_sums[:, :HALF])
-        rest_rounded = sb.tile([P, LANES - 1, 2, P, 2], BF16, name="rest_rounded", tag="dz_grouped", align_bytes=64)
-        round_rows(nc.vector.tensor_copy, rest_rounded[:, 0:1], w_rest[:, 0:1, :])
-        round_rows(nc.vector.tensor_copy, rest_rounded[:, 1:3], w_rest[:, 1:3, :])
-        nc.vector.tensor_copy(out_window[0][:].indirect(halves_of_list[0]), de_first[:])
-        rest_grouped = sb.tile([P, K - P, LANES], BF16, name="rest_grouped", align_bytes=64)
-        turn_rows(rest_grouped[:, :P, :], rest_rounded[:, 0:1], 1)
-        turn_rows(rest_grouped[:, P:, :], rest_rounded[:, 1:3], 2)
-        quantize(rest_grouped[:, :P, :], w_codes[:, P : 2 * P], w_scales[:, P : 2 * P], E4M3)
-        quantize(rest_grouped[:, P:, :], w_codes[:, 2 * P :], w_scales[:, 2 * P :], E4M3)
-        de_second = sb.tile([P, HALF], F32, name="de_second", tag="dz_grouped", align_bytes=64)
-        nc.scalar.copy(de_second[:], first_sums[:, HALF:])
-        nc.vector.tensor_copy(out_window[0][:].indirect(halves_of_list[1]), de_second[:])
-        nc.sync.dma_start(out_rows[:, 0, :], out_window[0][:])
-
-        for t, tag in ((1, "rest_grouped"), (3, "dz_grouped")):
-            window = sb.tile([P, ITEMS], F32, name="window_on_" + tag, tag=tag, align_bytes=64)
-            nc.gpsimd.memset(window[:], 0.0)
-            out_window.update({t: window})
-
-        sums = {t: second_product(t) for t in (2, 1, 3)}
-
-        def scatter_lane(t, tag):
+        def scatter_lane(t, de_sums, tag):
             de = sb.tile([P, SLOTS], F32, name="de%d" % t, tag=tag)
-            nc.scalar.copy(de[:], sums[t][:])
+            nc.scalar.copy(de[:], de_sums[:])
             nc.vector.tensor_copy(out_window[t][:].indirect(offsets[:]), de[:])
             nc.sync.dma_start(out_rows[:, t, :], out_window[t][:])
+
+        scatter_lane(0, second_product(0), "w_rounded1")
+        sums2 = second_product(2)
+        turn_w(2)
+        quantize_w(2)
+        window = sb.tile([P, ITEMS], F32, name="third_window", tag="w_grouped2", align_bytes=64)
+        nc.gpsimd.memset(window[:], 0.0)
+        out_window.update({1: window})
+        sums1 = second_product(1)
+        sums3 = second_product(3)
 
         pair_tags = ("dz_codes", "dz_scales", "w_codes", "w_scales")
         pairs = [
@@ -267,11 +265,11 @@ def tile_attend_gtower_tnh_E_pl_kernel(tc, W, xT, G, hT, cf, ts, offs, out_0, ou
             for c in range(CHUNKS):
                 round_lane(nc.gpsimd.tensor_copy if c == CHUNKS - 1 else nc.scalar.copy, t, c)
 
-        scatter_lane(2, "de2")
-        scatter_lane(1, "de1")
+        scatter_lane(2, sums2, "w_rounded2")
+        scatter_lane(1, sums1, "de1")
         round_low_lane(0)
         round_lane(nc.scalar.copy, 2, 0)
-        scatter_lane(3, "de2")
+        scatter_lane(3, sums3, "w_rounded2")
         for c in range(1, CHUNKS):
             round_lane(nc.scalar.copy, 2, c)
         round_low_lane(1)
@@ -303,8 +301,7 @@ def tile_attend_gtower_tnh_E_pl_kernel(tc, W, xT, G, hT, cf, ts, offs, out_0, ou
         weave(nc.scalar.copy, U32, 3, high)
         finish(1, whole)
         finish(2, whole)
-        finish(3, low)
-        finish(3, high)
+        finish(3, whole)
 
         scale_rows = out_2[0].bitcast(I32).rearrange("r (c n) -> c r n", c=CHUNKS)
         for q in range(QUADRANTS):

@@ -25,7 +25,7 @@ BYTES = 4 * (3 * K * K + K * ITEMS + K + ITEMS) + 2 * P * SLOTS // 16 + 4 * K * 
 
 BLOCKS = SLOTS // P
 HALF = SLOTS // 2
-VECTOR_SLOTS = 320
+VECTOR_SLOTS = 384
 SCATTER_ORDER = (0, 2, 1, 3)
 CHUNK = 512
 CHUNKS = ITEMS // CHUNK
@@ -107,17 +107,18 @@ def tile_attend_gtower_tnh_E_pl_kernel(tc, W, xT, G, hT, cf, ts, offs, out_0, ou
 
         x_codes = sb.tile([P, K], U32, name="x_codes", align_bytes=64)
         x_scales = sb.tile([P, K], U8, name="x_scales", align_bytes=64)
-        quantize(x_grouped[:], x_codes[:], x_scales[:], E4M3)
         g_grouped = sb.tile([P, SLOTS, LANES], BF16, name="g_grouped", align_bytes=64)
         g_by_slot = g_raw[:].rearrange("p j i -> p i j")
         nc.vector.tensor_copy(g_grouped[:, :HALF, :], g_by_slot[:, :HALF, :])
         nc.vector.tensor_copy(g_grouped[:, HALF:VECTOR_SLOTS, :], g_by_slot[:, HALF:VECTOR_SLOTS, :])
         nc.scalar.copy(g_grouped[:, VECTOR_SLOTS:, :], g_by_slot[:, VECTOR_SLOTS:, :])
-        g_codes = sb.tile([P, SLOTS], U32, name="g_codes", align_bytes=64)
-        g_scales = sb.tile([P, SLOTS], U8, name="g_scales", align_bytes=64)
-        for v in range(2):
-            half = slice(v * HALF, (v + 1) * HALF)
-            quantize(g_grouped[:, half, :], g_codes[:, half], g_scales[:, half], E5M2)
+        e5_codes = sb.tile([P, 2 * SLOTS], U32, name="e5_codes", align_bytes=64)
+        e5_scales = sb.tile([P, 2 * SLOTS], U8, name="e5_scales", align_bytes=64)
+        g_codes, dz_codes = e5_codes[:, :SLOTS], e5_codes[:, SLOTS:]
+        g_scales, dz_scales = e5_scales[:, :SLOTS], e5_scales[:, SLOTS:]
+        quantize(g_grouped[:, :HALF, :], g_codes[:, :HALF], g_scales[:, :HALF], E5M2)
+        quantize(x_grouped[:], x_codes[:], x_scales[:], E4M3)
+        quantize(g_grouped[:, HALF:, :], g_codes[:, HALF:], g_scales[:, HALF:], E5M2)
         second_window = sb.tile([P, ITEMS], F32, name="second_window", tag="g_grouped", align_bytes=64)
         nc.gpsimd.memset(second_window[:], 0.0)
         out_window.update({2: second_window})
@@ -158,7 +159,7 @@ def tile_attend_gtower_tnh_E_pl_kernel(tc, W, xT, G, hT, cf, ts, offs, out_0, ou
             nc.scalar.activation(h_squared[:], h[:], ACT.Square)
             squares.append(h_squared)
 
-        h_tags = ("h0", "g_codes", "h2")
+        h_tags = ("h0", "x_scales", "h2")
         square_tags = ("minus_ts", "scaled0", "h_squared2")
         for t in range(LANES):
             turned = acc.tile([P, BLOCKS, P], F32, name="sums%d" % t)
@@ -192,33 +193,45 @@ def tile_attend_gtower_tnh_E_pl_kernel(tc, W, xT, G, hT, cf, ts, offs, out_0, ou
         def quantize_w(n):
             quantize(w_grouped[n][:], w_codes[:, w_codes_parts[n]], w_scales[:, w_codes_parts[n]], E4M3)
 
-        last_tags = ("h_window2", "h_last1")
-        for v in range(2):
-            gather_and_square(LANES - 1, v, halves_of_list[v], HALF, last_tags[v], "h_last_squared%d" % v)
         turn_w(0)
+        last_squared = sb.tile([P, 2, HALF], F32, name="last_squared", tag="w_raw0")
+        for v, tag in enumerate(("h_window2", "h_last1")):
+            h = sb.tile([P, HALF], F32, name="h_last%d" % v, tag=tag, align_bytes=64)
+            nc.vector.tensor_copy(h[:], h_window[LANES - 1][:].indirect(halves_of_list[v]))
+            nc.scalar.activation(last_squared[:, v, :], h[:], ACT.Square)
         dz_high = sb.tile([P, 2, 2, HALF], BF16, name="dz_high", tag="h_window3", align_bytes=64)
-        nc.vector.scalar_tensor_tensor(
-            dz_high[:, :, 0, :],
-            squares[2][:].rearrange("p (v i) -> p v i", v=2),
-            1.0,
-            factors[2][:].rearrange("p (v i) -> p v i", v=2),
-            ALU.subtract,
-            ALU.mult,
-        )
-        for v in range(2):
-            half = slice(v * HALF, (v + 1) * HALF)
+        halves = [slice(v * HALF, (v + 1) * HALF) for v in range(2)]
+
+        def high_lane(t, v, square):
             nc.vector.scalar_tensor_tensor(
-                dz_high[:, v, 1, :], squares[LANES - 1 + v][:], 1.0, factors[LANES - 1][:, half], ALU.subtract, ALU.mult
+                dz_high[:, v, t - 2, :], square, 1.0, factors[t][:, halves[v]], ALU.subtract, ALU.mult
             )
-        for v in range(2):
-            half = slice(v * HALF, (v + 1) * HALF)
-            nc.vector.tensor_copy(dz_grouped[:, half, 2:LANES], dz_high[:, v].rearrange("p t i -> p i t"))
-        dz_codes = sb.tile([P, SLOTS], U32, name="dz_codes", align_bytes=64)
-        dz_scales = sb.tile([P, SLOTS], U8, name="dz_scales", align_bytes=64)
-        for v in range(2):
-            half = slice(v * HALF, (v + 1) * HALF)
-            quantize(dz_grouped[:, half, :], dz_codes[:, half], dz_scales[:, half], E5M2)
+
+        def place_high(v):
+            nc.vector.tensor_copy(dz_grouped[:, halves[v], 2:LANES], dz_high[:, v].rearrange("p t i -> p i t"))
+
+        def quantize_dz(v):
+            quantize(dz_grouped[:, halves[v], :], dz_codes[:, halves[v]], dz_scales[:, halves[v]], E5M2)
+
+        high_lane(2, 0, squares[2][:, halves[0]])
+        high_lane(3, 0, last_squared[:, 0, :])
+        high_lane(2, 1, squares[2][:, halves[1]])
+        place_high(0)
+        high_lane(3, 1, last_squared[:, 1, :])
         quantize_w(0)
+        quantize_dz(0)
+        early_sums = turn.tile([P, SLOTS], F32, name="bank")
+        nc.tensor.matmul_mx(
+            out=early_sums[:],
+            lhsT=w_codes[:, :P].bitcast(E4M3),
+            lhsT_scale=w_scales[:, :P],
+            rhs=e5_codes[:, HALF : HALF + SLOTS].bitcast(E5M2),
+            rhs_scale=e5_scales[:, HALF : HALF + SLOTS],
+            start=True,
+            stop=True,
+        )
+        place_high(1)
+        quantize_dz(1)
         turn_w(1)
         quantize_w(1)
 
@@ -230,8 +243,8 @@ def tile_attend_gtower_tnh_E_pl_kernel(tc, W, xT, G, hT, cf, ts, offs, out_0, ou
                 out=de_sums[:],
                 lhsT=w_codes[:, rows].bitcast(E4M3),
                 lhsT_scale=w_scales[:, rows],
-                rhs=dz_codes[:].bitcast(E5M2),
-                rhs_scale=dz_scales[:],
+                rhs=dz_codes.bitcast(E5M2),
+                rhs_scale=dz_scales,
                 start=True,
                 stop=True,
             )
@@ -243,7 +256,12 @@ def tile_attend_gtower_tnh_E_pl_kernel(tc, W, xT, G, hT, cf, ts, offs, out_0, ou
             nc.vector.tensor_copy(out_window[t][:].indirect(offsets[:]), de[:])
             nc.sync.dma_start(out_rows[:, t, :], out_window[t][:])
 
-        scatter_lane(0, second_product(0), "w_rounded1")
+        sums0 = second_product(0)
+        for v, de_sums, tag in ((0, early_sums, "de0_early"), (1, sums0, "de0")):
+            de = sb.tile([P, HALF], F32, name="de0_%d" % v, tag=tag, align_bytes=64)
+            nc.scalar.copy(de[:], de_sums[:, HALF:])
+            nc.vector.tensor_copy(out_window[0][:].indirect(halves_of_list[v]), de[:])
+        nc.sync.dma_start(out_rows[:, 0, :], out_window[0][:])
         sums2 = second_product(2)
         turn_w(2)
         quantize_w(2)
@@ -253,7 +271,7 @@ def tile_attend_gtower_tnh_E_pl_kernel(tc, W, xT, G, hT, cf, ts, offs, out_0, ou
         sums1 = second_product(1)
         sums3 = second_product(3)
 
-        pair_tags = ("dz_codes", "dz_scales", "w_codes", "w_scales")
+        pair_tags = ("e5_codes", "e5_scales", "w_codes", "w_scales")
         pairs = [
             sb.tile([P, 2, CHUNK, 2], BF16, name="pairs%d" % c, tag=pair_tags[c], align_bytes=64) for c in range(CHUNKS)
         ]

@@ -43,6 +43,8 @@ def tile_attend_gtower_tnh_E_pl_kernel(tc, W, xT, G, hT, cf, ts, offs, out_0, ou
         x_raw = [sb.tile([P, 2, K], F32, name="x_raw%d" % v) for v in range(2)]
         halves_of_list = [offsets[:, v * HALF // 16 : (v + 1) * HALF // 16] for v in range(2)]
 
+        cf_lanes = sb.tile([P, LANES], F32, name="cf_lanes")
+        nc.sync.dma_start(cf_lanes[:], cf.rearrange("(p t) o -> p (t o)", t=LANES))
         ts_row = sb.tile([1, ITEMS], F32, name="ts_row")
         nc.sync.dma_start(ts_row[:], ts[0:1, :])
         nc.sync.dma_start(x_raw[0][:], x_rows[:, 0:2, :])
@@ -52,9 +54,9 @@ def tile_attend_gtower_tnh_E_pl_kernel(tc, W, xT, G, hT, cf, ts, offs, out_0, ou
         nc.vector.memset(ts_window[:], 0.0)
         out_window = {0: sb.tile([P, ITEMS], F32, name="out_window0")}
         nc.vector.memset(out_window[0][:], 0.0)
+        minus_cf = sb.tile([P, LANES], F32, name="minus_cf")
+        nc.scalar.activation(minus_cf[:], cf_lanes[:], ACT.Copy, scale=-1.0)
         nc.scalar.copy(ts_window[0:1, :], ts_row[:])
-        cf_lanes = sb.tile([P, LANES], F32, name="cf_lanes")
-        nc.scalar.dma_start(cf_lanes[:], cf.rearrange("(p t) o -> p (t o)", t=LANES))
 
         w_rows = W.rearrange("(m t) k -> m t k", t=LANES)
         h_rows = hT.rearrange("(p t) n -> p t n", t=LANES)
@@ -102,8 +104,8 @@ def tile_attend_gtower_tnh_E_pl_kernel(tc, W, xT, G, hT, cf, ts, offs, out_0, ou
         ts_bank = turn.tile([P, LANES, P], F32, name="bank")
         for b in range(BLOCKS):
             nc.tensor.transpose(ts_bank[:, b, :], ts_listed[:, b * P : (b + 1) * P], ident[:])
-        minus_ts = sb.tile([P, BLOCKS], F32, name="minus_ts")
-        nc.scalar.activation(minus_ts[:], ts_bank[:, :, 0], ACT.Copy, scale=-1.0)
+        ts_columns = sb.tile([P, BLOCKS], F32, name="ts_columns")
+        nc.scalar.copy(ts_columns[:], ts_bank[:, :, 0])
 
         x_codes = sb.tile([P, K], U32, name="x_codes", align_bytes=64)
         x_scales = sb.tile([P, K], U8, name="x_scales", align_bytes=64)
@@ -141,9 +143,9 @@ def tile_attend_gtower_tnh_E_pl_kernel(tc, W, xT, G, hT, cf, ts, offs, out_0, ou
             )
             scaled = sb.tile([P, K], F32, name="scaled%d" % b)
             if b < BLOCKS - 1:
-                nc.scalar.activation(scaled[:], slot_sums[:], ACT.Copy, scale=minus_ts[:, b : b + 1])
+                nc.scalar.activation(scaled[:], slot_sums[:], ACT.Copy, scale=ts_columns[:, b : b + 1])
             else:
-                nc.vector.tensor_scalar_mul(scaled[:], slot_sums[:], minus_ts[:, b : b + 1])
+                nc.vector.tensor_scalar_mul(scaled[:], slot_sums[:], ts_columns[:, b : b + 1])
             dv_by_slot.append(scaled)
 
         last_window = sb.tile([P, ITEMS], F32, name="last_window", tag="x_codes", align_bytes=64)
@@ -160,14 +162,14 @@ def tile_attend_gtower_tnh_E_pl_kernel(tc, W, xT, G, hT, cf, ts, offs, out_0, ou
             squares.append(h_squared)
 
         h_tags = ("h0", "x_scales", "h2")
-        square_tags = ("minus_ts", "scaled0", "h_squared2")
+        square_tags = ("ts_columns", "h_squared1", "h_squared2")
         for t in range(LANES):
             turned = acc.tile([P, BLOCKS, P], F32, name="sums%d" % t)
             for b in range(BLOCKS):
                 nc.tensor.transpose(turned[:, b, :], dv_by_slot[b][:, t * P : (t + 1) * P], ident[:])
             factor = sb.tile([P, SLOTS], F32, name="factor%d" % t)
             nc.scalar.activation(
-                factor[:], turned[:].rearrange("p b n -> p (b n)"), ACT.Copy, scale=cf_lanes[:, t : t + 1]
+                factor[:], turned[:].rearrange("p b n -> p (b n)"), ACT.Copy, scale=minus_cf[:, t : t + 1]
             )
             factors.append(factor)
             if t < LANES - 1:
@@ -256,15 +258,18 @@ def tile_attend_gtower_tnh_E_pl_kernel(tc, W, xT, G, hT, cf, ts, offs, out_0, ou
             nc.vector.tensor_copy(out_window[t][:].indirect(offsets[:]), de[:])
             nc.sync.dma_start(out_rows[:, t, :], out_window[t][:])
 
-        sums0 = second_product(0)
-        for v, de_sums, tag in ((0, early_sums, "de0_early"), (1, sums0, "de0")):
-            de = sb.tile([P, HALF], F32, name="de0_%d" % v, tag=tag, align_bytes=64)
+        def scatter_first(v, de_sums, tag):
+            de = sb.tile([P, HALF], F32, name="de0_%d" % v, tag=tag)
             nc.scalar.copy(de[:], de_sums[:, HALF:])
             nc.vector.tensor_copy(out_window[0][:].indirect(halves_of_list[v]), de[:])
-        nc.sync.dma_start(out_rows[:, 0, :], out_window[0][:])
+
+        scatter_first(0, early_sums, "de0_early")
+        sums0 = second_product(0)
         sums2 = second_product(2)
         turn_w(2)
         quantize_w(2)
+        scatter_first(1, sums0, "w_rounded2")
+        nc.sync.dma_start(out_rows[:, 0, :], out_window[0][:])
         window = sb.tile([P, ITEMS], F32, name="third_window", tag="w_grouped2", align_bytes=64)
         nc.gpsimd.memset(window[:], 0.0)
         out_window.update({1: window})
@@ -283,11 +288,11 @@ def tile_attend_gtower_tnh_E_pl_kernel(tc, W, xT, G, hT, cf, ts, offs, out_0, ou
             for c in range(CHUNKS):
                 round_lane(nc.gpsimd.tensor_copy if c == CHUNKS - 1 else nc.scalar.copy, t, c)
 
-        scatter_lane(2, sums2, "w_rounded2")
+        scatter_lane(2, sums2, "de2")
         scatter_lane(1, sums1, "de1")
         round_low_lane(0)
         round_lane(nc.scalar.copy, 2, 0)
-        scatter_lane(3, sums3, "w_rounded2")
+        scatter_lane(3, sums3, "de2")
         for c in range(1, CHUNKS):
             round_lane(nc.scalar.copy, 2, c)
         round_low_lane(1)
@@ -305,9 +310,10 @@ def tile_attend_gtower_tnh_E_pl_kernel(tc, W, xT, G, hT, cf, ts, offs, out_0, ou
             apart = pairs[c][:].rearrange("p u n e -> p (u n e)").bitcast(dtype).rearrange("p (u n) -> p n u", u=2)
             copy(woven[:, columns, :], apart[:, columns, :])
 
-        def finish(c, columns):
-            quantize(y_grouped[c][:, columns, :], y_codes[c][:, columns], y_scales[4 * c : P, columns], E4M3)
-            nc.sync.dma_start(words[:, c * CHUNK : (c + 1) * CHUNK][:, columns], y_codes[c][:, columns].bitcast(I32))
+        def finish(c, *parts):
+            for columns in parts:
+                quantize(y_grouped[c][:, columns, :], y_codes[c][:, columns], y_scales[4 * c : P, columns], E4M3)
+            nc.sync.dma_start(words[:, c * CHUNK : (c + 1) * CHUNK], y_codes[c][:].bitcast(I32))
 
         whole, low, high = slice(0, CHUNK), slice(0, CHUNK // 2), slice(CHUNK // 2, CHUNK)
         weave(nc.vector.tensor_copy, I32, 0, whole)
@@ -319,7 +325,7 @@ def tile_attend_gtower_tnh_E_pl_kernel(tc, W, xT, G, hT, cf, ts, offs, out_0, ou
         weave(nc.scalar.copy, U32, 3, high)
         finish(1, whole)
         finish(2, whole)
-        finish(3, whole)
+        finish(3, low, high)
 
         scale_rows = out_2[0].bitcast(I32).rearrange("r (c n) -> c r n", c=CHUNKS)
         for q in range(QUADRANTS):

@@ -26,7 +26,7 @@ BYTES = 4 * (3 * K * K + K * ITEMS + K + ITEMS) + 2 * P * SLOTS // 16 + 4 * K * 
 BLOCKS = SLOTS // P
 HALF = SLOTS // 2
 VECTOR_SLOTS = 384
-SCATTER_ORDER = (0, 2, 1, 3)
+TS_ROW = P - 1
 CHUNK = 512
 CHUNKS = ITEMS // CHUNK
 
@@ -35,43 +35,43 @@ def tile_attend_gtower_tnh_E_pl_kernel(tc, W, xT, G, hT, cf, ts, offs, out_0, ou
     nc = tc.nc
     with ExitStack() as ctx:
         sb = ctx.enter_context(tc.tile_pool(name="sb", bufs=1))
+        placed = ctx.enter_context(tc.tile_pool(name="placed", bufs=1))
         turn = ctx.enter_context(tc.psum_pool(name="turn", bufs=4))
         acc = ctx.enter_context(tc.psum_pool(name="acc", bufs=1))
 
-        offsets = sb.tile([P, SLOTS // 16], U16, name="offsets")
         x_rows = xT.rearrange("(m t) k -> m t k", t=LANES)
-        x_raw = [sb.tile([P, 2, K], F32, name="x_raw%d" % v) for v in range(2)]
-        halves_of_list = [offsets[:, v * HALF // 16 : (v + 1) * HALF // 16] for v in range(2)]
-
-        cf_lanes = sb.tile([P, LANES], F32, name="cf_lanes")
-        nc.sync.dma_start(cf_lanes[:], cf.rearrange("(p t) o -> p (t o)", t=LANES))
-        ts_row = sb.tile([1, ITEMS], F32, name="ts_row")
-        nc.sync.dma_start(ts_row[:], ts[0:1, :])
-        nc.sync.dma_start(x_raw[0][:], x_rows[:, 0:2, :])
-        nc.sync.dma_start(offsets[:], offs)
-        nc.sync.dma_start(x_raw[1][:], x_rows[:, 2:4, :])
-        ts_window = sb.tile([P, ITEMS], F32, name="ts_window")
-        nc.vector.memset(ts_window[:], 0.0)
-        out_window = {0: sb.tile([P, ITEMS], F32, name="out_window0")}
-        nc.vector.memset(out_window[0][:], 0.0)
-        minus_cf = sb.tile([P, LANES], F32, name="minus_cf")
-        nc.scalar.activation(minus_cf[:], cf_lanes[:], ACT.Copy, scale=-1.0)
-        nc.scalar.copy(ts_window[0:1, :], ts_row[:])
-
         w_rows = W.rearrange("(m t) k -> m t k", t=LANES)
         h_rows = hT.rearrange("(p t) n -> p t n", t=LANES)
         out_rows = out_0.rearrange("(p t) n -> p t n", t=LANES)
+        halves = [slice(v * HALF, (v + 1) * HALF) for v in range(2)]
 
-        g_raw = sb.tile([P, LANES, SLOTS], F32, name="g_raw")
-        nc.sync.dma_start(g_raw[:], G.rearrange("(p j) i -> p j i", j=LANES))
+        offsets = sb.tile([P, SLOTS // 16], U16, name="offsets")
+        halves_of_list = [offsets[:, v * HALF // 16 : (v + 1) * HALF // 16] for v in range(2)]
+        ts_window = sb.tile([P, ITEMS], F32, name="ts_window")
+        x_raw = [sb.tile([P, 2, K], F32, name="x_raw%d" % v) for v in range(2)]
+        cf_lanes = sb.tile([P, LANES], F32, name="cf_lanes")
+        g_raw = sb.tile([P, LANES, SLOTS], F32, name="g_raw", align_bytes=64)
         h_window = [sb.tile([P, ITEMS], F32, name="h_window%d" % t, align_bytes=64) for t in range(LANES)]
-        for t in range(LANES):
+        w_raw = [sb.tile([P, K], F32, name="w_raw%d" % t) for t in range(LANES)]
+
+        nc.sync.dma_start(ts_window[TS_ROW:P, :], ts[0:1, :])
+        nc.sync.dma_start(offsets[:], offs)
+        nc.sync.dma_start(g_raw[:], G.rearrange("(p j) i -> p j i", j=LANES))
+        nc.sync.dma_start(x_raw[0][:], x_rows[:, 0:2, :])
+        nc.sync.dma_start(cf_lanes[:], cf.rearrange("(p t) o -> p (t o)", t=LANES))
+        nc.sync.dma_start(x_raw[1][:], x_rows[:, 2:4, :])
+        for t in range(LANES - 1):
             nc.sync.dma_start(h_window[t][:], h_rows[:, t, :])
-        w_parts = [w_rows[:, 0:1, :], w_rows[:, 2:3, :], w_rows[:, 1:LANES:2, :]]
-        w_raw = []
-        for n, part in enumerate(w_parts):
-            w_raw.append(sb.tile([P, part.shape[1], K], F32, name="w_raw%d" % n))
-            nc.sync.dma_start(w_raw[n][:], part)
+        nc.sync.dma_start(w_raw[0][:], w_rows[:, 0, :])
+        nc.sync.dma_start(h_window[LANES - 1][:], h_rows[:, LANES - 1, :])
+        for t in range(1, LANES):
+            nc.sync.dma_start(w_raw[t][:], w_rows[:, t, :])
+
+        nc.vector.memset(ts_window[0:TS_ROW, :], 0.0)
+        out_window = {}
+        for t in range(2):
+            out_window.update({t: sb.tile([P, ITEMS], F32, name="out_window%d" % t)})
+            nc.vector.memset(out_window[t][:], 0.0)
 
         ident = sb.tile([P, P], F32, name="ident")
         make_identity(nc, ident[:])
@@ -93,190 +93,164 @@ def tile_attend_gtower_tnh_E_pl_kernel(tc, W, xT, G, hT, cf, ts, offs, out_0, ou
                 bank[:, 0 : 2 * lanes, :].rearrange("p (t u) m -> p t m u", u=2),
             )
 
-        x_grouped = sb.tile([P, K, LANES], BF16, name="x_grouped", align_bytes=64)
-        for v in range(2):
-            x_rounded = sb.tile([P, 2, 2, P, 2], BF16, name="x_rounded%d" % v)
-            round_rows(nc.vector.tensor_copy, x_rounded[:], x_raw[v][:])
-            turn_rows(x_grouped[:, 2 * v * P : 2 * (v + 1) * P, :], x_rounded[:], 2)
-
         ts_listed = sb.tile([P, SLOTS], F32, name="ts_listed")
-        nc.vector.tensor_copy(ts_listed[:], ts_window[:].indirect(offsets[:]))
+        nc.scalar.activation(ts_listed[:], ts_window[:].indirect(offsets[:]), ACT.Copy)
+        g_grouped = sb.tile([P, SLOTS, LANES], BF16, name="g_grouped", align_bytes=64)
+        g_by_slot = g_raw[:].rearrange("p j i -> p i j")
+        nc.vector.tensor_copy(g_grouped[:, :VECTOR_SLOTS, :], g_by_slot[:, :VECTOR_SLOTS, :])
+        nc.scalar.copy(g_grouped[:, VECTOR_SLOTS:, :], g_by_slot[:, VECTOR_SLOTS:, :])
+        g_codes = sb.tile([P, SLOTS], U32, name="g_codes", align_bytes=64)
+        g_scales = sb.tile([P, SLOTS], U8, name="g_scales", align_bytes=64)
+        quantize(g_grouped[:], g_codes[:], g_scales[:], E5M2)
+
         ts_bank = turn.tile([P, LANES, P], F32, name="bank")
         for b in range(BLOCKS):
             nc.tensor.transpose(ts_bank[:, b, :], ts_listed[:, b * P : (b + 1) * P], ident[:])
         ts_columns = sb.tile([P, BLOCKS], F32, name="ts_columns")
-        nc.scalar.copy(ts_columns[:], ts_bank[:, :, 0])
+        nc.scalar.copy(ts_columns[:], ts_bank[:, :, TS_ROW])
+
+        spread_bank = turn.tile([P, LANES, P], F32, name="bank")
+        for b in range(BLOCKS):
+            nc.tensor.transpose(spread_bank[:, b, :], ts_columns[:, b : b + 1].to_broadcast([P, P]), ident[:])
+        minus_ts = sb.tile([P, SLOTS], F32, name="minus_ts")
+        nc.scalar.activation(minus_ts[:], spread_bank[:].rearrange("p b n -> p (b n)"), ACT.Copy, scale=-1.0)
 
         x_codes = sb.tile([P, K], U32, name="x_codes", align_bytes=64)
         x_scales = sb.tile([P, K], U8, name="x_scales", align_bytes=64)
-        g_grouped = sb.tile([P, SLOTS, LANES], BF16, name="g_grouped", align_bytes=64)
-        g_by_slot = g_raw[:].rearrange("p j i -> p i j")
-        nc.vector.tensor_copy(g_grouped[:, :HALF, :], g_by_slot[:, :HALF, :])
-        nc.vector.tensor_copy(g_grouped[:, HALF:VECTOR_SLOTS, :], g_by_slot[:, HALF:VECTOR_SLOTS, :])
-        nc.scalar.copy(g_grouped[:, VECTOR_SLOTS:, :], g_by_slot[:, VECTOR_SLOTS:, :])
-        e5_codes = sb.tile([P, 2 * SLOTS], U32, name="e5_codes", align_bytes=64)
-        e5_scales = sb.tile([P, 2 * SLOTS], U8, name="e5_scales", align_bytes=64)
-        g_codes, dz_codes = e5_codes[:, :SLOTS], e5_codes[:, SLOTS:]
-        g_scales, dz_scales = e5_scales[:, :SLOTS], e5_scales[:, SLOTS:]
-        quantize(g_grouped[:, :HALF, :], g_codes[:, :HALF], g_scales[:, :HALF], E5M2)
-        quantize(x_grouped[:], x_codes[:], x_scales[:], E4M3)
-        quantize(g_grouped[:, HALF:, :], g_codes[:, HALF:], g_scales[:, HALF:], E5M2)
-        second_window = sb.tile([P, ITEMS], F32, name="second_window", tag="g_grouped", align_bytes=64)
-        nc.gpsimd.memset(second_window[:], 0.0)
-        out_window.update({2: second_window})
+        for v in range(2):
+            x_rounded = sb.tile([P, 2, 2, P, 2], BF16, name="x_rounded%d" % v, align_bytes=64)
+            round_rows(nc.vector.tensor_copy, x_rounded[:], x_raw[v][:])
+            x_grouped = sb.tile([P, 2 * P, LANES], BF16, name="x_grouped%d" % v, align_bytes=64)
+            turn_rows(x_grouped[:], x_rounded[:], 2)
+            quantize(x_grouped[:], x_codes[:, halves[v]], x_scales[:, halves[v]], E4M3)
 
-        w_codes = sb.tile([P, K], U32, name="w_codes", align_bytes=64)
-        w_scales = sb.tile([P, K], U8, name="w_scales", align_bytes=64)
-
-        dv_by_slot = []
-        for b in range(BLOCKS):
-            block = slice(b * P, (b + 1) * P)
-            slot_sums = turn.tile([P, K], F32, name="bank")
+        def product(sums, codes, scales, lane, e5_codes, e5_scales):
+            rows = slice(lane * P, (lane + 1) * P)
             nc.tensor.matmul_mx(
-                out=slot_sums[:],
-                lhsT=g_codes[:, block].bitcast(E5M2),
-                lhsT_scale=g_scales[:, block],
-                rhs=x_codes[:].bitcast(E4M3),
-                rhs_scale=x_scales[:],
+                out=sums,
+                lhsT=codes[:, rows].bitcast(E4M3),
+                lhsT_scale=scales[:, rows],
+                rhs=e5_codes.bitcast(E5M2),
+                rhs_scale=e5_scales,
                 start=True,
                 stop=True,
             )
-            scaled = sb.tile([P, K], F32, name="scaled%d" % b)
-            if b < BLOCKS - 1:
-                nc.scalar.activation(scaled[:], slot_sums[:], ACT.Copy, scale=ts_columns[:, b : b + 1])
-            else:
-                nc.vector.tensor_scalar_mul(scaled[:], slot_sums[:], ts_columns[:, b : b + 1])
-            dv_by_slot.append(scaled)
 
-        last_window = sb.tile([P, ITEMS], F32, name="last_window", tag="x_codes", align_bytes=64)
-        nc.gpsimd.memset(last_window[:], 0.0)
-        out_window.update({3: last_window})
         factors = []
-        squares = []
+        for t in range(LANES):
+            dv = acc.tile([P, SLOTS], F32, name="sums%d" % t)
+            product(dv[:], x_codes, x_scales, t, g_codes[:], g_scales[:])
+            factor = sb.tile([P, SLOTS], F32, name="factor%d" % t)
+            nc.vector.scalar_tensor_tensor(factor[:], dv[:], cf_lanes[:, t : t + 1], minus_ts[:], ALU.mult, ALU.mult)
+            factors.append(factor)
 
-        def gather_and_square(t, part, offsets_part, width, h_tag, square_tag):
-            h = sb.tile([P, width], F32, name="h%d_%d" % (t, part), tag=h_tag, align_bytes=64)
-            nc.vector.tensor_copy(h[:], h_window[t][:].indirect(offsets_part))
-            h_squared = sb.tile([P, width], F32, name="h_squared%d_%d" % (t, part), tag=square_tag)
+        for t, tag in ((2, "x_grouped1"), (3, "x_codes")):
+            out_window.update({t: sb.tile([P, ITEMS], F32, name="out_window%d" % t, tag=tag, align_bytes=64)})
+            nc.gpsimd.memset(out_window[t][:], 0.0)
+
+        squares = []
+        for t in range(LANES - 1):
+            h = sb.tile([P, SLOTS], F32, name="h%d" % t, tag="x_rounded1" if t == 0 else "h%d" % t, align_bytes=64)
+            nc.scalar.activation(h[:], h_window[t][:].indirect(offsets[:]), ACT.Copy)
+            h_squared = sb.tile([P, SLOTS], F32, name="h_squared%d" % t)
             nc.scalar.activation(h_squared[:], h[:], ACT.Square)
             squares.append(h_squared)
 
-        h_tags = ("h0", "x_scales", "h2")
-        square_tags = ("ts_columns", "h_squared1", "h_squared2")
-        for t in range(LANES):
-            turned = acc.tile([P, BLOCKS, P], F32, name="sums%d" % t)
-            for b in range(BLOCKS):
-                nc.tensor.transpose(turned[:, b, :], dv_by_slot[b][:, t * P : (t + 1) * P], ident[:])
-            factor = sb.tile([P, SLOTS], F32, name="factor%d" % t)
-            nc.scalar.activation(
-                factor[:], turned[:].rearrange("p b n -> p (b n)"), ACT.Copy, scale=minus_cf[:, t : t + 1]
-            )
-            factors.append(factor)
-            if t < LANES - 1:
-                gather_and_square(t, 0, offsets[:], SLOTS, h_tags[t], square_tags[t])
+        def slope_times(dz_lane, square, factor):
+            nc.vector.scalar_tensor_tensor(dz_lane, square, 1.0, factor, ALU.subtract, ALU.mult)
 
-        dz_low = sb.tile([P, 2, SLOTS], BF16, name="dz_low", tag="h_window2", align_bytes=64)
+        dz_low = sb.tile([P, 2, SLOTS], BF16, name="dz_low")
         for t in range(2):
-            nc.vector.scalar_tensor_tensor(dz_low[:, t, :], squares[t][:], 1.0, factors[t][:], ALU.subtract, ALU.mult)
-        dz_grouped = sb.tile([P, SLOTS, LANES], BF16, name="dz_grouped", align_bytes=64)
+            slope_times(dz_low[:, t, :], squares[t][:], factors[t][:])
+        dz_grouped = placed.tile([P, SLOTS, LANES], BF16, name="dz_grouped", align_bytes=64, offset=0)
         nc.vector.tensor_copy(dz_grouped[:, :, 0:2], dz_low[:].rearrange("p t i -> p i t"))
+        dz_high = sb.tile([P, 2, SLOTS], BF16, name="dz_high")
+        slope_times(dz_high[:, 0, :], squares[2][:], factors[2][:])
 
-        w_codes_parts = (slice(0, P), slice(P, 2 * P), slice(2 * P, K))
-        w_grouped = []
+        def turn_w(t, grouped):
+            rounded = sb.tile([P, 1, 2, P, 2], BF16, name="w_rounded%d" % t)
+            round_rows(nc.scalar.copy, rounded[:], w_raw[t][:].unsqueeze(1))
+            turn_rows(grouped, rounded[:], 1)
 
-        def turn_w(n):
-            lanes = w_raw[n].shape[1]
-            rounded = sb.tile([P, lanes, 2, P, 2], BF16, name="w_rounded%d" % n)
-            round_rows(nc.scalar.copy, rounded[:], w_raw[n][:])
-            grouped = sb.tile([P, lanes * P, LANES], BF16, name="w_grouped%d" % n, align_bytes=64)
-            turn_rows(grouped[:], rounded[:], lanes)
-            w_grouped.append(grouped)
+        w_grouped0 = sb.tile([P, P, LANES], BF16, name="w_grouped0", align_bytes=64)
+        turn_w(0, w_grouped0[:])
 
-        def quantize_w(n):
-            quantize(w_grouped[n][:], w_codes[:, w_codes_parts[n]], w_scales[:, w_codes_parts[n]], E4M3)
-
-        turn_w(0)
-        last_squared = sb.tile([P, 2, HALF], F32, name="last_squared", tag="w_raw0")
-        for v, tag in enumerate(("h_window2", "h_last1")):
-            h = sb.tile([P, HALF], F32, name="h_last%d" % v, tag=tag, align_bytes=64)
-            nc.vector.tensor_copy(h[:], h_window[LANES - 1][:].indirect(halves_of_list[v]))
-            nc.scalar.activation(last_squared[:, v, :], h[:], ACT.Square)
-        dz_high = sb.tile([P, 2, 2, HALF], BF16, name="dz_high", tag="h_window3", align_bytes=64)
-        halves = [slice(v * HALF, (v + 1) * HALF) for v in range(2)]
-
-        def high_lane(t, v, square):
-            nc.vector.scalar_tensor_tensor(
-                dz_high[:, v, t - 2, :], square, 1.0, factors[t][:, halves[v]], ALU.subtract, ALU.mult
+        h_last = [sb.tile([P, HALF], F32, name="h_last%d" % v) for v in range(2)]
+        nc.vector.tensor_copy(h_last[0][:], h_window[LANES - 1][:].indirect(halves_of_list[0]))
+        nc.scalar.activation(h_last[1][:], h_window[LANES - 1][:].indirect(halves_of_list[1]), ACT.Copy)
+        w_codes = sb.tile([P, K], U32, name="w_codes", tag="h_window3", align_bytes=64)
+        w_scales = sb.tile([P, K], U8, name="w_scales", align_bytes=64)
+        quantize(w_grouped0[:], w_codes[:, :P], w_scales[:, :P], E4M3)
+        for v in range(2):
+            last_squared = sb.tile([P, HALF], F32, name="last_squared%d" % v)
+            nc.scalar.activation(last_squared[:], h_last[v][:], ACT.Square)
+            slope_times(dz_high[:, 1, halves[v]], last_squared[:], factors[LANES - 1][:, halves[v]])
+        for v in range(2):
+            nc.vector.tensor_copy(
+                dz_grouped[:, halves[v], 2:LANES], dz_high[:, :, halves[v]].rearrange("p t i -> p i t")
             )
-
-        def place_high(v):
-            nc.vector.tensor_copy(dz_grouped[:, halves[v], 2:LANES], dz_high[:, v].rearrange("p t i -> p i t"))
-
-        def quantize_dz(v):
+        dz_codes = sb.tile([P, SLOTS], U32, name="dz_codes", align_bytes=64)
+        dz_scales = sb.tile([P, SLOTS], U8, name="dz_scales", align_bytes=64)
+        for v in range(2):
             quantize(dz_grouped[:, halves[v], :], dz_codes[:, halves[v]], dz_scales[:, halves[v]], E5M2)
+        w_grouped1 = placed.tile([P, P, LANES], BF16, name="w_grouped1", align_bytes=64, offset=4096)
+        turn_w(1, w_grouped1[:])
+        quantize(w_grouped1[:], w_codes[:, P : 2 * P], w_scales[:, P : 2 * P], E4M3)
 
-        high_lane(2, 0, squares[2][:, halves[0]])
-        high_lane(3, 0, last_squared[:, 0, :])
-        high_lane(2, 1, squares[2][:, halves[1]])
-        place_high(0)
-        high_lane(3, 1, last_squared[:, 1, :])
-        quantize_w(0)
-        quantize_dz(0)
-        early_sums = turn.tile([P, SLOTS], F32, name="bank")
-        nc.tensor.matmul_mx(
-            out=early_sums[:],
-            lhsT=w_codes[:, :P].bitcast(E4M3),
-            lhsT_scale=w_scales[:, :P],
-            rhs=e5_codes[:, HALF : HALF + SLOTS].bitcast(E5M2),
-            rhs_scale=e5_scales[:, HALF : HALF + SLOTS],
-            start=True,
-            stop=True,
-        )
-        place_high(1)
-        quantize_dz(1)
-        turn_w(1)
-        quantize_w(1)
+        first_sums = []
+        for v in range(2):
+            sums = turn.tile([P, SLOTS], F32, name="bank")
+            product(sums[:, :HALF], w_codes, w_scales, 0, dz_codes[:, halves[v]], dz_scales[:, halves[v]])
+            first_sums.append(sums)
+        sums1 = acc.tile([P, SLOTS], F32, name="sums1")
+        product(sums1[:], w_codes, w_scales, 1, dz_codes[:], dz_scales[:])
 
-        def second_product(t):
-            place = SCATTER_ORDER.index(t)
-            rows = slice(place * P, (place + 1) * P)
-            de_sums = acc.tile([P, SLOTS], F32, name="sums%d" % t)
-            nc.tensor.matmul_mx(
-                out=de_sums[:],
-                lhsT=w_codes[:, rows].bitcast(E4M3),
-                lhsT_scale=w_scales[:, rows],
-                rhs=dz_codes.bitcast(E5M2),
-                rhs_scale=dz_scales,
-                start=True,
-                stop=True,
-            )
-            return de_sums
+        def scatter_half(t, v, sums, de):
+            if t % 2 == 0:
+                nc.scalar.copy(de, sums)
+                nc.scalar.activation(out_window[t][:].indirect(halves_of_list[v]), de, ACT.Copy)
+            else:
+                nc.vector.tensor_copy(de, sums)
+                nc.vector.tensor_copy(out_window[t][:].indirect(halves_of_list[v]), de)
 
-        def scatter_lane(t, de_sums, tag):
-            de = sb.tile([P, SLOTS], F32, name="de%d" % t, tag=tag)
-            nc.scalar.copy(de[:], de_sums[:])
-            nc.vector.tensor_copy(out_window[t][:].indirect(offsets[:]), de[:])
+        def store_lane(t):
             nc.sync.dma_start(out_rows[:, t, :], out_window[t][:])
 
-        def scatter_first(v, de_sums, tag):
-            de = sb.tile([P, HALF], F32, name="de0_%d" % v, tag=tag)
-            nc.scalar.copy(de[:], de_sums[:, HALF:])
-            nc.vector.tensor_copy(out_window[0][:].indirect(halves_of_list[v]), de[:])
+        scatter_half(0, 0, first_sums[0][:, :HALF], sb.tile([P, HALF], F32, name="de0_0")[:])
+        scatter_half(1, 0, sums1[:, halves[0]], sb.tile([P, HALF], F32, name="de1_0")[:])
 
-        scatter_first(0, early_sums, "de0_early")
-        sums0 = second_product(0)
-        sums2 = second_product(2)
-        turn_w(2)
-        quantize_w(2)
-        scatter_first(1, sums0, "w_rounded2")
-        nc.sync.dma_start(out_rows[:, 0, :], out_window[0][:])
-        window = sb.tile([P, ITEMS], F32, name="third_window", tag="w_grouped2", align_bytes=64)
-        nc.gpsimd.memset(window[:], 0.0)
-        out_window.update({1: window})
-        sums1 = second_product(1)
-        sums3 = second_product(3)
+        w_rounded_late = placed.tile([P, 2, 2, P, 2], BF16, name="w_rounded_late", align_bytes=64, offset=3072)
+        for t in range(2, LANES):
+            nc.gpsimd.tensor_scalar(
+                w_rounded_late[:, t - 2].rearrange("m u p e -> m p u e"),
+                w_raw[t][:].rearrange("m (p u e) -> m p u e", u=2, e=2),
+                1.0,
+                0.0,
+                ALU.mult,
+                ALU.add,
+            )
+        w_grouped_late = sb.tile([P, 2 * P, LANES], BF16, name="w_grouped_late", align_bytes=64)
+        turn_rows(w_grouped_late[:], w_rounded_late[:], 2)
+        quantize(w_grouped_late[:], w_codes[:, 2 * P :], w_scales[:, 2 * P :], E4M3)
 
-        pair_tags = ("e5_codes", "e5_scales", "w_codes", "w_scales")
+        de0_late = placed.tile([P, HALF], F32, name="de0_1", align_bytes=64, offset=3072)
+        scatter_half(0, 1, first_sums[1][:, :HALF], de0_late[:])
+        de1_late = sb.tile([P, HALF], F32, name="de1_1", tag="w_grouped_late", align_bytes=64)
+        scatter_half(1, 1, sums1[:, halves[1]], de1_late[:])
+        store_lane(0)
+        store_lane(1)
+
+        late_sums = {}
+        for t in range(2, LANES):
+            late_sums.update({t: acc.tile([P, SLOTS], F32, name="sums%d" % t)})
+            product(late_sums[t][:], w_codes, w_scales, t, dz_codes[:], dz_scales[:])
+        for t in range(2, LANES):
+            for v in range(2):
+                de = sb.tile([P, HALF], F32, name="de%d_%d" % (t, v), align_bytes=64)
+                scatter_half(t, v, late_sums[t][:, halves[v]], de[:])
+            store_lane(t)
+
+        pair_tags = ("pairs0", "pairs1", "de2_0", "de2_1")
         pairs = [
             sb.tile([P, 2, CHUNK, 2], BF16, name="pairs%d" % c, tag=pair_tags[c], align_bytes=64) for c in range(CHUNKS)
         ]
@@ -284,48 +258,40 @@ def tile_attend_gtower_tnh_E_pl_kernel(tc, W, xT, G, hT, cf, ts, offs, out_0, ou
         def round_lane(copy, t, c):
             copy(pairs[c][:, t // 2, :, t % 2], out_window[t][:, c * CHUNK : (c + 1) * CHUNK])
 
-        def round_low_lane(t):
-            for c in range(CHUNKS):
-                round_lane(nc.gpsimd.tensor_copy if c == CHUNKS - 1 else nc.scalar.copy, t, c)
-
-        scatter_lane(2, sums2, "de2")
-        scatter_lane(1, sums1, "de1")
-        round_low_lane(0)
-        round_lane(nc.scalar.copy, 2, 0)
-        scatter_lane(3, sums3, "de2")
-        for c in range(1, CHUNKS):
-            round_lane(nc.scalar.copy, 2, c)
-        round_low_lane(1)
-        round_lane(nc.vector.tensor_copy, 3, 0)
-        for c in range(1, CHUNKS):
-            round_lane(nc.scalar.copy, 3, c)
-
         y_scales = sb.tile([P, CHUNK], U8, name="y_scales", align_bytes=64)
         words = out_1[0].rearrange("p n t -> p (n t)").bitcast(I32)
         y_grouped = [sb.tile([P, CHUNK, LANES], BF16, name="y_grouped%d" % c, align_bytes=64) for c in range(CHUNKS)]
         y_codes = [sb.tile([P, CHUNK], U32, name="y_codes%d" % c, align_bytes=64) for c in range(CHUNKS)]
 
-        def weave(copy, dtype, c, columns):
+        def weave(copy, dtype, c):
             woven = y_grouped[c][:].rearrange("p n t -> p (n t)").bitcast(dtype).rearrange("p (n u) -> p n u", u=2)
             apart = pairs[c][:].rearrange("p u n e -> p (u n e)").bitcast(dtype).rearrange("p (u n) -> p n u", u=2)
-            copy(woven[:, columns, :], apart[:, columns, :])
+            copy(woven, apart)
 
-        def finish(c, *parts):
-            for columns in parts:
-                quantize(y_grouped[c][:, columns, :], y_codes[c][:, columns], y_scales[4 * c : P, columns], E4M3)
+        def finish(c):
+            quantize(y_grouped[c][:], y_codes[c][:], y_scales[4 * c : P, :], E4M3)
             nc.sync.dma_start(words[:, c * CHUNK : (c + 1) * CHUNK], y_codes[c][:].bitcast(I32))
 
-        whole, low, high = slice(0, CHUNK), slice(0, CHUNK // 2), slice(CHUNK // 2, CHUNK)
-        weave(nc.vector.tensor_copy, I32, 0, whole)
-        weave(nc.vector.tensor_copy, I32, 1, whole)
-        finish(0, whole)
-        weave(nc.vector.tensor_copy, I32, 2, low)
-        weave(nc.scalar.copy, U32, 2, high)
-        weave(nc.scalar.copy, U32, 3, low)
-        weave(nc.scalar.copy, U32, 3, high)
-        finish(1, whole)
-        finish(2, whole)
-        finish(3, low, high)
+        for c in range(2):
+            for t in range(2):
+                round_lane(nc.gpsimd.tensor_copy, t, c)
+        for t in range(LANES):
+            round_lane(nc.scalar.copy, t, 2)
+        for t in range(2):
+            round_lane(nc.scalar.copy, t, 3)
+        for c in range(2):
+            for t in range(2, LANES):
+                round_lane(nc.vector.tensor_copy, t, c)
+        weave(nc.vector.tensor_copy, I32, 0)
+        for t in range(2, LANES):
+            round_lane(nc.vector.tensor_copy, t, 3)
+        weave(nc.scalar.copy, U32, 3)
+        finish(0)
+        weave(nc.vector.tensor_copy, I32, 1)
+        weave(nc.vector.tensor_copy, I32, 2)
+        finish(1)
+        finish(2)
+        finish(3)
 
         scale_rows = out_2[0].bitcast(I32).rearrange("r (c n) -> c r n", c=CHUNKS)
         for q in range(QUADRANTS):

@@ -35,9 +35,10 @@ def tile_attend_gtower_tnh_E_pl_kernel(tc, W, xT, G, hT, cf, ts, offs, out_0, ou
     nc = tc.nc
     with ExitStack() as ctx:
         sb = ctx.enter_context(tc.tile_pool(name="sb", bufs=1))
-        placed = ctx.enter_context(tc.tile_pool(name="placed", bufs=1))
-        turn = ctx.enter_context(tc.psum_pool(name="turn", bufs=4))
-        acc = ctx.enter_context(tc.psum_pool(name="acc", bufs=1))
+        psum = ctx.enter_context(tc.psum_pool(name="psum", bufs=1))
+
+        def bank(n):
+            return psum.tile([P, SLOTS], F32, name="bank%d" % n)
 
         x_rows = xT.rearrange("(m t) k -> m t k", t=LANES)
         w_rows = W.rearrange("(m t) k -> m t k", t=LANES)
@@ -54,12 +55,12 @@ def tile_attend_gtower_tnh_E_pl_kernel(tc, W, xT, G, hT, cf, ts, offs, out_0, ou
         h_window = [sb.tile([P, ITEMS], F32, name="h_window%d" % t, align_bytes=64) for t in range(LANES)]
         w_raw = [sb.tile([P, K], F32, name="w_raw%d" % t) for t in range(LANES)]
 
+        nc.sync.dma_start(cf_lanes[:], cf.rearrange("(p t) o -> p (t o)", t=LANES))
         nc.sync.dma_start(ts_window[TS_ROW:P, :], ts[0:1, :])
         nc.sync.dma_start(offsets[:], offs)
-        nc.sync.dma_start(g_raw[:], G.rearrange("(p j) i -> p j i", j=LANES))
         nc.sync.dma_start(x_raw[0][:], x_rows[:, 0:2, :])
-        nc.sync.dma_start(cf_lanes[:], cf.rearrange("(p t) o -> p (t o)", t=LANES))
         nc.sync.dma_start(x_raw[1][:], x_rows[:, 2:4, :])
+        nc.sync.dma_start(g_raw[:], G.rearrange("(p j) i -> p j i", j=LANES))
         for t in range(LANES - 1):
             nc.sync.dma_start(h_window[t][:], h_rows[:, t, :])
         nc.sync.dma_start(w_raw[0][:], w_rows[:, 0, :])
@@ -67,11 +68,16 @@ def tile_attend_gtower_tnh_E_pl_kernel(tc, W, xT, G, hT, cf, ts, offs, out_0, ou
         for t in range(1, LANES):
             nc.sync.dma_start(w_raw[t][:], w_rows[:, t, :])
 
-        nc.vector.memset(ts_window[0:TS_ROW, :], 0.0)
-        out_window = {}
-        for t in range(2):
-            out_window.update({t: sb.tile([P, ITEMS], F32, name="out_window%d" % t)})
-            nc.vector.memset(out_window[t][:], 0.0)
+        nc.gpsimd.memset(ts_window[0:TS_ROW, :], 0.0)
+        out_window = {0: sb.tile([P, ITEMS], F32, name="out_window0")}
+        nc.vector.memset(out_window[0][:], 0.0)
+
+        def clear_window(t, window):
+            out_window.update({t: window})
+            nc.gpsimd.memset(window[:], 0.0)
+
+        minus_cf = sb.tile([P, LANES], F32, name="minus_cf")
+        nc.scalar.activation(minus_cf[:], cf_lanes[:], ACT.Copy, scale=-1.0)
 
         ident = sb.tile([P, P], F32, name="ident")
         make_identity(nc, ident[:])
@@ -82,38 +88,41 @@ def tile_attend_gtower_tnh_E_pl_kernel(tc, W, xT, G, hT, cf, ts, offs, out_0, ou
         def round_rows(copy, rounded, raw):
             copy(rounded.rearrange("m t u p e -> m t p u e"), raw.rearrange("m t (p u e) -> m t p u e", u=2, e=2))
 
-        def turn_rows(grouped, rounded, lanes):
-            rounded_pairs = rounded.rearrange("m t u p e -> m (t u p e)").bitcast(F32)
+        def turn_pairs(rounded_parts, bank_number):
+            runs = []
+            for part in rounded_parts:
+                part_pairs = part.rearrange("m t u p e -> m (t u p e)").bitcast(F32)
+                runs.extend(part_pairs[:, n * P : (n + 1) * P] for n in range(2 * part.shape[1]))
+            turned = bank(bank_number)
+            for run in range(len(runs)):
+                nc.tensor.transpose(turned[:, run * P : (run + 1) * P], runs[run], ident[:])
+            return turned
+
+        def group_pairs(grouped, turned, lanes):
             grouped_pairs = grouped.rearrange("p c j -> p (c j)").bitcast(F32)
-            bank = turn.tile([P, LANES, P], F32, name="bank")
-            for run in range(2 * lanes):
-                nc.tensor.transpose(bank[:, run, :], rounded_pairs[:, run * P : (run + 1) * P], ident[:])
             nc.scalar.copy(
                 grouped_pairs.rearrange("p (t m u) -> p t m u", t=lanes, u=2),
-                bank[:, 0 : 2 * lanes, :].rearrange("p (t u) m -> p t m u", u=2),
+                turned[:, 0 : 2 * lanes * P].rearrange("p (t u m) -> p t m u", t=lanes, u=2),
             )
+
+        def turn_rows(grouped, rounded_parts, lanes, bank_number):
+            group_pairs(grouped, turn_pairs(rounded_parts, bank_number), lanes)
 
         ts_listed = sb.tile([P, SLOTS], F32, name="ts_listed")
         nc.scalar.activation(ts_listed[:], ts_window[:].indirect(offsets[:]), ACT.Copy)
-        g_grouped = sb.tile([P, SLOTS, LANES], BF16, name="g_grouped", align_bytes=64)
-        g_by_slot = g_raw[:].rearrange("p j i -> p i j")
-        nc.vector.tensor_copy(g_grouped[:, :VECTOR_SLOTS, :], g_by_slot[:, :VECTOR_SLOTS, :])
-        nc.scalar.copy(g_grouped[:, VECTOR_SLOTS:, :], g_by_slot[:, VECTOR_SLOTS:, :])
-        g_codes = sb.tile([P, SLOTS], U32, name="g_codes", align_bytes=64)
-        g_scales = sb.tile([P, SLOTS], U8, name="g_scales", align_bytes=64)
-        quantize(g_grouped[:], g_codes[:], g_scales[:], E5M2)
-
-        ts_bank = turn.tile([P, LANES, P], F32, name="bank")
+        ts_bank = bank(0)
         for b in range(BLOCKS):
-            nc.tensor.transpose(ts_bank[:, b, :], ts_listed[:, b * P : (b + 1) * P], ident[:])
+            nc.tensor.transpose(ts_bank[:, b * P : (b + 1) * P], ts_listed[:, b * P : (b + 1) * P], ident[:])
         ts_columns = sb.tile([P, BLOCKS], F32, name="ts_columns")
-        nc.scalar.copy(ts_columns[:], ts_bank[:, :, TS_ROW])
+        nc.scalar.copy(ts_columns[:], ts_bank[:, TS_ROW::P])
 
-        spread_bank = turn.tile([P, LANES, P], F32, name="bank")
+        spread_bank = bank(1)
         for b in range(BLOCKS):
-            nc.tensor.transpose(spread_bank[:, b, :], ts_columns[:, b : b + 1].to_broadcast([P, P]), ident[:])
-        minus_ts = sb.tile([P, SLOTS], F32, name="minus_ts")
-        nc.scalar.activation(minus_ts[:], spread_bank[:].rearrange("p b n -> p (b n)"), ACT.Copy, scale=-1.0)
+            nc.tensor.transpose(
+                spread_bank[:, b * P : (b + 1) * P], ts_columns[:, b : b + 1].to_broadcast([P, P]), ident[:]
+            )
+        ts_spread = sb.tile([P, SLOTS], F32, name="ts_spread")
+        nc.scalar.copy(ts_spread[:], spread_bank[:])
 
         x_codes = sb.tile([P, K], U32, name="x_codes", align_bytes=64)
         x_scales = sb.tile([P, K], U8, name="x_scales", align_bytes=64)
@@ -121,8 +130,15 @@ def tile_attend_gtower_tnh_E_pl_kernel(tc, W, xT, G, hT, cf, ts, offs, out_0, ou
             x_rounded = sb.tile([P, 2, 2, P, 2], BF16, name="x_rounded%d" % v, align_bytes=64)
             round_rows(nc.vector.tensor_copy, x_rounded[:], x_raw[v][:])
             x_grouped = sb.tile([P, 2 * P, LANES], BF16, name="x_grouped%d" % v, align_bytes=64)
-            turn_rows(x_grouped[:], x_rounded[:], 2)
+            turn_rows(x_grouped[:], [x_rounded[:]], 2, 2 + v)
             quantize(x_grouped[:], x_codes[:, halves[v]], x_scales[:, halves[v]], E4M3)
+        g_grouped = sb.tile([P, SLOTS, LANES], BF16, name="g_grouped", align_bytes=64)
+        g_by_slot = g_raw[:].rearrange("p j i -> p i j")
+        nc.vector.tensor_copy(g_grouped[:, :VECTOR_SLOTS, :], g_by_slot[:, :VECTOR_SLOTS, :])
+        nc.scalar.copy(g_grouped[:, VECTOR_SLOTS:, :], g_by_slot[:, VECTOR_SLOTS:, :])
+        g_codes = sb.tile([P, SLOTS], U32, name="g_codes", align_bytes=64)
+        g_scales = sb.tile([P, SLOTS], U8, name="g_scales", align_bytes=64)
+        quantize(g_grouped[:], g_codes[:], g_scales[:], E5M2)
 
         def product(sums, codes, scales, lane, e5_codes, e5_scales):
             rows = slice(lane * P, (lane + 1) * P)
@@ -138,19 +154,18 @@ def tile_attend_gtower_tnh_E_pl_kernel(tc, W, xT, G, hT, cf, ts, offs, out_0, ou
 
         factors = []
         for t in range(LANES):
-            dv = acc.tile([P, SLOTS], F32, name="sums%d" % t)
+            dv = bank(LANES + t)
             product(dv[:], x_codes, x_scales, t, g_codes[:], g_scales[:])
             factor = sb.tile([P, SLOTS], F32, name="factor%d" % t)
-            nc.vector.scalar_tensor_tensor(factor[:], dv[:], cf_lanes[:, t : t + 1], minus_ts[:], ALU.mult, ALU.mult)
+            nc.vector.scalar_tensor_tensor(factor[:], dv[:], minus_cf[:, t : t + 1], ts_spread[:], ALU.mult, ALU.mult)
             factors.append(factor)
 
-        for t, tag in ((2, "x_grouped1"), (3, "x_codes")):
-            out_window.update({t: sb.tile([P, ITEMS], F32, name="out_window%d" % t, tag=tag, align_bytes=64)})
-            nc.gpsimd.memset(out_window[t][:], 0.0)
+        clear_window(1, sb.tile([P, ITEMS], F32, name="out_window1", tag="g_grouped", align_bytes=64))
+        clear_window(3, sb.tile([P, ITEMS], F32, name="out_window3", tag="x_codes", align_bytes=64))
 
         squares = []
         for t in range(LANES - 1):
-            h = sb.tile([P, SLOTS], F32, name="h%d" % t, tag="x_rounded1" if t == 0 else "h%d" % t, align_bytes=64)
+            h = sb.tile([P, SLOTS], F32, name="h%d" % t, tag="g_raw" if t == 0 else "h%d" % t, align_bytes=64)
             nc.scalar.activation(h[:], h_window[t][:].indirect(offsets[:]), ACT.Copy)
             h_squared = sb.tile([P, SLOTS], F32, name="h_squared%d" % t)
             nc.scalar.activation(h_squared[:], h[:], ACT.Square)
@@ -162,18 +177,19 @@ def tile_attend_gtower_tnh_E_pl_kernel(tc, W, xT, G, hT, cf, ts, offs, out_0, ou
         dz_low = sb.tile([P, 2, SLOTS], BF16, name="dz_low")
         for t in range(2):
             slope_times(dz_low[:, t, :], squares[t][:], factors[t][:])
-        dz_grouped = placed.tile([P, SLOTS, LANES], BF16, name="dz_grouped", align_bytes=64, offset=0)
+        dz_grouped = sb.tile([P, SLOTS, LANES], BF16, name="dz_grouped", align_bytes=64)
         nc.vector.tensor_copy(dz_grouped[:, :, 0:2], dz_low[:].rearrange("p t i -> p i t"))
+
+        def turn_w(t, copy):
+            rounded = sb.tile([P, 2, P, 2], BF16, name="w_rounded%d" % t)
+            copy(rounded[:].rearrange("m u p e -> m p u e"), w_raw[t][:].rearrange("m (p u e) -> m p u e", u=2, e=2))
+            grouped = sb.tile([P, P, LANES], BF16, name="w_grouped%d" % t, align_bytes=64)
+            turn_rows(grouped[:], [rounded[:].unsqueeze(1)], 1, t)
+            return grouped
+
+        w_grouped0 = turn_w(0, nc.vector.tensor_copy)
         dz_high = sb.tile([P, 2, SLOTS], BF16, name="dz_high")
         slope_times(dz_high[:, 0, :], squares[2][:], factors[2][:])
-
-        def turn_w(t, grouped):
-            rounded = sb.tile([P, 1, 2, P, 2], BF16, name="w_rounded%d" % t)
-            round_rows(nc.scalar.copy, rounded[:], w_raw[t][:].unsqueeze(1))
-            turn_rows(grouped, rounded[:], 1)
-
-        w_grouped0 = sb.tile([P, P, LANES], BF16, name="w_grouped0", align_bytes=64)
-        turn_w(0, w_grouped0[:])
 
         h_last = [sb.tile([P, HALF], F32, name="h_last%d" % v) for v in range(2)]
         nc.vector.tensor_copy(h_last[0][:], h_window[LANES - 1][:].indirect(halves_of_list[0]))
@@ -185,75 +201,78 @@ def tile_attend_gtower_tnh_E_pl_kernel(tc, W, xT, G, hT, cf, ts, offs, out_0, ou
             last_squared = sb.tile([P, HALF], F32, name="last_squared%d" % v)
             nc.scalar.activation(last_squared[:], h_last[v][:], ACT.Square)
             slope_times(dz_high[:, 1, halves[v]], last_squared[:], factors[LANES - 1][:, halves[v]])
+        w_grouped1 = turn_w(1, nc.scalar.copy)
         for v in range(2):
             nc.vector.tensor_copy(
                 dz_grouped[:, halves[v], 2:LANES], dz_high[:, :, halves[v]].rearrange("p t i -> p i t")
             )
         dz_codes = sb.tile([P, SLOTS], U32, name="dz_codes", align_bytes=64)
         dz_scales = sb.tile([P, SLOTS], U8, name="dz_scales", align_bytes=64)
-        for v in range(2):
-            quantize(dz_grouped[:, halves[v], :], dz_codes[:, halves[v]], dz_scales[:, halves[v]], E5M2)
-        w_grouped1 = placed.tile([P, P, LANES], BF16, name="w_grouped1", align_bytes=64, offset=4096)
-        turn_w(1, w_grouped1[:])
+        quantize(dz_grouped[:, halves[0], :], dz_codes[:, halves[0]], dz_scales[:, halves[0]], E5M2)
         quantize(w_grouped1[:], w_codes[:, P : 2 * P], w_scales[:, P : 2 * P], E4M3)
+        quantize(dz_grouped[:, halves[1], :], dz_codes[:, halves[1]], dz_scales[:, halves[1]], E5M2)
+        clear_window(2, sb.tile([P, ITEMS], F32, name="out_window2", tag="dz_grouped", align_bytes=64))
 
-        first_sums = []
+        first_sums = {}
         for v in range(2):
-            sums = turn.tile([P, SLOTS], F32, name="bank")
-            product(sums[:, :HALF], w_codes, w_scales, 0, dz_codes[:, halves[v]], dz_scales[:, halves[v]])
-            first_sums.append(sums)
-        sums1 = acc.tile([P, SLOTS], F32, name="sums1")
-        product(sums1[:], w_codes, w_scales, 1, dz_codes[:], dz_scales[:])
+            for t in range(2):
+                sums = bank(2 + 2 * t + v)[:, :HALF]
+                product(sums, w_codes, w_scales, t, dz_codes[:, halves[v]], dz_scales[:, halves[v]])
+                first_sums.update({(t, v): sums})
 
-        def scatter_half(t, v, sums, de):
+        def scatter_half(t, v, de):
             if t % 2 == 0:
-                nc.scalar.copy(de, sums)
                 nc.scalar.activation(out_window[t][:].indirect(halves_of_list[v]), de, ACT.Copy)
             else:
-                nc.vector.tensor_copy(de, sums)
                 nc.vector.tensor_copy(out_window[t][:].indirect(halves_of_list[v]), de)
 
         def store_lane(t):
             nc.sync.dma_start(out_rows[:, t, :], out_window[t][:])
 
-        scatter_half(0, 0, first_sums[0][:, :HALF], sb.tile([P, HALF], F32, name="de0_0")[:])
-        scatter_half(1, 0, sums1[:, halves[0]], sb.tile([P, HALF], F32, name="de1_0")[:])
-
-        w_rounded_late = placed.tile([P, 2, 2, P, 2], BF16, name="w_rounded_late", align_bytes=64, offset=3072)
+        w_rounded_late = [
+            sb.tile([P, 1, 2, P, 2], BF16, name="w_rounded%d" % t, tag=tag) for t, tag in ((2, "w_rounded2"), (3, "w_rounded1"))
+        ]
         for t in range(2, LANES):
-            nc.gpsimd.tensor_scalar(
-                w_rounded_late[:, t - 2].rearrange("m u p e -> m p u e"),
-                w_raw[t][:].rearrange("m (p u e) -> m p u e", u=2, e=2),
-                1.0,
-                0.0,
-                ALU.mult,
-                ALU.add,
-            )
-        w_grouped_late = sb.tile([P, 2 * P, LANES], BF16, name="w_grouped_late", align_bytes=64)
-        turn_rows(w_grouped_late[:], w_rounded_late[:], 2)
-        quantize(w_grouped_late[:], w_codes[:, 2 * P :], w_scales[:, 2 * P :], E4M3)
+            round_rows(nc.scalar.copy, w_rounded_late[t - 2][:], w_raw[t][:].unsqueeze(1))
+        de0 = sb.tile([P, HALF], F32, name="de0_0")
+        nc.scalar.copy(de0[:], first_sums[0, 0])
+        scatter_half(0, 0, de0[:])
+        de1 = sb.tile([P, HALF], F32, name="de1_0")
+        nc.vector.tensor_copy(de1[:], first_sums[1, 0])
+        scatter_half(1, 0, de1[:])
 
-        de0_late = placed.tile([P, HALF], F32, name="de0_1", align_bytes=64, offset=3072)
-        scatter_half(0, 1, first_sums[1][:, :HALF], de0_late[:])
+        turned_late = turn_pairs([part[:] for part in w_rounded_late], 2)
+        de0_late = sb.tile([P, HALF], F32, name="de0_1", tag="w_rounded1")
+        nc.scalar.copy(de0_late[:], first_sums[0, 1])
+        w_grouped_late = sb.tile([P, 2 * P, LANES], BF16, name="w_grouped_late", align_bytes=64)
+        group_pairs(w_grouped_late[:], turned_late, 2)
+        quantize(w_grouped_late[:], w_codes[:, 2 * P :], w_scales[:, 2 * P :], E4M3)
         de1_late = sb.tile([P, HALF], F32, name="de1_1", tag="w_grouped_late", align_bytes=64)
-        scatter_half(1, 1, sums1[:, halves[1]], de1_late[:])
+        nc.vector.tensor_copy(de1_late[:], first_sums[1, 1])
+        scatter_half(0, 1, de0_late[:])
+        scatter_half(1, 1, de1_late[:])
         store_lane(0)
         store_lane(1)
 
-        late_sums = {}
-        for t in range(2, LANES):
-            late_sums.update({t: acc.tile([P, SLOTS], F32, name="sums%d" % t)})
-            product(late_sums[t][:], w_codes, w_scales, t, dz_codes[:], dz_scales[:])
-        for t in range(2, LANES):
+        late_de = {}
+        for t in (3, 2):
+            sums = bank(LANES + t)
+            product(sums[:], w_codes, w_scales, t, dz_codes[:], dz_scales[:])
+            late_de.update({t: [sb.tile([P, HALF], F32, name="de%d_%d" % (t, v), align_bytes=64) for v in range(2)]})
             for v in range(2):
-                de = sb.tile([P, HALF], F32, name="de%d_%d" % (t, v), align_bytes=64)
-                scatter_half(t, v, late_sums[t][:, halves[v]], de[:])
+                nc.scalar.copy(late_de[t][v][:], sums[:, halves[v]])
+        for t in (3, 2):
+            for v in range(2):
+                scatter_half(t, v, late_de[t][v][:])
             store_lane(t)
 
-        pair_tags = ("pairs0", "pairs1", "de2_0", "de2_1")
-        pairs = [
-            sb.tile([P, 2, CHUNK, 2], BF16, name="pairs%d" % c, tag=pair_tags[c], align_bytes=64) for c in range(CHUNKS)
-        ]
+        pairs_early = sb.tile([P, 2, 2 * CHUNK, 2], BF16, name="pairs_early", align_bytes=64)
+        pairs = [pairs_early[:, :, :CHUNK, :], pairs_early[:, :, CHUNK:, :]]
+        for c, tag in ((2, "de2_0"), (3, "de2_1")):
+            pairs.append(sb.tile([P, 2, CHUNK, 2], BF16, name="pairs%d" % c, tag=tag, align_bytes=64)[:])
+
+        def round_early(copy, t):
+            copy(pairs_early[:, t // 2, :, t % 2], out_window[t][:, : 2 * CHUNK])
 
         def round_lane(copy, t, c):
             copy(pairs[c][:, t // 2, :, t % 2], out_window[t][:, c * CHUNK : (c + 1) * CHUNK])
@@ -263,35 +282,36 @@ def tile_attend_gtower_tnh_E_pl_kernel(tc, W, xT, G, hT, cf, ts, offs, out_0, ou
         y_grouped = [sb.tile([P, CHUNK, LANES], BF16, name="y_grouped%d" % c, align_bytes=64) for c in range(CHUNKS)]
         y_codes = [sb.tile([P, CHUNK], U32, name="y_codes%d" % c, align_bytes=64) for c in range(CHUNKS)]
 
-        def weave(copy, dtype, c):
+        def weave(copy, dtype, c, columns):
             woven = y_grouped[c][:].rearrange("p n t -> p (n t)").bitcast(dtype).rearrange("p (n u) -> p n u", u=2)
-            apart = pairs[c][:].rearrange("p u n e -> p (u n e)").bitcast(dtype).rearrange("p (u n) -> p n u", u=2)
-            copy(woven, apart)
+            apart = pairs[c].rearrange("p u n e -> p u (n e)").bitcast(dtype).rearrange("p u n -> p n u")
+            copy(woven[:, columns, :], apart[:, columns, :])
 
-        def finish(c):
-            quantize(y_grouped[c][:], y_codes[c][:], y_scales[4 * c : P, :], E4M3)
+        def finish(c, *parts):
+            for columns in parts or (slice(0, CHUNK),):
+                quantize(y_grouped[c][:, columns, :], y_codes[c][:, columns], y_scales[4 * c : P, columns], E4M3)
             nc.sync.dma_start(words[:, c * CHUNK : (c + 1) * CHUNK], y_codes[c][:].bitcast(I32))
 
-        for c in range(2):
-            for t in range(2):
-                round_lane(nc.gpsimd.tensor_copy, t, c)
-        for t in range(LANES):
-            round_lane(nc.scalar.copy, t, 2)
+        whole, low, high = slice(0, CHUNK), slice(0, CHUNK // 2), slice(CHUNK // 2, CHUNK)
         for t in range(2):
+            round_early(nc.gpsimd.tensor_copy, t)
+        for t in range(2):
+            round_lane(nc.scalar.copy, t, 2)
+        for t in range(LANES):
             round_lane(nc.scalar.copy, t, 3)
-        for c in range(2):
-            for t in range(2, LANES):
-                round_lane(nc.vector.tensor_copy, t, c)
-        weave(nc.vector.tensor_copy, I32, 0)
-        for t in range(2, LANES):
-            round_lane(nc.vector.tensor_copy, t, 3)
-        weave(nc.scalar.copy, U32, 3)
+        weave(nc.scalar.copy, U32, 3, low)
+        weave(nc.scalar.copy, U32, 3, high)
+        round_early(nc.vector.tensor_copy, 3)
+        round_lane(nc.vector.tensor_copy, 3, 2)
+        round_early(nc.vector.tensor_copy, 2)
+        round_lane(nc.vector.tensor_copy, 2, 2)
+        weave(nc.vector.tensor_copy, I32, 0, whole)
+        weave(nc.vector.tensor_copy, I32, 1, whole)
         finish(0)
-        weave(nc.vector.tensor_copy, I32, 1)
-        weave(nc.vector.tensor_copy, I32, 2)
+        weave(nc.vector.tensor_copy, I32, 2, whole)
         finish(1)
         finish(2)
-        finish(3)
+        finish(3, low, high)
 
         scale_rows = out_2[0].bitcast(I32).rearrange("r (c n) -> c r n", c=CHUNKS)
         for q in range(QUADRANTS):

@@ -53,7 +53,7 @@ def tile_attend_gtower_tnh_E_pl_kernel(tc, W, xT, G, hT, cf, ts, offs, out_0, ou
         cf_lanes = sb.tile([P, LANES], F32, name="cf_lanes")
         g_raw = sb.tile([P, LANES, SLOTS], F32, name="g_raw", align_bytes=64)
         h_window = [sb.tile([P, ITEMS], F32, name="h_window%d" % t, align_bytes=64) for t in range(LANES)]
-        w_raw = [sb.tile([P, K], F32, name="w_raw%d" % t) for t in range(LANES)]
+        w_raw = [sb.tile([P, K], F32, name="w_raw%d" % t, align_bytes=64) for t in range(LANES)]
 
         nc.sync.dma_start(cf_lanes[:], cf.rearrange("(p t) o -> p (t o)", t=LANES))
         nc.sync.dma_start(ts_window[TS_ROW:P, :], ts[0:1, :])
@@ -68,9 +68,11 @@ def tile_attend_gtower_tnh_E_pl_kernel(tc, W, xT, G, hT, cf, ts, offs, out_0, ou
         for t in range(1, LANES):
             nc.sync.dma_start(w_raw[t][:], w_rows[:, t, :])
 
-        nc.gpsimd.memset(ts_window[0:TS_ROW, :], 0.0)
-        out_window = {0: sb.tile([P, ITEMS], F32, name="out_window0")}
-        nc.vector.memset(out_window[0][:], 0.0)
+        nc.vector.memset(ts_window[0:TS_ROW, :], 0.0)
+        out_window = {}
+        for t in range(2):
+            out_window.update({t: sb.tile([P, ITEMS], F32, name="out_window%d" % t)})
+            nc.vector.memset(out_window[t][:], 0.0)
 
         def clear_window(t, window):
             out_window.update({t: window})
@@ -160,8 +162,8 @@ def tile_attend_gtower_tnh_E_pl_kernel(tc, W, xT, G, hT, cf, ts, offs, out_0, ou
             nc.vector.scalar_tensor_tensor(factor[:], dv[:], minus_cf[:, t : t + 1], ts_spread[:], ALU.mult, ALU.mult)
             factors.append(factor)
 
-        clear_window(1, sb.tile([P, ITEMS], F32, name="out_window1", tag="g_grouped", align_bytes=64))
-        clear_window(3, sb.tile([P, ITEMS], F32, name="out_window3", tag="x_codes", align_bytes=64))
+        clear_window(3, sb.tile([P, ITEMS], F32, name="out_window3", tag="g_grouped", align_bytes=64))
+        clear_window(2, sb.tile([P, ITEMS], F32, name="out_window2", tag="x_codes", align_bytes=64))
 
         squares = []
         for t in range(LANES - 1):
@@ -180,11 +182,17 @@ def tile_attend_gtower_tnh_E_pl_kernel(tc, W, xT, G, hT, cf, ts, offs, out_0, ou
         dz_grouped = sb.tile([P, SLOTS, LANES], BF16, name="dz_grouped", align_bytes=64)
         nc.vector.tensor_copy(dz_grouped[:, :, 0:2], dz_low[:].rearrange("p t i -> p i t"))
 
-        def turn_w(t, copy):
-            rounded = sb.tile([P, 2, P, 2], BF16, name="w_rounded%d" % t)
+        def gpsimd_round(rounded, values):
+            nc.gpsimd.tensor_scalar(rounded, values, 1.0, 0.0, ALU.mult, ALU.add)
+
+        def round_w(t, copy):
+            rounded = sb.tile([P, 2, P, 2], BF16, name="w_rounded%d" % t, align_bytes=64)
             copy(rounded[:].rearrange("m u p e -> m p u e"), w_raw[t][:].rearrange("m (p u e) -> m p u e", u=2, e=2))
+            return rounded[:].unsqueeze(1)
+
+        def turn_w(t, copy):
             grouped = sb.tile([P, P, LANES], BF16, name="w_grouped%d" % t, align_bytes=64)
-            turn_rows(grouped[:], [rounded[:].unsqueeze(1)], 1, t)
+            turn_rows(grouped[:], [round_w(t, copy)], 1, t)
             return grouped
 
         w_grouped0 = turn_w(0, nc.vector.tensor_copy)
@@ -201,7 +209,12 @@ def tile_attend_gtower_tnh_E_pl_kernel(tc, W, xT, G, hT, cf, ts, offs, out_0, ou
             last_squared = sb.tile([P, HALF], F32, name="last_squared%d" % v)
             nc.scalar.activation(last_squared[:], h_last[v][:], ACT.Square)
             slope_times(dz_high[:, 1, halves[v]], last_squared[:], factors[LANES - 1][:, halves[v]])
-        w_grouped1 = turn_w(1, nc.scalar.copy)
+        turned1 = turn_pairs([round_w(1, gpsimd_round)], 1)
+        turned_late = turn_pairs([round_w(t, nc.scalar.copy) for t in range(2, LANES)], 0)
+        w_grouped1 = sb.tile([P, P, LANES], BF16, name="w_grouped1", tag="w_raw3", align_bytes=64)
+        group_pairs(w_grouped1[:], turned1, 1)
+        w_grouped_late = sb.tile([P, 2 * P, LANES], BF16, name="w_grouped_late", align_bytes=64)
+        group_pairs(w_grouped_late[:], turned_late, 2)
         for v in range(2):
             nc.vector.tensor_copy(
                 dz_grouped[:, halves[v], 2:LANES], dz_high[:, :, halves[v]].rearrange("p t i -> p i t")
@@ -209,14 +222,13 @@ def tile_attend_gtower_tnh_E_pl_kernel(tc, W, xT, G, hT, cf, ts, offs, out_0, ou
         dz_codes = sb.tile([P, SLOTS], U32, name="dz_codes", align_bytes=64)
         dz_scales = sb.tile([P, SLOTS], U8, name="dz_scales", align_bytes=64)
         quantize(dz_grouped[:, halves[0], :], dz_codes[:, halves[0]], dz_scales[:, halves[0]], E5M2)
-        quantize(w_grouped1[:], w_codes[:, P : 2 * P], w_scales[:, P : 2 * P], E4M3)
         quantize(dz_grouped[:, halves[1], :], dz_codes[:, halves[1]], dz_scales[:, halves[1]], E5M2)
-        clear_window(2, sb.tile([P, ITEMS], F32, name="out_window2", tag="dz_grouped", align_bytes=64))
+        quantize(w_grouped1[:], w_codes[:, P : 2 * P], w_scales[:, P : 2 * P], E4M3)
 
         first_sums = {}
-        for v in range(2):
-            for t in range(2):
-                sums = bank(2 + 2 * t + v)[:, :HALF]
+        for t in range(2):
+            for v in range(2):
+                sums = bank(1 + 2 * t + v)[:, :HALF]
                 product(sums, w_codes, w_scales, t, dz_codes[:, halves[v]], dz_scales[:, halves[v]])
                 first_sums.update({(t, v): sums})
 
@@ -229,47 +241,37 @@ def tile_attend_gtower_tnh_E_pl_kernel(tc, W, xT, G, hT, cf, ts, offs, out_0, ou
         def store_lane(t):
             nc.sync.dma_start(out_rows[:, t, :], out_window[t][:])
 
-        w_rounded_late = [
-            sb.tile([P, 1, 2, P, 2], BF16, name="w_rounded%d" % t, tag=tag) for t, tag in ((2, "w_rounded2"), (3, "w_rounded1"))
-        ]
-        for t in range(2, LANES):
-            round_rows(nc.scalar.copy, w_rounded_late[t - 2][:], w_raw[t][:].unsqueeze(1))
-        de0 = sb.tile([P, HALF], F32, name="de0_0")
-        nc.scalar.copy(de0[:], first_sums[0, 0])
-        scatter_half(0, 0, de0[:])
-        de1 = sb.tile([P, HALF], F32, name="de1_0")
-        nc.vector.tensor_copy(de1[:], first_sums[1, 0])
-        scatter_half(1, 0, de1[:])
+        def empty_bank(copy, name, tag, sums):
+            de = sb.tile([P, HALF], F32, name=name, tag=tag, align_bytes=64)
+            copy(de[:], sums)
+            return de[:]
 
-        turned_late = turn_pairs([part[:] for part in w_rounded_late], 2)
-        de0_late = sb.tile([P, HALF], F32, name="de0_1", tag="w_rounded1")
-        nc.scalar.copy(de0_late[:], first_sums[0, 1])
-        w_grouped_late = sb.tile([P, 2 * P, LANES], BF16, name="w_grouped_late", align_bytes=64)
-        group_pairs(w_grouped_late[:], turned_late, 2)
+        de0 = [empty_bank(nc.scalar.copy, "de0_%d" % v, "de0_%d" % v, first_sums[0, v]) for v in range(2)]
         quantize(w_grouped_late[:], w_codes[:, 2 * P :], w_scales[:, 2 * P :], E4M3)
-        de1_late = sb.tile([P, HALF], F32, name="de1_1", tag="w_grouped_late", align_bytes=64)
-        nc.vector.tensor_copy(de1_late[:], first_sums[1, 1])
-        scatter_half(0, 1, de0_late[:])
-        scatter_half(1, 1, de1_late[:])
-        store_lane(0)
-        store_lane(1)
+        vector_tags = ("w_grouped_late", "de1_1")
+        de1 = [empty_bank(nc.vector.tensor_copy, "de1_%d" % v, vector_tags[v], first_sums[1, v]) for v in range(2)]
+        for t, de in ((0, de0), (1, de1)):
+            for v in range(2):
+                scatter_half(t, v, de[v])
+            store_lane(t)
 
-        late_de = {}
-        for t in (3, 2):
-            sums = bank(LANES + t)
-            product(sums[:], w_codes, w_scales, t, dz_codes[:], dz_scales[:])
-            late_de.update({t: [sb.tile([P, HALF], F32, name="de%d_%d" % (t, v), align_bytes=64) for v in range(2)]})
+        late_sums = {}
+        for t in range(2, LANES):
+            late_sums.update({t: bank(LANES + t)})
+            product(late_sums[t][:], w_codes, w_scales, t, dz_codes[:], dz_scales[:])
+        de2 = [empty_bank(nc.scalar.copy, "de2_%d" % v, "de0_%d" % v, late_sums[2][:, halves[v]]) for v in range(2)]
+        de3 = [
+            empty_bank(nc.vector.tensor_copy, "de3_%d" % v, vector_tags[v], late_sums[3][:, halves[v]]) for v in range(2)
+        ]
+        for t, de in ((2, de2), (3, de3)):
             for v in range(2):
-                nc.scalar.copy(late_de[t][v][:], sums[:, halves[v]])
-        for t in (3, 2):
-            for v in range(2):
-                scatter_half(t, v, late_de[t][v][:])
+                scatter_half(t, v, de[v])
             store_lane(t)
 
         pairs_early = sb.tile([P, 2, 2 * CHUNK, 2], BF16, name="pairs_early", align_bytes=64)
         pairs = [pairs_early[:, :, :CHUNK, :], pairs_early[:, :, CHUNK:, :]]
-        for c, tag in ((2, "de2_0"), (3, "de2_1")):
-            pairs.append(sb.tile([P, 2, CHUNK, 2], BF16, name="pairs%d" % c, tag=tag, align_bytes=64)[:])
+        pairs.append(sb.tile([P, 2, CHUNK, 2], BF16, name="pairs2", tag="de0_0", align_bytes=64)[:])
+        pairs.append(sb.tile([P, 2, CHUNK, 2], BF16, name="pairs3", tag="de0_1", align_bytes=64)[:])
 
         def round_early(copy, t):
             copy(pairs_early[:, t // 2, :, t % 2], out_window[t][:, : 2 * CHUNK])
@@ -280,21 +282,24 @@ def tile_attend_gtower_tnh_E_pl_kernel(tc, W, xT, G, hT, cf, ts, offs, out_0, ou
         y_scales = sb.tile([P, CHUNK], U8, name="y_scales", align_bytes=64)
         words = out_1[0].rearrange("p n t -> p (n t)").bitcast(I32)
         y_grouped = [sb.tile([P, CHUNK, LANES], BF16, name="y_grouped%d" % c, align_bytes=64) for c in range(CHUNKS)]
-        y_codes = [sb.tile([P, CHUNK], U32, name="y_codes%d" % c, align_bytes=64) for c in range(CHUNKS)]
+        y_codes = sb.tile([P, ITEMS], U32, name="y_codes", align_bytes=64)
 
         def weave(copy, dtype, c, columns):
             woven = y_grouped[c][:].rearrange("p n t -> p (n t)").bitcast(dtype).rearrange("p (n u) -> p n u", u=2)
             apart = pairs[c].rearrange("p u n e -> p u (n e)").bitcast(dtype).rearrange("p u n -> p n u")
             copy(woven[:, columns, :], apart[:, columns, :])
 
-        def finish(c, *parts):
-            for columns in parts or (slice(0, CHUNK),):
-                quantize(y_grouped[c][:, columns, :], y_codes[c][:, columns], y_scales[4 * c : P, columns], E4M3)
-            nc.sync.dma_start(words[:, c * CHUNK : (c + 1) * CHUNK], y_codes[c][:].bitcast(I32))
+        def quantize_y(c, columns):
+            codes = y_codes[:, c * CHUNK : (c + 1) * CHUNK]
+            quantize(y_grouped[c][:, columns, :], codes[:, columns], y_scales[4 * c : P, columns], E4M3)
+
+        def store_codes(first, last):
+            columns = slice(first * CHUNK, last * CHUNK)
+            nc.sync.dma_start(words[:, columns], y_codes[:, columns].bitcast(I32))
 
         whole, low, high = slice(0, CHUNK), slice(0, CHUNK // 2), slice(CHUNK // 2, CHUNK)
         for t in range(2):
-            round_early(nc.gpsimd.tensor_copy, t)
+            round_early(gpsimd_round, t)
         for t in range(2):
             round_lane(nc.scalar.copy, t, 2)
         for t in range(LANES):
@@ -307,11 +312,15 @@ def tile_attend_gtower_tnh_E_pl_kernel(tc, W, xT, G, hT, cf, ts, offs, out_0, ou
         round_lane(nc.vector.tensor_copy, 2, 2)
         weave(nc.vector.tensor_copy, I32, 0, whole)
         weave(nc.vector.tensor_copy, I32, 1, whole)
-        finish(0)
+        quantize_y(0, whole)
         weave(nc.vector.tensor_copy, I32, 2, whole)
-        finish(1)
-        finish(2)
-        finish(3, low, high)
+        quantize_y(1, whole)
+        store_codes(0, 2)
+        quantize_y(2, whole)
+        store_codes(2, 3)
+        quantize_y(3, low)
+        quantize_y(3, high)
+        store_codes(3, 4)
 
         scale_rows = out_2[0].bitcast(I32).rearrange("r (c n) -> c r n", c=CHUNKS)
         for q in range(QUADRANTS):

@@ -118,29 +118,31 @@ def tile_attend_gtower_tnh_E_pl_kernel(tc, W, xT, G, hT, cf, ts, offs, out_0, ou
         ts_columns = sb.tile([P, BLOCKS], F32, name="ts_columns")
         nc.scalar.copy(ts_columns[:], ts_bank[:, TS_ROW::P])
 
-        spread_bank = bank(1)
+        x_codes = sb.tile([P, K], U32, name="x_codes", align_bytes=64)
+        x_scales = sb.tile([P, K], U8, name="x_scales", align_bytes=64)
+        x_grouped = []
+        for v in range(2):
+            x_rounded = sb.tile([P, 2, 2, P, 2], BF16, name="x_rounded%d" % v, align_bytes=64)
+            round_rows(nc.vector.tensor_copy, x_rounded[:], x_raw[v][:])
+            x_grouped.append(sb.tile([P, 2 * P, LANES], BF16, name="x_grouped%d" % v, align_bytes=64))
+            turn_rows(x_grouped[v][:], [x_rounded[:]], 2, 2 + v)
+        g_grouped = sb.tile([P, SLOTS, LANES], BF16, name="g_grouped", tag="x_rounded1", align_bytes=64)
+        g_by_slot = g_raw[:].rearrange("p j i -> p i j")
+        nc.vector.tensor_copy(g_grouped[:, :VECTOR_SLOTS, :], g_by_slot[:, :VECTOR_SLOTS, :])
+        nc.scalar.copy(g_grouped[:, VECTOR_SLOTS:, :], g_by_slot[:, VECTOR_SLOTS:, :])
+        g_codes = sb.tile([P, SLOTS], U32, name="g_codes", align_bytes=64)
+        g_scales = sb.tile([P, SLOTS], U8, name="g_scales", align_bytes=64)
+        quantize(x_grouped[0][:], x_codes[:, halves[0]], x_scales[:, halves[0]], E4M3)
+        quantize(g_grouped[:], g_codes[:], g_scales[:], E5M2)
+        quantize(x_grouped[1][:], x_codes[:, halves[1]], x_scales[:, halves[1]], E4M3)
+
+        spread_bank = bank(2)
         for b in range(BLOCKS):
             nc.tensor.transpose(
                 spread_bank[:, b * P : (b + 1) * P], ts_columns[:, b : b + 1].to_broadcast([P, P]), ident[:]
             )
         ts_spread = sb.tile([P, SLOTS], F32, name="ts_spread")
         nc.scalar.copy(ts_spread[:], spread_bank[:])
-
-        x_codes = sb.tile([P, K], U32, name="x_codes", align_bytes=64)
-        x_scales = sb.tile([P, K], U8, name="x_scales", align_bytes=64)
-        for v in range(2):
-            x_rounded = sb.tile([P, 2, 2, P, 2], BF16, name="x_rounded%d" % v, align_bytes=64)
-            round_rows(nc.vector.tensor_copy, x_rounded[:], x_raw[v][:])
-            x_grouped = sb.tile([P, 2 * P, LANES], BF16, name="x_grouped%d" % v, align_bytes=64)
-            turn_rows(x_grouped[:], [x_rounded[:]], 2, 2 + v)
-            quantize(x_grouped[:], x_codes[:, halves[v]], x_scales[:, halves[v]], E4M3)
-        g_grouped = sb.tile([P, SLOTS, LANES], BF16, name="g_grouped", align_bytes=64)
-        g_by_slot = g_raw[:].rearrange("p j i -> p i j")
-        nc.vector.tensor_copy(g_grouped[:, :VECTOR_SLOTS, :], g_by_slot[:, :VECTOR_SLOTS, :])
-        nc.scalar.copy(g_grouped[:, VECTOR_SLOTS:, :], g_by_slot[:, VECTOR_SLOTS:, :])
-        g_codes = sb.tile([P, SLOTS], U32, name="g_codes", align_bytes=64)
-        g_scales = sb.tile([P, SLOTS], U8, name="g_scales", align_bytes=64)
-        quantize(g_grouped[:], g_codes[:], g_scales[:], E5M2)
 
         def product(sums, codes, scales, lane, e5_codes, e5_scales):
             rows = slice(lane * P, (lane + 1) * P)
@@ -162,7 +164,7 @@ def tile_attend_gtower_tnh_E_pl_kernel(tc, W, xT, G, hT, cf, ts, offs, out_0, ou
             nc.vector.scalar_tensor_tensor(factor[:], dv[:], minus_cf[:, t : t + 1], ts_spread[:], ALU.mult, ALU.mult)
             factors.append(factor)
 
-        clear_window(3, sb.tile([P, ITEMS], F32, name="out_window3", tag="g_grouped", align_bytes=64))
+        clear_window(3, sb.tile([P, ITEMS], F32, name="out_window3", tag="x_grouped1", align_bytes=64))
         clear_window(2, sb.tile([P, ITEMS], F32, name="out_window2", tag="x_codes", align_bytes=64))
 
         squares = []
@@ -179,8 +181,6 @@ def tile_attend_gtower_tnh_E_pl_kernel(tc, W, xT, G, hT, cf, ts, offs, out_0, ou
         dz_low = sb.tile([P, 2, SLOTS], BF16, name="dz_low")
         for t in range(2):
             slope_times(dz_low[:, t, :], squares[t][:], factors[t][:])
-        dz_grouped = sb.tile([P, SLOTS, LANES], BF16, name="dz_grouped", align_bytes=64)
-        nc.vector.tensor_copy(dz_grouped[:, :, 0:2], dz_low[:].rearrange("p t i -> p i t"))
 
         def gpsimd_round(rounded, values):
             nc.gpsimd.tensor_scalar(rounded, values, 1.0, 0.0, ALU.mult, ALU.add)
@@ -196,6 +196,8 @@ def tile_attend_gtower_tnh_E_pl_kernel(tc, W, xT, G, hT, cf, ts, offs, out_0, ou
             return grouped
 
         w_grouped0 = turn_w(0, nc.vector.tensor_copy)
+        dz_grouped = sb.tile([P, SLOTS, LANES], BF16, name="dz_grouped", tag="w_raw0", align_bytes=64)
+        nc.vector.tensor_copy(dz_grouped[:, :, 0:2], dz_low[:].rearrange("p t i -> p i t"))
         dz_high = sb.tile([P, 2, SLOTS], BF16, name="dz_high")
         slope_times(dz_high[:, 0, :], squares[2][:], factors[2][:])
 

@@ -270,13 +270,16 @@ def tile_attend_gtower_tnh_E_pl_kernel(tc, W, xT, G, hT, cf, ts, offs, out_0, ou
                 scatter_half(t, v, de[v])
             store_lane(t)
 
-        pairs_early = sb.tile([P, 2, 2 * CHUNK, 2], BF16, name="pairs_early", align_bytes=64)
-        pairs = [pairs_early[:, :, :CHUNK, :], pairs_early[:, :, CHUNK:, :]]
-        pairs.append(sb.tile([P, 2, CHUNK, 2], BF16, name="pairs2", tag="de0_0", align_bytes=64)[:])
-        pairs.append(sb.tile([P, 2, CHUNK, 2], BF16, name="pairs3", tag="de0_1", align_bytes=64)[:])
+        pairs_middle = sb.tile([P, 2, 2 * CHUNK, 2], BF16, name="pairs_middle", tag="de0_0", align_bytes=64)
+        pairs = [
+            sb.tile([P, 2, CHUNK, 2], BF16, name="pairs_first", tag="de1_1", align_bytes=64)[:],
+            pairs_middle[:, :, :CHUNK, :],
+            pairs_middle[:, :, CHUNK:, :],
+            sb.tile([P, 2, CHUNK, 2], BF16, name="pairs_last", tag="de0_1", align_bytes=64)[:],
+        ]
 
-        def round_early(copy, t):
-            copy(pairs_early[:, t // 2, :, t % 2], out_window[t][:, : 2 * CHUNK])
+        def round_middle(copy, t):
+            copy(pairs_middle[:, t // 2, :, t % 2], out_window[t][:, CHUNK : 3 * CHUNK])
 
         def round_lane(copy, t, c):
             copy(pairs[c][:, t // 2, :, t % 2], out_window[t][:, c * CHUNK : (c + 1) * CHUNK])
@@ -301,17 +304,16 @@ def tile_attend_gtower_tnh_E_pl_kernel(tc, W, xT, G, hT, cf, ts, offs, out_0, ou
 
         whole, low, high = slice(0, CHUNK), slice(0, CHUNK // 2), slice(CHUNK // 2, CHUNK)
         for t in range(2):
-            round_early(gpsimd_round, t)
-        for t in range(2):
-            round_lane(nc.scalar.copy, t, 2)
+            round_middle(nc.scalar.copy, t)
         for t in range(LANES):
             round_lane(nc.scalar.copy, t, 3)
         weave(nc.scalar.copy, U32, 3, low)
         weave(nc.scalar.copy, U32, 3, high)
-        round_early(nc.vector.tensor_copy, 3)
-        round_lane(nc.vector.tensor_copy, 3, 2)
-        round_early(nc.vector.tensor_copy, 2)
-        round_lane(nc.vector.tensor_copy, 2, 2)
+        for t in range(2):
+            round_lane(nc.vector.tensor_copy, t, 0)
+        for t in (3, 2):
+            round_lane(nc.vector.tensor_copy, t, 0)
+            round_middle(nc.vector.tensor_copy, t)
         weave(nc.vector.tensor_copy, I32, 0, whole)
         weave(nc.vector.tensor_copy, I32, 1, whole)
         quantize_y(0, whole)

@@ -35,6 +35,7 @@ def tile_attend_gtower_tnh_E_pl_kernel(tc, W, xT, G, hT, cf, ts, offs, out_0, ou
     nc = tc.nc
     with ExitStack() as ctx:
         sb = ctx.enter_context(tc.tile_pool(name="sb", bufs=1))
+        placed = ctx.enter_context(tc.tile_pool(name="placed", bufs=1))
         psum = ctx.enter_context(tc.psum_pool(name="psum", bufs=1))
 
         def bank(n):
@@ -243,12 +244,16 @@ def tile_attend_gtower_tnh_E_pl_kernel(tc, W, xT, G, hT, cf, ts, offs, out_0, ou
         def store_lane(t):
             nc.sync.dma_start(out_rows[:, t, :], out_window[t][:])
 
-        def empty_bank(copy, name, tag, sums):
-            de = sb.tile([P, HALF], F32, name=name, tag=tag, align_bytes=64)
+        def empty_bank(copy, name, place, sums):
+            if isinstance(place, str):
+                de = sb.tile([P, HALF], F32, name=name, tag=place, align_bytes=64)
+            else:
+                de = placed.tile([P, HALF], F32, name=name, align_bytes=64, offset=place)
             copy(de[:], sums)
             return de[:]
 
-        de0 = [empty_bank(nc.scalar.copy, "de0_%d" % v, "de0_%d" % v, first_sums[0, v]) for v in range(2)]
+        scalar_places = ("de0_0", 6 * HALF)
+        de0 = [empty_bank(nc.scalar.copy, "de0_%d" % v, scalar_places[v], first_sums[0, v]) for v in range(2)]
         quantize(w_grouped_late[:], w_codes[:, 2 * P :], w_scales[:, 2 * P :], E4M3)
         vector_tags = ("w_grouped_late", "de1_1")
         de1 = [empty_bank(nc.vector.tensor_copy, "de1_%d" % v, vector_tags[v], first_sums[1, v]) for v in range(2)]
@@ -261,7 +266,7 @@ def tile_attend_gtower_tnh_E_pl_kernel(tc, W, xT, G, hT, cf, ts, offs, out_0, ou
         for t in range(2, LANES):
             late_sums.update({t: bank(LANES + t)})
             product(late_sums[t][:], w_codes, w_scales, t, dz_codes[:], dz_scales[:])
-        de2 = [empty_bank(nc.scalar.copy, "de2_%d" % v, "de0_%d" % v, late_sums[2][:, halves[v]]) for v in range(2)]
+        de2 = [empty_bank(nc.scalar.copy, "de2_%d" % v, scalar_places[v], late_sums[2][:, halves[v]]) for v in range(2)]
         de3 = [
             empty_bank(nc.vector.tensor_copy, "de3_%d" % v, vector_tags[v], late_sums[3][:, halves[v]]) for v in range(2)
         ]
@@ -272,27 +277,34 @@ def tile_attend_gtower_tnh_E_pl_kernel(tc, W, xT, G, hT, cf, ts, offs, out_0, ou
 
         pairs_middle = sb.tile([P, 2, 2 * CHUNK, 2], BF16, name="pairs_middle", tag="de0_0", align_bytes=64)
         pairs = [
-            sb.tile([P, 2, CHUNK, 2], BF16, name="pairs_first", tag="de1_1", align_bytes=64)[:],
+            sb.tile([P, 2, CHUNK, 2], BF16, name="pairs_first", align_bytes=64)[:],
             pairs_middle[:, :, :CHUNK, :],
             pairs_middle[:, :, CHUNK:, :],
-            sb.tile([P, 2, CHUNK, 2], BF16, name="pairs_last", tag="de0_1", align_bytes=64)[:],
+        ]
+        pairs_last = [
+            placed.tile([P, 2, CHUNK // 2, 2], BF16, name="pairs_last%d" % v, align_bytes=64, offset=8 * HALF * v)[:]
+            for v in range(2)
         ]
 
         def round_middle(copy, t):
             copy(pairs_middle[:, t // 2, :, t % 2], out_window[t][:, CHUNK : 3 * CHUNK])
 
-        def round_lane(copy, t, c):
-            copy(pairs[c][:, t // 2, :, t % 2], out_window[t][:, c * CHUNK : (c + 1) * CHUNK])
+        def round_first(copy, t):
+            copy(pairs[0][:, t // 2, :, t % 2], out_window[t][:, :CHUNK])
+
+        def round_last(t, v):
+            first = ITEMS - CHUNK + v * CHUNK // 2
+            nc.scalar.copy(pairs_last[v][:, t // 2, :, t % 2], out_window[t][:, first : first + CHUNK // 2])
 
         y_scales = sb.tile([P, CHUNK], U8, name="y_scales", align_bytes=64)
         words = out_1[0].rearrange("p n t -> p (n t)").bitcast(I32)
         y_grouped = [sb.tile([P, CHUNK, LANES], BF16, name="y_grouped%d" % c, align_bytes=64) for c in range(CHUNKS)]
         y_codes = sb.tile([P, ITEMS], U32, name="y_codes", align_bytes=64)
 
-        def weave(copy, dtype, c, columns):
-            woven = y_grouped[c][:].rearrange("p n t -> p (n t)").bitcast(dtype).rearrange("p (n u) -> p n u", u=2)
-            apart = pairs[c].rearrange("p u n e -> p u (n e)").bitcast(dtype).rearrange("p u n -> p n u")
-            copy(woven[:, columns, :], apart[:, columns, :])
+        def weave(c, columns, source):
+            woven = y_grouped[c][:].rearrange("p n t -> p (n t)").bitcast(I32).rearrange("p (n u) -> p n u", u=2)
+            apart = source.rearrange("p u n e -> p u (n e)").bitcast(I32).rearrange("p u n -> p n u")
+            nc.vector.tensor_copy(woven[:, columns, :], apart)
 
         def quantize_y(c, columns):
             codes = y_codes[:, c * CHUNK : (c + 1) * CHUNK]
@@ -304,24 +316,25 @@ def tile_attend_gtower_tnh_E_pl_kernel(tc, W, xT, G, hT, cf, ts, offs, out_0, ou
 
         whole, low, high = slice(0, CHUNK), slice(0, CHUNK // 2), slice(CHUNK // 2, CHUNK)
         for t in range(2):
-            round_middle(nc.scalar.copy, t)
-        for t in range(LANES):
-            round_lane(nc.scalar.copy, t, 3)
-        weave(nc.scalar.copy, U32, 3, low)
-        weave(nc.scalar.copy, U32, 3, high)
+            round_first(gpsimd_round, t)
         for t in range(2):
-            round_lane(nc.vector.tensor_copy, t, 0)
+            round_middle(nc.scalar.copy, t)
+        for v in range(2):
+            for t in range(LANES):
+                round_last(t, v)
         for t in (3, 2):
-            round_lane(nc.vector.tensor_copy, t, 0)
+            round_first(nc.vector.tensor_copy, t)
             round_middle(nc.vector.tensor_copy, t)
-        weave(nc.vector.tensor_copy, I32, 0, whole)
-        weave(nc.vector.tensor_copy, I32, 1, whole)
+        weave(0, whole, pairs[0])
+        weave(1, whole, pairs[1])
         quantize_y(0, whole)
-        weave(nc.vector.tensor_copy, I32, 2, whole)
+        weave(2, whole, pairs[2])
         quantize_y(1, whole)
         store_codes(0, 2)
+        weave(3, low, pairs_last[0])
         quantize_y(2, whole)
         store_codes(2, 3)
+        weave(3, high, pairs_last[1])
         quantize_y(3, low)
         quantize_y(3, high)
         store_codes(3, 4)

@@ -35,7 +35,6 @@ def tile_attend_gtower_tnh_E_pl_kernel(tc, W, xT, G, hT, cf, ts, offs, out_0, ou
     nc = tc.nc
     with ExitStack() as ctx:
         sb = ctx.enter_context(tc.tile_pool(name="sb", bufs=1))
-        placed = ctx.enter_context(tc.tile_pool(name="placed", bufs=1))
         psum = ctx.enter_context(tc.psum_pool(name="psum", bufs=1))
 
         def bank(n):
@@ -56,10 +55,10 @@ def tile_attend_gtower_tnh_E_pl_kernel(tc, W, xT, G, hT, cf, ts, offs, out_0, ou
         h_window = [sb.tile([P, ITEMS], F32, name="h_window%d" % t, align_bytes=64) for t in range(LANES)]
         w_raw = [sb.tile([P, K], F32, name="w_raw%d" % t, align_bytes=64) for t in range(LANES)]
 
+        nc.sync.dma_start(x_raw[0][:], x_rows[:, 0:2, :])
         nc.sync.dma_start(cf_lanes[:], cf.rearrange("(p t) o -> p (t o)", t=LANES))
         nc.sync.dma_start(ts_window[TS_ROW:P, :], ts[0:1, :])
         nc.sync.dma_start(offsets[:], offs)
-        nc.sync.dma_start(x_raw[0][:], x_rows[:, 0:2, :])
         nc.sync.dma_start(x_raw[1][:], x_rows[:, 2:4, :])
         nc.sync.dma_start(g_raw[:], G.rearrange("(p j) i -> p j i", j=LANES))
         for t in range(LANES - 1):
@@ -108,8 +107,14 @@ def tile_attend_gtower_tnh_E_pl_kernel(tc, W, xT, G, hT, cf, ts, offs, out_0, ou
                 turned[:, 0 : 2 * lanes * P].rearrange("p (t u m) -> p t m u", t=lanes, u=2),
             )
 
-        def turn_rows(grouped, rounded_parts, lanes, bank_number):
-            group_pairs(grouped, turn_pairs(rounded_parts, bank_number), lanes)
+        x_codes = sb.tile([P, K], U32, name="x_codes", align_bytes=64)
+        x_scales = sb.tile([P, K], U8, name="x_scales", align_bytes=64)
+        x_grouped = []
+        for v in range(2):
+            x_rounded = sb.tile([P, 2, 2, P, 2], BF16, name="x_rounded%d" % v, align_bytes=64)
+            round_rows(nc.vector.tensor_copy, x_rounded[:], x_raw[v][:])
+            x_grouped.append(sb.tile([P, 2 * P, LANES], BF16, name="x_grouped%d" % v, align_bytes=64))
+            group_pairs(x_grouped[v][:], turn_pairs([x_rounded[:]], 2 + v), 2)
 
         ts_listed = sb.tile([P, SLOTS], F32, name="ts_listed")
         nc.scalar.activation(ts_listed[:], ts_window[:].indirect(offsets[:]), ACT.Copy)
@@ -119,14 +124,6 @@ def tile_attend_gtower_tnh_E_pl_kernel(tc, W, xT, G, hT, cf, ts, offs, out_0, ou
         ts_columns = sb.tile([P, BLOCKS], F32, name="ts_columns")
         nc.scalar.copy(ts_columns[:], ts_bank[:, TS_ROW::P])
 
-        x_codes = sb.tile([P, K], U32, name="x_codes", align_bytes=64)
-        x_scales = sb.tile([P, K], U8, name="x_scales", align_bytes=64)
-        x_grouped = []
-        for v in range(2):
-            x_rounded = sb.tile([P, 2, 2, P, 2], BF16, name="x_rounded%d" % v, align_bytes=64)
-            round_rows(nc.vector.tensor_copy, x_rounded[:], x_raw[v][:])
-            x_grouped.append(sb.tile([P, 2 * P, LANES], BF16, name="x_grouped%d" % v, align_bytes=64))
-            turn_rows(x_grouped[v][:], [x_rounded[:]], 2, 2 + v)
         g_grouped = sb.tile([P, SLOTS, LANES], BF16, name="g_grouped", tag="x_rounded1", align_bytes=64)
         g_by_slot = g_raw[:].rearrange("p j i -> p i j")
         nc.vector.tensor_copy(g_grouped[:, :VECTOR_SLOTS, :], g_by_slot[:, :VECTOR_SLOTS, :])
@@ -183,20 +180,13 @@ def tile_attend_gtower_tnh_E_pl_kernel(tc, W, xT, G, hT, cf, ts, offs, out_0, ou
         for t in range(2):
             slope_times(dz_low[:, t, :], squares[t][:], factors[t][:])
 
-        def gpsimd_round(rounded, values):
-            nc.gpsimd.tensor_scalar(rounded, values, 1.0, 0.0, ALU.mult, ALU.add)
-
         def round_w(t, copy):
             rounded = sb.tile([P, 2, P, 2], BF16, name="w_rounded%d" % t, align_bytes=64)
             copy(rounded[:].rearrange("m u p e -> m p u e"), w_raw[t][:].rearrange("m (p u e) -> m p u e", u=2, e=2))
             return rounded[:].unsqueeze(1)
 
-        def turn_w(t, copy):
-            grouped = sb.tile([P, P, LANES], BF16, name="w_grouped%d" % t, align_bytes=64)
-            turn_rows(grouped[:], [round_w(t, copy)], 1, t)
-            return grouped
-
-        w_grouped0 = turn_w(0, nc.vector.tensor_copy)
+        w_grouped0 = sb.tile([P, P, LANES], BF16, name="w_grouped0", align_bytes=64)
+        group_pairs(w_grouped0[:], turn_pairs([round_w(0, nc.vector.tensor_copy)], 0), 1)
         dz_grouped = sb.tile([P, SLOTS, LANES], BF16, name="dz_grouped", tag="w_raw0", align_bytes=64)
         nc.vector.tensor_copy(dz_grouped[:, :, 0:2], dz_low[:].rearrange("p t i -> p i t"))
         dz_high = sb.tile([P, 2, SLOTS], BF16, name="dz_high")
@@ -208,16 +198,16 @@ def tile_attend_gtower_tnh_E_pl_kernel(tc, W, xT, G, hT, cf, ts, offs, out_0, ou
         w_codes = sb.tile([P, K], U32, name="w_codes", tag="h_window3", align_bytes=64)
         w_scales = sb.tile([P, K], U8, name="w_scales", align_bytes=64)
         quantize(w_grouped0[:], w_codes[:, :P], w_scales[:, :P], E4M3)
+        turned_middle = turn_pairs([round_w(t, nc.vector.tensor_copy) for t in (1, 2)], 1)
         for v in range(2):
             last_squared = sb.tile([P, HALF], F32, name="last_squared%d" % v)
             nc.scalar.activation(last_squared[:], h_last[v][:], ACT.Square)
             slope_times(dz_high[:, 1, halves[v]], last_squared[:], factors[LANES - 1][:, halves[v]])
-        turned1 = turn_pairs([round_w(1, gpsimd_round)], 1)
-        turned_late = turn_pairs([round_w(t, nc.scalar.copy) for t in range(2, LANES)], 0)
-        w_grouped1 = sb.tile([P, P, LANES], BF16, name="w_grouped1", tag="w_raw3", align_bytes=64)
-        group_pairs(w_grouped1[:], turned1, 1)
-        w_grouped_late = sb.tile([P, 2 * P, LANES], BF16, name="w_grouped_late", align_bytes=64)
-        group_pairs(w_grouped_late[:], turned_late, 2)
+        turned_last = turn_pairs([round_w(3, nc.scalar.copy)], 0)
+        w_grouped_middle = sb.tile([P, 2 * P, LANES], BF16, name="w_grouped_middle", tag="w_raw3", align_bytes=64)
+        group_pairs(w_grouped_middle[:], turned_middle, 2)
+        w_grouped3 = sb.tile([P, P, LANES], BF16, name="w_grouped3", align_bytes=64)
+        group_pairs(w_grouped3[:], turned_last, 1)
         for v in range(2):
             nc.vector.tensor_copy(
                 dz_grouped[:, halves[v], 2:LANES], dz_high[:, :, halves[v]].rearrange("p t i -> p i t")
@@ -225,121 +215,100 @@ def tile_attend_gtower_tnh_E_pl_kernel(tc, W, xT, G, hT, cf, ts, offs, out_0, ou
         dz_codes = sb.tile([P, SLOTS], U32, name="dz_codes", align_bytes=64)
         dz_scales = sb.tile([P, SLOTS], U8, name="dz_scales", align_bytes=64)
         quantize(dz_grouped[:, halves[0], :], dz_codes[:, halves[0]], dz_scales[:, halves[0]], E5M2)
+        quantize(w_grouped_middle[:], w_codes[:, P : 3 * P], w_scales[:, P : 3 * P], E4M3)
         quantize(dz_grouped[:, halves[1], :], dz_codes[:, halves[1]], dz_scales[:, halves[1]], E5M2)
-        quantize(w_grouped1[:], w_codes[:, P : 2 * P], w_scales[:, P : 2 * P], E4M3)
+        quantize(w_grouped3[:], w_codes[:, 3 * P :], w_scales[:, 3 * P :], E4M3)
 
-        first_sums = {}
-        for t in range(2):
-            for v in range(2):
-                sums = bank(1 + 2 * t + v)[:, :HALF]
-                product(sums, w_codes, w_scales, t, dz_codes[:, halves[v]], dz_scales[:, halves[v]])
-                first_sums.update({(t, v): sums})
-
-        def scatter_half(t, v, de):
-            if t % 2 == 0:
-                nc.scalar.activation(out_window[t][:].indirect(halves_of_list[v]), de, ACT.Copy)
-            else:
-                nc.vector.tensor_copy(out_window[t][:].indirect(halves_of_list[v]), de)
+        steps = [(0, 0), (0, 1), (2, 0), (2, 1)]
+        places = [(0, halves[0]), (1, halves[0]), (1, halves[1]), (2, halves[0])]
+        sums = [[bank(2 + 2 * n + e) for n in range(3)] for e in range(2)]
+        for (lane, v), (n, columns) in zip(steps, places):
+            for e in range(2):
+                product(
+                    sums[e][n][:, columns], w_codes, w_scales, lane + e, dz_codes[:, halves[v]], dz_scales[:, halves[v]]
+                )
 
         def store_lane(t):
             nc.sync.dma_start(out_rows[:, t, :], out_window[t][:])
 
-        def empty_bank(copy, name, place, sums):
-            if isinstance(place, str):
-                de = sb.tile([P, HALF], F32, name=name, tag=place, align_bytes=64)
-            else:
-                de = placed.tile([P, HALF], F32, name=name, align_bytes=64, offset=place)
-            copy(de[:], sums)
-            return de[:]
+        y_row = sb.tile([P, LANES * ITEMS], BF16, name="y_row", align_bytes=64)
+        y_lanes = y_row[:].rearrange("p (c t n) -> p c t n", c=CHUNKS, t=LANES)
 
-        scalar_places = ("de0_0", 6 * HALF)
-        de0 = [empty_bank(nc.scalar.copy, "de0_%d" % v, scalar_places[v], first_sums[0, v]) for v in range(2)]
-        quantize(w_grouped_late[:], w_codes[:, 2 * P :], w_scales[:, 2 * P :], E4M3)
-        vector_tags = ("w_grouped_late", "de1_1")
-        de1 = [empty_bank(nc.vector.tensor_copy, "de1_%d" % v, vector_tags[v], first_sums[1, v]) for v in range(2)]
-        for t, de in ((0, de0), (1, de1)):
-            for v in range(2):
-                scatter_half(t, v, de[v])
-            store_lane(t)
+        def round_lane(copy, t, first, last):
+            copy(y_lanes[:, first:last, t, :], out_window[t][:].rearrange("p (c n) -> p c n", c=CHUNKS)[:, first:last, :])
 
-        late_sums = {}
-        for t in range(2, LANES):
-            late_sums.update({t: bank(LANES + t)})
-            product(late_sums[t][:], w_codes, w_scales, t, dz_codes[:], dz_scales[:])
-        de2 = [empty_bank(nc.scalar.copy, "de2_%d" % v, scalar_places[v], late_sums[2][:, halves[v]]) for v in range(2)]
-        de3 = [
-            empty_bank(nc.vector.tensor_copy, "de3_%d" % v, vector_tags[v], late_sums[3][:, halves[v]]) for v in range(2)
-        ]
-        for t, de in ((2, de2), (3, de3)):
-            for v in range(2):
-                scatter_half(t, v, de[v])
-            store_lane(t)
+        def gpsimd_round(rounded, values):
+            nc.gpsimd.tensor_scalar(rounded, values, 1.0, 0.0, ALU.mult, ALU.add)
 
-        pairs_middle = sb.tile([P, 2, 2 * CHUNK, 2], BF16, name="pairs_middle", tag="de0_0", align_bytes=64)
-        pairs = [
-            sb.tile([P, 2, CHUNK, 2], BF16, name="pairs_first", align_bytes=64)[:],
-            pairs_middle[:, :, :CHUNK, :],
-            pairs_middle[:, :, CHUNK:, :],
-        ]
-        pairs_last = [
-            placed.tile([P, 2, CHUNK // 2, 2], BF16, name="pairs_last%d" % v, align_bytes=64, offset=8 * HALF * v)[:]
-            for v in range(2)
-        ]
+        def scalar_scatter(t, part_of_list, de):
+            nc.scalar.activation(out_window[t][:].indirect(part_of_list), de, ACT.Copy)
 
-        def round_middle(copy, t):
-            copy(pairs_middle[:, t // 2, :, t % 2], out_window[t][:, CHUNK : 3 * CHUNK])
+        def vector_scatter(t, part_of_list, de):
+            nc.vector.tensor_copy(out_window[t][:].indirect(part_of_list), de)
 
-        def round_first(copy, t):
-            copy(pairs[0][:, t // 2, :, t % 2], out_window[t][:, :CHUNK])
+        chunks = [slice(c * CHUNK, (c + 1) * CHUNK) for c in range(CHUNKS)]
+        copies = (nc.scalar.copy, nc.vector.tensor_copy)
+        scatters = (scalar_scatter, vector_scatter)
+        de_rest = []
+        for e in range(2):
+            de_first = sb.tile([P, HALF], F32, name="de_first%d" % e)
+            de_rest.append(sb.tile([P, 3 * HALF], F32, name="de_rest%d" % e))
+            copies[e](de_first[:], sums[e][0][:, halves[0]])
+            scatters[e](e, halves_of_list[0], de_first[:])
+            copies[e](de_rest[e][:, :SLOTS], sums[e][1][:])
+            copies[e](de_rest[e][:, SLOTS:], sums[e][2][:, halves[0]])
+            scatters[e](e, halves_of_list[1], de_rest[e][:, :HALF])
+            store_lane(e)
+        for t in range(2):
+            round_lane(gpsimd_round, t, 0, 3)
+        scalar_scatter(2, halves_of_list[0], de_rest[0][:, HALF:SLOTS])
+        round_lane(nc.scalar.copy, 0, 3, 4)
+        scalar_scatter(2, halves_of_list[1], de_rest[0][:, SLOTS:])
+        store_lane(2)
+        vector_scatter(3, offsets[:], de_rest[1][:, HALF:])
+        store_lane(3)
 
-        def round_last(t, v):
-            first = ITEMS - CHUNK + v * CHUNK // 2
-            nc.scalar.copy(pairs_last[v][:, t // 2, :, t % 2], out_window[t][:, first : first + CHUNK // 2])
-
-        y_scales = sb.tile([P, CHUNK], U8, name="y_scales", align_bytes=64)
-        words = out_1[0].rearrange("p n t -> p (n t)").bitcast(I32)
         y_grouped = [sb.tile([P, CHUNK, LANES], BF16, name="y_grouped%d" % c, align_bytes=64) for c in range(CHUNKS)]
         y_codes = sb.tile([P, ITEMS], U32, name="y_codes", align_bytes=64)
+        y_scales = sb.tile([P, 2 * CHUNK], U8, name="y_scales", align_bytes=64)
+        words = out_1[0].rearrange("p n t -> p (n t)").bitcast(I32)
 
-        def weave(c, columns, source):
-            woven = y_grouped[c][:].rearrange("p n t -> p (n t)").bitcast(I32).rearrange("p (n u) -> p n u", u=2)
-            apart = source.rearrange("p u n e -> p u (n e)").bitcast(I32).rearrange("p u n -> p n u")
-            nc.vector.tensor_copy(woven[:, columns, :], apart)
+        def interleave(copy, c, columns):
+            copy(
+                y_grouped[c][:, columns, :].rearrange("p (n i) t -> p n t i", i=4),
+                y_lanes[:, c, :, columns].rearrange("p t (n i) -> p n t i", i=4),
+            )
 
         def quantize_y(c, columns):
-            codes = y_codes[:, c * CHUNK : (c + 1) * CHUNK]
-            quantize(y_grouped[c][:, columns, :], codes[:, columns], y_scales[4 * c : P, columns], E4M3)
+            plane = y_scales[4 * (c // 2) : P, chunks[c % 2]]
+            quantize(y_grouped[c][:, columns, :], y_codes[:, chunks[c]][:, columns], plane[:, columns], E4M3)
 
         def store_codes(first, last):
             columns = slice(first * CHUNK, last * CHUNK)
             nc.sync.dma_start(words[:, columns], y_codes[:, columns].bitcast(I32))
 
         whole, low, high = slice(0, CHUNK), slice(0, CHUNK // 2), slice(CHUNK // 2, CHUNK)
-        for t in range(2):
-            round_first(gpsimd_round, t)
-        for t in range(2):
-            round_middle(nc.scalar.copy, t)
-        for v in range(2):
-            for t in range(LANES):
-                round_last(t, v)
-        for t in (3, 2):
-            round_first(nc.vector.tensor_copy, t)
-            round_middle(nc.vector.tensor_copy, t)
-        weave(0, whole, pairs[0])
-        weave(1, whole, pairs[1])
+        for c in range(CHUNKS):
+            round_lane(nc.scalar.copy, 2, c, c + 1)
+        for c in range(CHUNKS - 1):
+            round_lane(nc.vector.tensor_copy, 3, c, c + 1)
+        round_lane(nc.scalar.copy, 1, 3, 4)
+        round_lane(nc.scalar.copy, 3, 3, 4)
+        interleave(nc.scalar.copy, 3, low)
+        interleave(nc.scalar.copy, 3, high)
+        interleave(nc.vector.tensor_copy, 0, whole)
+        interleave(nc.vector.tensor_copy, 1, whole)
         quantize_y(0, whole)
-        weave(2, whole, pairs[2])
+        interleave(nc.vector.tensor_copy, 2, whole)
         quantize_y(1, whole)
         store_codes(0, 2)
-        weave(3, low, pairs_last[0])
         quantize_y(2, whole)
         store_codes(2, 3)
-        weave(3, high, pairs_last[1])
         quantize_y(3, low)
         quantize_y(3, high)
         store_codes(3, 4)
 
-        scale_rows = out_2[0].bitcast(I32).rearrange("r (c n) -> c r n", c=CHUNKS)
+        scale_rows = out_2[0].bitcast(I32).rearrange("r (a n) -> a r n", a=2)
         for q in range(QUADRANTS):
             queue = nc.sync if q % 2 == 0 else nc.scalar
-            queue.dma_start(scale_rows[:, 4 * q : 4 * q + 4, :], y_scales[32 * q : 32 * q + 16, :].bitcast(I32))
+            queue.dma_start(scale_rows[:, 4 * q : 4 * q + 4, :], y_scales[32 * q : 32 * q + 8, :].bitcast(I32))

@@ -69,10 +69,8 @@ def tile_attend_gtower_tnh_E_pl_kernel(tc, W, xT, G, hT, cf, ts, offs, out_0, ou
             nc.sync.dma_start(w_raw[t][:], w_rows[:, t, :])
 
         nc.vector.memset(ts_window[0:TS_ROW, :], 0.0)
-        out_window = {}
-        for t in range(2):
-            out_window.update({t: sb.tile([P, ITEMS], F32, name="out_window%d" % t)})
-            nc.vector.memset(out_window[t][:], 0.0)
+        out_window = {0: sb.tile([P, ITEMS], F32, name="out_window0")}
+        nc.vector.memset(out_window[0][:], 0.0)
 
         def clear_window(t, window):
             out_window.update({t: window})
@@ -107,6 +105,9 @@ def tile_attend_gtower_tnh_E_pl_kernel(tc, W, xT, G, hT, cf, ts, offs, out_0, ou
                 turned[:, 0 : 2 * lanes * P].rearrange("p (t u m) -> p t m u", t=lanes, u=2),
             )
 
+        ts_listed = sb.tile([P, SLOTS], F32, name="ts_listed")
+        nc.scalar.activation(ts_listed[:], ts_window[:].indirect(offsets[:]), ACT.Copy)
+
         x_codes = sb.tile([P, K], U32, name="x_codes", align_bytes=64)
         x_scales = sb.tile([P, K], U8, name="x_scales", align_bytes=64)
         x_grouped = []
@@ -116,8 +117,6 @@ def tile_attend_gtower_tnh_E_pl_kernel(tc, W, xT, G, hT, cf, ts, offs, out_0, ou
             x_grouped.append(sb.tile([P, 2 * P, LANES], BF16, name="x_grouped%d" % v, align_bytes=64))
             group_pairs(x_grouped[v][:], turn_pairs([x_rounded[:]], 2 + v), 2)
 
-        ts_listed = sb.tile([P, SLOTS], F32, name="ts_listed")
-        nc.scalar.activation(ts_listed[:], ts_window[:].indirect(offsets[:]), ACT.Copy)
         ts_bank = bank(0)
         for b in range(BLOCKS):
             nc.tensor.transpose(ts_bank[:, b * P : (b + 1) * P], ts_listed[:, b * P : (b + 1) * P], ident[:])
@@ -162,7 +161,7 @@ def tile_attend_gtower_tnh_E_pl_kernel(tc, W, xT, G, hT, cf, ts, offs, out_0, ou
             nc.vector.scalar_tensor_tensor(factor[:], dv[:], minus_cf[:, t : t + 1], ts_spread[:], ALU.mult, ALU.mult)
             factors.append(factor)
 
-        clear_window(3, sb.tile([P, ITEMS], F32, name="out_window3", tag="x_grouped1", align_bytes=64))
+        clear_window(1, sb.tile([P, ITEMS], F32, name="out_window1", tag="x_grouped1", align_bytes=64))
         clear_window(2, sb.tile([P, ITEMS], F32, name="out_window2", tag="x_codes", align_bytes=64))
 
         squares = []
@@ -218,6 +217,7 @@ def tile_attend_gtower_tnh_E_pl_kernel(tc, W, xT, G, hT, cf, ts, offs, out_0, ou
         quantize(w_grouped_middle[:], w_codes[:, P : 3 * P], w_scales[:, P : 3 * P], E4M3)
         quantize(dz_grouped[:, halves[1], :], dz_codes[:, halves[1]], dz_scales[:, halves[1]], E5M2)
         quantize(w_grouped3[:], w_codes[:, 3 * P :], w_scales[:, 3 * P :], E4M3)
+        clear_window(3, sb.tile([P, ITEMS], F32, name="out_window3", tag="w_grouped3", align_bytes=64))
 
         steps = [(0, 0), (0, 1), (2, 0), (2, 1)]
         places = [(0, halves[0]), (1, halves[0]), (1, halves[1]), (2, halves[0])]

@@ -270,7 +270,7 @@ def tile_attend_gtower_tnh_E_pl_kernel(tc, W, xT, G, hT, cf, ts, offs, out_0, ou
 
         y_grouped = [sb.tile([P, CHUNK, LANES], BF16, name="y_grouped%d" % c, align_bytes=64) for c in range(CHUNKS)]
         y_codes = sb.tile([P, ITEMS], U32, name="y_codes", align_bytes=64)
-        y_scales = sb.tile([P, 2 * CHUNK], U8, name="y_scales", align_bytes=64)
+        y_scales = sb.tile([P, CHUNK], U8, name="y_scales", align_bytes=64)
         words = out_1[0].rearrange("p n t -> p (n t)").bitcast(I32)
 
         def interleave(copy, c, columns):
@@ -280,8 +280,7 @@ def tile_attend_gtower_tnh_E_pl_kernel(tc, W, xT, G, hT, cf, ts, offs, out_0, ou
             )
 
         def quantize_y(c, columns):
-            plane = y_scales[4 * (c // 2) : P, chunks[c % 2]]
-            quantize(y_grouped[c][:, columns, :], y_codes[:, chunks[c]][:, columns], plane[:, columns], E4M3)
+            quantize(y_grouped[c][:, columns, :], y_codes[:, chunks[c]][:, columns], y_scales[4 * c : P, columns], E4M3)
 
         def store_codes(first, last):
             columns = slice(first * CHUNK, last * CHUNK)
@@ -299,16 +298,18 @@ def tile_attend_gtower_tnh_E_pl_kernel(tc, W, xT, G, hT, cf, ts, offs, out_0, ou
         interleave(nc.vector.tensor_copy, 0, whole)
         interleave(nc.vector.tensor_copy, 1, whole)
         quantize_y(0, whole)
-        interleave(nc.vector.tensor_copy, 2, whole)
+        interleave(nc.vector.tensor_copy, 2, low)
         quantize_y(1, whole)
         store_codes(0, 2)
-        quantize_y(2, whole)
+        interleave(nc.vector.tensor_copy, 2, high)
+        quantize_y(2, low)
+        quantize_y(2, high)
         store_codes(2, 3)
         quantize_y(3, low)
         quantize_y(3, high)
         store_codes(3, 4)
 
-        scale_rows = out_2[0].bitcast(I32).rearrange("r (a n) -> a r n", a=2)
+        scale_rows = out_2[0].bitcast(I32).rearrange("r (c n) -> c r n", c=CHUNKS)
         for q in range(QUADRANTS):
             queue = nc.sync if q % 2 == 0 else nc.scalar
-            queue.dma_start(scale_rows[:, 4 * q : 4 * q + 4, :], y_scales[32 * q : 32 * q + 8, :].bitcast(I32))
+            queue.dma_start(scale_rows[:, 4 * q : 4 * q + 4, :], y_scales[32 * q : 32 * q + 16, :].bitcast(I32))

@@ -219,14 +219,16 @@ def tile_attend_gtower_tnh_E_pl_kernel(tc, W, xT, G, hT, cf, ts, offs, out_0, ou
         quantize(w_grouped3[:], w_codes[:, 3 * P :], w_scales[:, 3 * P :], E4M3)
         clear_window(3, sb.tile([P, ITEMS], F32, name="out_window3", tag="w_grouped3", align_bytes=64))
 
-        steps = [(0, 0), (0, 1), (2, 0), (2, 1)]
-        places = [(0, halves[0]), (1, halves[0]), (1, halves[1]), (2, halves[0])]
-        sums = [[bank(2 + 2 * n + e) for n in range(3)] for e in range(2)]
-        for (lane, v), (n, columns) in zip(steps, places):
-            for e in range(2):
-                product(
-                    sums[e][n][:, columns], w_codes, w_scales, lane + e, dz_codes[:, halves[v]], dz_scales[:, halves[v]]
-                )
+        sums = {}
+        shared_bank = bank(5)
+        for pair in range(2):
+            for v in range(2):
+                for t in (2 * pair, 2 * pair + 1):
+                    if (t, v) in ((1, 1), (3, 0)):
+                        sums.update({(t, v): shared_bank[:, halves[pair]]})
+                    else:
+                        sums.update({(t, v): bank((2 + 4 * pair + 2 * v + t % 2) % 8)[:, :HALF]})
+                    product(sums[t, v], w_codes, w_scales, t, dz_codes[:, halves[v]], dz_scales[:, halves[v]])
 
         def store_lane(t):
             nc.sync.dma_start(out_rows[:, t, :], out_window[t][:])
@@ -247,25 +249,29 @@ def tile_attend_gtower_tnh_E_pl_kernel(tc, W, xT, G, hT, cf, ts, offs, out_0, ou
             nc.vector.tensor_copy(out_window[t][:].indirect(part_of_list), de)
 
         chunks = [slice(c * CHUNK, (c + 1) * CHUNK) for c in range(CHUNKS)]
-        copies = (nc.scalar.copy, nc.vector.tensor_copy)
-        scatters = (scalar_scatter, vector_scatter)
-        de_rest = []
-        for e in range(2):
-            de_first = sb.tile([P, HALF], F32, name="de_first%d" % e)
-            de_rest.append(sb.tile([P, 3 * HALF], F32, name="de_rest%d" % e))
-            copies[e](de_first[:], sums[e][0][:, halves[0]])
-            scatters[e](e, halves_of_list[0], de_first[:])
-            copies[e](de_rest[e][:, :SLOTS], sums[e][1][:])
-            copies[e](de_rest[e][:, SLOTS:], sums[e][2][:, halves[0]])
-            scatters[e](e, halves_of_list[1], de_rest[e][:, :HALF])
-            store_lane(e)
+        de_scalar = sb.tile([P, 2 * SLOTS], F32, name="de_scalar")
+        quarters = [de_scalar[:, n * HALF : (n + 1) * HALF] for n in range(4)]
+        nc.scalar.copy(quarters[0], sums[0, 0])
+        scalar_scatter(0, halves_of_list[0], quarters[0])
+        nc.scalar.copy(quarters[1], sums[0, 1])
+        nc.scalar.copy(quarters[2], sums[2, 0])
+        scalar_scatter(0, halves_of_list[1], quarters[1])
+        store_lane(0)
+        nc.scalar.copy(quarters[3], sums[2, 1])
+        de_vector = sb.tile([P, 2 * SLOTS], F32, name="de_vector")
+        nc.vector.tensor_copy(de_vector[:, :HALF], sums[1, 0])
+        vector_scatter(1, halves_of_list[0], de_vector[:, :HALF])
+        nc.vector.tensor_copy(de_vector[:, HALF : 3 * HALF], shared_bank[:])
+        nc.vector.tensor_copy(de_vector[:, 3 * HALF :], sums[3, 1])
+        vector_scatter(1, halves_of_list[1], de_vector[:, HALF:SLOTS])
+        store_lane(1)
         for t in range(2):
             round_lane(gpsimd_round, t, 0, 3)
-        scalar_scatter(2, halves_of_list[0], de_rest[0][:, HALF:SLOTS])
+        scalar_scatter(2, halves_of_list[0], quarters[2])
         round_lane(nc.scalar.copy, 0, 3, 4)
-        scalar_scatter(2, halves_of_list[1], de_rest[0][:, SLOTS:])
+        scalar_scatter(2, halves_of_list[1], quarters[3])
         store_lane(2)
-        vector_scatter(3, offsets[:], de_rest[1][:, HALF:])
+        vector_scatter(3, offsets[:], de_vector[:, SLOTS:])
         store_lane(3)
 
         y_grouped = [sb.tile([P, CHUNK, LANES], BF16, name="y_grouped%d" % c, align_bytes=64) for c in range(CHUNKS)]
@@ -283,7 +289,7 @@ def tile_attend_gtower_tnh_E_pl_kernel(tc, W, xT, G, hT, cf, ts, offs, out_0, ou
             quantize(y_grouped[c][:, columns, :], y_codes[:, chunks[c]][:, columns], y_scales[4 * c : P, columns], E4M3)
 
         def store_codes(first, last):
-            columns = slice(first * CHUNK, last * CHUNK)
+            columns = slice(first * CHUNK // 2, last * CHUNK // 2)
             nc.sync.dma_start(words[:, columns], y_codes[:, columns].bitcast(I32))
 
         whole, low, high = slice(0, CHUNK), slice(0, CHUNK // 2), slice(CHUNK // 2, CHUNK)
@@ -300,14 +306,15 @@ def tile_attend_gtower_tnh_E_pl_kernel(tc, W, xT, G, hT, cf, ts, offs, out_0, ou
         quantize_y(0, whole)
         interleave(nc.vector.tensor_copy, 2, low)
         quantize_y(1, whole)
-        store_codes(0, 2)
+        store_codes(0, 4)
         interleave(nc.vector.tensor_copy, 2, high)
         quantize_y(2, low)
         quantize_y(2, high)
-        store_codes(2, 3)
+        store_codes(4, 6)
         quantize_y(3, low)
+        store_codes(6, 7)
         quantize_y(3, high)
-        store_codes(3, 4)
+        store_codes(7, 8)
 
         scale_rows = out_2[0].bitcast(I32).rearrange("r (c n) -> c r n", c=CHUNKS)
         for q in range(QUADRANTS):

@@ -29,6 +29,9 @@ VECTOR_SLOTS = 384
 TS_ROW = P - 1
 CHUNK = 512
 CHUNKS = ITEMS // CHUNK
+PIECE = CHUNK // 2
+TURNED = 3
+COPIED = ITEMS - TURNED * PIECE
 
 
 def tile_attend_gtower_tnh_E_pl_kernel(tc, W, xT, G, hT, cf, ts, offs, out_0, out_1, out_2):
@@ -233,11 +236,13 @@ def tile_attend_gtower_tnh_E_pl_kernel(tc, W, xT, G, hT, cf, ts, offs, out_0, ou
         def store_lane(t):
             nc.sync.dma_start(out_rows[:, t, :], out_window[t][:])
 
-        y_row = sb.tile([P, LANES * ITEMS], BF16, name="y_row", align_bytes=64)
-        y_lanes = y_row[:].rearrange("p (c t n) -> p c t n", c=CHUNKS, t=LANES)
+        y_row = sb.tile([P, 3 * LANES * CHUNK], BF16, name="y_row", align_bytes=64)
+        y_lanes = y_row[:].rearrange("p (c t n) -> p c t n", c=3, t=LANES)
+        whole, low, high = slice(0, CHUNK), slice(0, PIECE), slice(PIECE, CHUNK)
 
-        def round_lane(copy, t, first, last):
-            copy(y_lanes[:, first:last, t, :], out_window[t][:].rearrange("p (c n) -> p c n", c=CHUNKS)[:, first:last, :])
+        def round_lane(copy, t, first, last, columns):
+            window = out_window[t][:].rearrange("p (c n) -> p c n", c=CHUNKS)
+            copy(y_lanes[:, first:last, t, columns], window[:, first:last, columns])
 
         def gpsimd_round(rounded, values):
             nc.gpsimd.tensor_scalar(rounded, values, 1.0, 0.0, ALU.mult, ALU.add)
@@ -247,6 +252,22 @@ def tile_attend_gtower_tnh_E_pl_kernel(tc, W, xT, G, hT, cf, ts, offs, out_0, ou
 
         def vector_scatter(t, part_of_list, de):
             nc.vector.tensor_copy(out_window[t][:].indirect(part_of_list), de)
+
+        y_pairs = [sb.tile([P, 2, 2, P, 2], BF16, name="y_pairs%d" % n, align_bytes=64) for n in range(TURNED)]
+
+        def turn_lanes(n, u):
+            turned = bank(2 + TURNED * u + n)
+            for b in range(2):
+                for e in range(2):
+                    first = COPIED + n * PIECE + b * P
+                    run = 2 * b + e
+                    nc.tensor.transpose(
+                        turned[:, run * P : (run + 1) * P], out_window[2 * u + e][:, first : first + P], ident[:]
+                    )
+            return turned
+
+        def round_pairs(n, u, turned):
+            nc.scalar.copy(y_pairs[n][:, :, u, :, :], turned[:].rearrange("m (b e p) -> m b p e", b=2, e=2))
 
         chunks = [slice(c * CHUNK, (c + 1) * CHUNK) for c in range(CHUNKS)]
         de_scalar = sb.tile([P, 2 * SLOTS], F32, name="de_scalar")
@@ -266,21 +287,24 @@ def tile_attend_gtower_tnh_E_pl_kernel(tc, W, xT, G, hT, cf, ts, offs, out_0, ou
         vector_scatter(1, halves_of_list[1], de_vector[:, HALF:SLOTS])
         store_lane(1)
         for t in range(2):
-            round_lane(gpsimd_round, t, 0, 3)
+            round_lane(gpsimd_round, t, 0, 2, whole)
+            round_lane(gpsimd_round, t, 2, 3, low)
+        turned_low = [turn_lanes(n, 0) for n in range(TURNED)]
         scalar_scatter(2, halves_of_list[0], quarters[2])
-        round_lane(nc.scalar.copy, 0, 3, 4)
+        round_pairs(0, 0, turned_low[0])
         scalar_scatter(2, halves_of_list[1], quarters[3])
         store_lane(2)
         vector_scatter(3, offsets[:], de_vector[:, SLOTS:])
         store_lane(3)
+        turned_high = [turn_lanes(n, 1) for n in range(TURNED)]
 
         y_grouped = [sb.tile([P, CHUNK, LANES], BF16, name="y_grouped%d" % c, align_bytes=64) for c in range(CHUNKS)]
         y_codes = sb.tile([P, ITEMS], U32, name="y_codes", align_bytes=64)
         y_scales = sb.tile([P, CHUNK], U8, name="y_scales", align_bytes=64)
         words = out_1[0].rearrange("p n t -> p (n t)").bitcast(I32)
 
-        def interleave(copy, c, columns):
-            copy(
+        def interleave(c, columns):
+            nc.vector.tensor_copy(
                 y_grouped[c][:, columns, :].rearrange("p (n i) t -> p n t i", i=4),
                 y_lanes[:, c, :, columns].rearrange("p t (n i) -> p n t i", i=4),
             )
@@ -289,32 +313,29 @@ def tile_attend_gtower_tnh_E_pl_kernel(tc, W, xT, G, hT, cf, ts, offs, out_0, ou
             quantize(y_grouped[c][:, columns, :], y_codes[:, chunks[c]][:, columns], y_scales[4 * c : P, columns], E4M3)
 
         def store_codes(first, last):
-            columns = slice(first * CHUNK // 2, last * CHUNK // 2)
+            columns = slice(first * CHUNK, last * CHUNK)
             nc.sync.dma_start(words[:, columns], y_codes[:, columns].bitcast(I32))
 
-        whole, low, high = slice(0, CHUNK), slice(0, CHUNK // 2), slice(CHUNK // 2, CHUNK)
-        for c in range(CHUNKS):
-            round_lane(nc.scalar.copy, 2, c, c + 1)
-        for c in range(CHUNKS - 1):
-            round_lane(nc.vector.tensor_copy, 3, c, c + 1)
-        round_lane(nc.scalar.copy, 1, 3, 4)
-        round_lane(nc.scalar.copy, 3, 3, 4)
-        interleave(nc.scalar.copy, 3, low)
-        interleave(nc.scalar.copy, 3, high)
-        interleave(nc.vector.tensor_copy, 0, whole)
-        interleave(nc.vector.tensor_copy, 1, whole)
+        for c in range(2):
+            round_lane(nc.scalar.copy, 2, c, c + 1, whole)
+            round_lane(nc.vector.tensor_copy, 3, c, c + 1, whole)
+        round_pairs(1, 0, turned_low[1])
+        round_pairs(0, 1, turned_high[0])
+        round_lane(nc.scalar.copy, 2, 2, 3, low)
+        round_lane(nc.vector.tensor_copy, 3, 2, 3, low)
+        round_pairs(1, 1, turned_high[1])
+        round_pairs(2, 0, turned_low[2])
+        round_pairs(2, 1, turned_high[2])
+        for n, (c, columns) in enumerate(((2, high), (3, low), (3, high))):
+            group_pairs(y_grouped[c][:, columns, :], turn_pairs([y_pairs[n][:]], n), 2)
+        interleave(0, whole)
+        interleave(1, whole)
         quantize_y(0, whole)
-        interleave(nc.vector.tensor_copy, 2, low)
-        quantize_y(1, whole)
-        store_codes(0, 4)
-        interleave(nc.vector.tensor_copy, 2, high)
-        quantize_y(2, low)
-        quantize_y(2, high)
-        store_codes(4, 6)
-        quantize_y(3, low)
-        store_codes(6, 7)
-        quantize_y(3, high)
-        store_codes(7, 8)
+        interleave(2, low)
+        for c in range(1, CHUNKS):
+            quantize_y(c, low)
+            quantize_y(c, high)
+            store_codes(0 if c == 1 else c, c + 1)
 
         scale_rows = out_2[0].bitcast(I32).rearrange("r (c n) -> c r n", c=CHUNKS)
         for q in range(QUADRANTS):

@@ -313,7 +313,7 @@ def tile_attend_gtower_tnh_E_pl_kernel(tc, W, xT, G, hT, cf, ts, offs, out_0, ou
             quantize(y_grouped[c][:, columns, :], y_codes[:, chunks[c]][:, columns], y_scales[4 * c : P, columns], E4M3)
 
         def store_codes(first, last):
-            columns = slice(first * CHUNK, last * CHUNK)
+            columns = slice(first * PIECE, last * PIECE)
             nc.sync.dma_start(words[:, columns], y_codes[:, columns].bitcast(I32))
 
         for c in range(2):
@@ -332,10 +332,15 @@ def tile_attend_gtower_tnh_E_pl_kernel(tc, W, xT, G, hT, cf, ts, offs, out_0, ou
         interleave(1, whole)
         quantize_y(0, whole)
         interleave(2, low)
-        for c in range(1, CHUNKS):
-            quantize_y(c, low)
-            quantize_y(c, high)
-            store_codes(0 if c == 1 else c, c + 1)
+        quantize_y(1, low)
+        store_codes(0, 3)
+        quantize_y(1, high)
+        quantize_y(2, low)
+        quantize_y(2, high)
+        store_codes(3, 6)
+        quantize_y(3, low)
+        quantize_y(3, high)
+        store_codes(6, 8)
 
         scale_rows = out_2[0].bitcast(I32).rearrange("r (c n) -> c r n", c=CHUNKS)
         for q in range(QUADRANTS):

@@ -31,7 +31,7 @@ CHUNK = 512
 CHUNKS = ITEMS // CHUNK
 PIECE = CHUNK // 2
 TURNED = 3
-COPIED = ITEMS - TURNED * PIECE
+TURNED_PIECES = (4, 6, 7)
 
 
 def tile_attend_gtower_tnh_E_pl_kernel(tc, W, xT, G, hT, cf, ts, offs, out_0, out_1, out_2):
@@ -259,7 +259,7 @@ def tile_attend_gtower_tnh_E_pl_kernel(tc, W, xT, G, hT, cf, ts, offs, out_0, ou
             turned = bank(2 + TURNED * u + n)
             for b in range(2):
                 for e in range(2):
-                    first = COPIED + n * PIECE + b * P
+                    first = TURNED_PIECES[n] * PIECE + b * P
                     run = 2 * b + e
                     nc.tensor.transpose(
                         turned[:, run * P : (run + 1) * P], out_window[2 * u + e][:, first : first + P], ident[:]
@@ -288,7 +288,7 @@ def tile_attend_gtower_tnh_E_pl_kernel(tc, W, xT, G, hT, cf, ts, offs, out_0, ou
         store_lane(1)
         for t in range(2):
             round_lane(gpsimd_round, t, 0, 2, whole)
-            round_lane(gpsimd_round, t, 2, 3, low)
+            round_lane(gpsimd_round, t, 2, 3, high)
         turned_low = [turn_lanes(n, 0) for n in range(TURNED)]
         scalar_scatter(2, halves_of_list[0], quarters[2])
         round_pairs(0, 0, turned_low[0])
@@ -321,23 +321,23 @@ def tile_attend_gtower_tnh_E_pl_kernel(tc, W, xT, G, hT, cf, ts, offs, out_0, ou
             round_lane(nc.vector.tensor_copy, 3, c, c + 1, whole)
         round_pairs(1, 0, turned_low[1])
         round_pairs(0, 1, turned_high[0])
-        round_lane(nc.scalar.copy, 2, 2, 3, low)
-        round_lane(nc.vector.tensor_copy, 3, 2, 3, low)
+        round_lane(nc.scalar.copy, 2, 2, 3, high)
+        round_lane(nc.vector.tensor_copy, 3, 2, 3, high)
         round_pairs(1, 1, turned_high[1])
         round_pairs(2, 0, turned_low[2])
         round_pairs(2, 1, turned_high[2])
-        for n, (c, columns) in enumerate(((2, high), (3, low), (3, high))):
+        for n, (c, columns) in enumerate(((2, low), (3, low), (3, high))):
             group_pairs(y_grouped[c][:, columns, :], turn_pairs([y_pairs[n][:]], n), 2)
         interleave(0, whole)
         interleave(1, whole)
-        quantize_y(0, whole)
-        interleave(2, low)
-        quantize_y(1, low)
-        store_codes(0, 3)
-        quantize_y(1, high)
+        for c in range(2):
+            quantize_y(c, low)
+            quantize_y(c, high)
+        store_codes(0, 4)
+        interleave(2, high)
         quantize_y(2, low)
         quantize_y(2, high)
-        store_codes(3, 6)
+        store_codes(4, 6)
         quantize_y(3, low)
         quantize_y(3, high)
         store_codes(6, 8)

from contextlib import ExitStack

import concourse.mybir as mybir
from concourse.masks import make_identity

F32 = mybir.dt.float32
BF16 = mybir.dt.bfloat16
I32 = mybir.dt.int32
U32 = mybir.dt.uint32
U16 = mybir.dt.uint16
U8 = mybir.dt.uint8
E4M3 = mybir.dt.float8_e4m3fn_x4
E5M2 = mybir.dt.float8_e5m2_x4
ALU = mybir.AluOpType
ACT = mybir.ActivationFunctionType

P = 128
LANES = 4
K = P * LANES
SLOTS = 512
ITEMS = 2048
QUADRANTS = 4
FLOPS = 2 * 2 * K * K * SLOTS
BYTES = 4 * (3 * K * K + K * ITEMS + K + ITEMS) + 2 * P * SLOTS // 16 + 4 * K * ITEMS + K * ITEMS + 16 * ITEMS

BLOCKS = SLOTS // P
HALF = SLOTS // 2
VECTOR_SLOTS = 384
TS_ROW = P - 1
CHUNK = 512
CHUNKS = ITEMS // CHUNK
PIECE = CHUNK // 2
TURNED = 3
TURNED_PIECES = (4, 6, 7)


def tile_attend_gtower_tnh_E_pl_kernel(tc, W, xT, G, hT, cf, ts, offs, out_0, out_1, out_2):
    nc = tc.nc
    with ExitStack() as ctx:
        sb = ctx.enter_context(tc.tile_pool(name="sb", bufs=1))
        psum = ctx.enter_context(tc.psum_pool(name="psum", bufs=1))

        def bank(n):
            return psum.tile([P, SLOTS], F32, name="bank%d" % n)

        x_rows = xT.rearrange("(m t) k -> m t k", t=LANES)
        w_rows = W.rearrange("(m t) k -> m t k", t=LANES)
        h_rows = hT.rearrange("(p t) n -> p t n", t=LANES)
        out_rows = out_0.rearrange("(p t) n -> p t n", t=LANES)
        halves = [slice(v * HALF, (v + 1) * HALF) for v in range(2)]

        offsets = sb.tile([P, SLOTS // 16], U16, name="offsets")
        halves_of_list = [offsets[:, v * HALF // 16 : (v + 1) * HALF // 16] for v in range(2)]
        ts_window = sb.tile([P, ITEMS], F32, name="ts_window")
        x_raw = [sb.tile([P, 2, K], F32, name="x_raw%d" % v) for v in range(2)]
        cf_lanes = sb.tile([P, LANES], F32, name="cf_lanes")
        g_raw = sb.tile([P, LANES, SLOTS], F32, name="g_raw", align_bytes=64)
        h_window = [sb.tile([P, ITEMS], F32, name="h_window%d" % t, align_bytes=64) for t in range(LANES)]
        w_raw = [sb.tile([P, K], F32, name="w_raw%d" % t, align_bytes=64) for t in range(LANES)]

        nc.sync.dma_start(x_raw[0][:], x_rows[:, 0:2, :])
        nc.sync.dma_start(cf_lanes[:], cf.rearrange("(p t) o -> p (t o)", t=LANES))
        nc.sync.dma_start(ts_window[TS_ROW:P, :], ts[0:1, :])
        nc.sync.dma_start(offsets[:], offs)
        nc.sync.dma_start(x_raw[1][:], x_rows[:, 2:4, :])
        nc.sync.dma_start(g_raw[:], G.rearrange("(p j) i -> p j i", j=LANES))
        for t in range(LANES - 1):
            nc.sync.dma_start(h_window[t][:], h_rows[:, t, :])
        nc.sync.dma_start(w_raw[0][:], w_rows[:, 0, :])
        nc.sync.dma_start(h_window[LANES - 1][:], h_rows[:, LANES - 1, :])
        for t in range(1, LANES):
            nc.sync.dma_start(w_raw[t][:], w_rows[:, t, :])

        nc.vector.memset(ts_window[0:TS_ROW, :], 0.0)
        out_window = {0: sb.tile([P, ITEMS], F32, name="out_window0")}
        nc.vector.memset(out_window[0][:], 0.0)

        def clear_window(t, window):
            out_window.update({t: window})
            nc.gpsimd.memset(window[:], 0.0)

        minus_cf = sb.tile([P, LANES], F32, name="minus_cf")
        nc.scalar.activation(minus_cf[:], cf_lanes[:], ACT.Copy, scale=-1.0)

        ident = sb.tile([P, P], F32, name="ident")
        make_identity(nc, ident[:])

        def quantize(grouped, codes, scales, fmt):
            nc.vector.quantize_mx(out=codes.bitcast(fmt), scales=scales, in_=grouped.rearrange("p c j -> p (c j)"))

        def round_rows(copy, rounded, raw):
            copy(rounded.rearrange("m t u p e -> m t p u e"), raw.rearrange("m t (p u e) -> m t p u e", u=2, e=2))

        def turn_pairs(rounded_parts, bank_number):
            runs = []
            for part in rounded_parts:
                part_pairs = part.rearrange("m t u p e -> m (t u p e)").bitcast(F32)
                runs.extend(part_pairs[:, n * P : (n + 1) * P] for n in range(2 * part.shape[1]))
            turned = bank(bank_number)
            for run in range(len(runs)):
                nc.tensor.transpose(turned[:, run * P : (run + 1) * P], runs[run], ident[:])
            return turned

        def group_pairs(grouped, turned, lanes):
            grouped_pairs = grouped.rearrange("p c j -> p (c j)").bitcast(F32)
            nc.scalar.copy(
                grouped_pairs.rearrange("p (t m u) -> p t m u", t=lanes, u=2),
                turned[:, 0 : 2 * lanes * P].rearrange("p (t u m) -> p t m u", t=lanes, u=2),
            )

        ts_listed = sb.tile([P, SLOTS], F32, name="ts_listed")
        nc.scalar.activation(ts_listed[:], ts_window[:].indirect(offsets[:]), ACT.Copy)

        x_codes = sb.tile([P, K], U32, name="x_codes", align_bytes=64)
        x_scales = sb.tile([P, K], U8, name="x_scales", align_bytes=64)
        x_grouped = []
        for v in range(2):
            x_rounded = sb.tile([P, 2, 2, P, 2], BF16, name="x_rounded%d" % v, align_bytes=64)
            round_rows(nc.vector.tensor_copy, x_rounded[:], x_raw[v][:])
            x_grouped.append(sb.tile([P, 2 * P, LANES], BF16, name="x_grouped%d" % v, align_bytes=64))
            group_pairs(x_grouped[v][:], turn_pairs([x_rounded[:]], 2 + v), 2)

        ts_bank = bank(0)
        for b in range(BLOCKS):
            nc.tensor.transpose(ts_bank[:, b * P : (b + 1) * P], ts_listed[:, b * P : (b + 1) * P], ident[:])
        ts_columns = sb.tile([P, BLOCKS], F32, name="ts_columns")
        nc.scalar.copy(ts_columns[:], ts_bank[:, TS_ROW::P])

        g_grouped = sb.tile([P, SLOTS, LANES], BF16, name="g_grouped", tag="x_rounded1", align_bytes=64)
        g_by_slot = g_raw[:].rearrange("p j i -> p i j")
        nc.vector.tensor_copy(g_grouped[:, :VECTOR_SLOTS, :], g_by_slot[:, :VECTOR_SLOTS, :])
        nc.scalar.copy(g_grouped[:, VECTOR_SLOTS:, :], g_by_slot[:, VECTOR_SLOTS:, :])
        g_codes = sb.tile([P, SLOTS], U32, name="g_codes", align_bytes=64)
        g_scales = sb.tile([P, SLOTS], U8, name="g_scales", align_bytes=64)
        quantize(x_grouped[0][:], x_codes[:, halves[0]], x_scales[:, halves[0]], E4M3)
        quantize(g_grouped[:], g_codes[:], g_scales[:], E5M2)
        quantize(x_grouped[1][:], x_codes[:, halves[1]], x_scales[:, halves[1]], E4M3)

        spread_bank = bank(2)
        for b in range(BLOCKS):
            nc.tensor.transpose(
                spread_bank[:, b * P : (b + 1) * P], ts_columns[:, b : b + 1].to_broadcast([P, P]), ident[:]
            )
        ts_spread = sb.tile([P, SLOTS], F32, name="ts_spread")
        nc.scalar.copy(ts_spread[:], spread_bank[:])

        def product(sums, codes, scales, lane, e5_codes, e5_scales):
            rows = slice(lane * P, (lane + 1) * P)
            nc.tensor.matmul_mx(
                out=sums,
                lhsT=codes[:, rows].bitcast(E4M3),
                lhsT_scale=scales[:, rows],
                rhs=e5_codes.bitcast(E5M2),
                rhs_scale=e5_scales,
                start=True,
                stop=True,
            )

        factors = []
        for t in range(LANES):
            dv = bank(LANES + t)
            product(dv[:], x_codes, x_scales, t, g_codes[:], g_scales[:])
            factor = sb.tile([P, SLOTS], F32, name="factor%d" % t)
            nc.vector.scalar_tensor_tensor(factor[:], dv[:], minus_cf[:, t : t + 1], ts_spread[:], ALU.mult, ALU.mult)
            factors.append(factor)

        clear_window(1, sb.tile([P, ITEMS], F32, name="out_window1", tag="x_grouped1", align_bytes=64))
        clear_window(2, sb.tile([P, ITEMS], F32, name="out_window2", tag="x_codes", align_bytes=64))

        squares = []
        for t in range(LANES - 1):
            h = sb.tile([P, SLOTS], F32, name="h%d" % t, tag="g_raw" if t == 0 else "h%d" % t, align_bytes=64)
            nc.scalar.activation(h[:], h_window[t][:].indirect(offsets[:]), ACT.Copy)
            h_squared = sb.tile([P, SLOTS], F32, name="h_squared%d" % t)
            nc.scalar.activation(h_squared[:], h[:], ACT.Square)
            squares.append(h_squared)

        def slope_times(dz_lane, square, factor):
            nc.vector.scalar_tensor_tensor(dz_lane, square, 1.0, factor, ALU.subtract, ALU.mult)

        dz_low = sb.tile([P, 2, SLOTS], BF16, name="dz_low")
        for t in range(2):
            slope_times(dz_low[:, t, :], squares[t][:], factors[t][:])

        def round_w(t, copy):
            rounded = sb.tile([P, 2, P, 2], BF16, name="w_rounded%d" % t, align_bytes=64)
            copy(rounded[:].rearrange("m u p e -> m p u e"), w_raw[t][:].rearrange("m (p u e) -> m p u e", u=2, e=2))
            return rounded[:].unsqueeze(1)

        w_grouped0 = sb.tile([P, P, LANES], BF16, name="w_grouped0", align_bytes=64)
        group_pairs(w_grouped0[:], turn_pairs([round_w(0, nc.vector.tensor_copy)], 0), 1)
        dz_grouped = sb.tile([P, SLOTS, LANES], BF16, name="dz_grouped", tag="w_raw0", align_bytes=64)
        nc.vector.tensor_copy(dz_grouped[:, :, 0:2], dz_low[:].rearrange("p t i -> p i t"))
        dz_high = sb.tile([P, 2, SLOTS], BF16, name="dz_high")
        slope_times(dz_high[:, 0, :], squares[2][:], factors[2][:])

        h_last = [sb.tile([P, HALF], F32, name="h_last%d" % v) for v in range(2)]
        nc.vector.tensor_copy(h_last[0][:], h_window[LANES - 1][:].indirect(halves_of_list[0]))
        nc.scalar.activation(h_last[1][:], h_window[LANES - 1][:].indirect(halves_of_list[1]), ACT.Copy)
        w_codes = sb.tile([P, K], U32, name="w_codes", tag="h_window3", align_bytes=64)
        w_scales = sb.tile([P, K], U8, name="w_scales", align_bytes=64)
        quantize(w_grouped0[:], w_codes[:, :P], w_scales[:, :P], E4M3)
        turned_middle = turn_pairs([round_w(t, nc.vector.tensor_copy) for t in (1, 2)], 1)
        for v in range(2):
            last_squared = sb.tile([P, HALF], F32, name="last_squared%d" % v)
            nc.scalar.activation(last_squared[:], h_last[v][:], ACT.Square)
            slope_times(dz_high[:, 1, halves[v]], last_squared[:], factors[LANES - 1][:, halves[v]])
        turned_last = turn_pairs([round_w(3, nc.scalar.copy)], 0)
        w_grouped_middle = sb.tile([P, 2 * P, LANES], BF16, name="w_grouped_middle", tag="w_raw3", align_bytes=64)
        group_pairs(w_grouped_middle[:], turned_middle, 2)
        w_grouped3 = sb.tile([P, P, LANES], BF16, name="w_grouped3", align_bytes=64)
        group_pairs(w_grouped3[:], turned_last, 1)
        for v in range(2):
            nc.vector.tensor_copy(
                dz_grouped[:, halves[v], 2:LANES], dz_high[:, :, halves[v]].rearrange("p t i -> p i t")
            )
        dz_codes = sb.tile([P, SLOTS], U32, name="dz_codes", align_bytes=64)
        dz_scales = sb.tile([P, SLOTS], U8, name="dz_scales", align_bytes=64)
        quantize(dz_grouped[:, halves[0], :], dz_codes[:, halves[0]], dz_scales[:, halves[0]], E5M2)
        quantize(w_grouped_middle[:], w_codes[:, P : 3 * P], w_scales[:, P : 3 * P], E4M3)
        quantize(dz_grouped[:, halves[1], :], dz_codes[:, halves[1]], dz_scales[:, halves[1]], E5M2)
        quantize(w_grouped3[:], w_codes[:, 3 * P :], w_scales[:, 3 * P :], E4M3)
        clear_window(3, sb.tile([P, ITEMS], F32, name="out_window3", tag="w_grouped3", align_bytes=64))

        sums = {}
        shared_bank = bank(5)
        for pair in range(2):
            for v in range(2):
                for t in (2 * pair, 2 * pair + 1):
                    if (t, v) in ((1, 1), (3, 0)):
                        sums.update({(t, v): shared_bank[:, halves[pair]]})
                    else:
                        sums.update({(t, v): bank((2 + 4 * pair + 2 * v + t % 2) % 8)[:, :HALF]})
                    product(sums[t, v], w_codes, w_scales, t, dz_codes[:, halves[v]], dz_scales[:, halves[v]])

        def store_lane(t):
            nc.sync.dma_start(out_rows[:, t, :], out_window[t][:])

        y_row = sb.tile([P, 3 * LANES * CHUNK], BF16, name="y_row", align_bytes=64)
        y_lanes = y_row[:].rearrange("p (c t n) -> p c t n", c=3, t=LANES)
        whole, low, high = slice(0, CHUNK), slice(0, PIECE), slice(PIECE, CHUNK)

        def round_lane(copy, t, first, last, columns):
            window = out_window[t][:].rearrange("p (c n) -> p c n", c=CHUNKS)
            copy(y_lanes[:, first:last, t, columns], window[:, first:last, columns])

        def gpsimd_round(rounded, values):
            nc.gpsimd.tensor_scalar(rounded, values, 1.0, 0.0, ALU.mult, ALU.add)

        def scalar_scatter(t, part_of_list, de):
            nc.scalar.activation(out_window[t][:].indirect(part_of_list), de, ACT.Copy)

        def vector_scatter(t, part_of_list, de):
            nc.vector.tensor_copy(out_window[t][:].indirect(part_of_list), de)

        y_pairs = [sb.tile([P, 2, 2, P, 2], BF16, name="y_pairs%d" % n, align_bytes=64) for n in range(TURNED)]

        def turn_lanes(n, u):
            turned = bank(2 + TURNED * u + n)
            for b in range(2):
                for e in range(2):
                    first = TURNED_PIECES[n] * PIECE + b * P
                    run = 2 * b + e
                    nc.tensor.transpose(
                        turned[:, run * P : (run + 1) * P], out_window[2 * u + e][:, first : first + P], ident[:]
                    )
            return turned

        def round_pairs(n, u, turned):
            nc.scalar.copy(y_pairs[n][:, :, u, :, :], turned[:].rearrange("m (b e p) -> m b p e", b=2, e=2))

        chunks = [slice(c * CHUNK, (c + 1) * CHUNK) for c in range(CHUNKS)]
        de_scalar = sb.tile([P, 2 * SLOTS], F32, name="de_scalar")
        quarters = [de_scalar[:, n * HALF : (n + 1) * HALF] for n in range(4)]
        nc.scalar.copy(quarters[0], sums[0, 0])
        scalar_scatter(0, halves_of_list[0], quarters[0])
        nc.scalar.copy(quarters[1], sums[0, 1])
        nc.scalar.copy(quarters[2], sums[2, 0])
        scalar_scatter(0, halves_of_list[1], quarters[1])
        store_lane(0)
        nc.scalar.copy(quarters[3], sums[2, 1])
        de_vector = sb.tile([P, 2 * SLOTS], F32, name="de_vector")
        nc.vector.tensor_copy(de_vector[:, :HALF], sums[1, 0])
        vector_scatter(1, halves_of_list[0], de_vector[:, :HALF])
        nc.vector.tensor_copy(de_vector[:, HALF : 3 * HALF], shared_bank[:])
        nc.vector.tensor_copy(de_vector[:, 3 * HALF :], sums[3, 1])
        vector_scatter(1, halves_of_list[1], de_vector[:, HALF:SLOTS])
        store_lane(1)
        for t in range(2):
            round_lane(gpsimd_round, t, 0, 2, whole)
            round_lane(gpsimd_round, t, 2, 3, high)
        turned_low = [turn_lanes(n, 0) for n in range(TURNED)]
        scalar_scatter(2, halves_of_list[0], quarters[2])
        round_pairs(0, 0, turned_low[0])
        scalar_scatter(2, halves_of_list[1], quarters[3])
        store_lane(2)
        vector_scatter(3, offsets[:], de_vector[:, SLOTS:])
        store_lane(3)
        turned_high = [turn_lanes(n, 1) for n in range(TURNED)]

        y_grouped = [sb.tile([P, CHUNK, LANES], BF16, name="y_grouped%d" % c, align_bytes=64) for c in range(CHUNKS)]
        y_codes = sb.tile([P, ITEMS], U32, name="y_codes", align_bytes=64)
        y_scales = sb.tile([P, CHUNK], U8, name="y_scales", align_bytes=64)
        words = out_1[0].rearrange("p n t -> p (n t)").bitcast(I32)

        def interleave(c, columns):
            nc.vector.tensor_copy(
                y_grouped[c][:, columns, :].rearrange("p (n i) t -> p n t i", i=4),
                y_lanes[:, c, :, columns].rearrange("p t (n i) -> p n t i", i=4),
            )

        def quantize_y(c, columns):
            quantize(y_grouped[c][:, columns, :], y_codes[:, chunks[c]][:, columns], y_scales[4 * c : P, columns], E4M3)

        def store_codes(first, last):
            columns = slice(first * PIECE, last * PIECE)
            nc.sync.dma_start(words[:, columns], y_codes[:, columns].bitcast(I32))

        for c in range(2):
            round_lane(nc.scalar.copy, 2, c, c + 1, whole)
            round_lane(nc.vector.tensor_copy, 3, c, c + 1, whole)
        round_pairs(1, 0, turned_low[1])
        round_pairs(0, 1, turned_high[0])
        round_lane(nc.scalar.copy, 2, 2, 3, high)
        round_lane(nc.vector.tensor_copy, 3, 2, 3, high)
        round_pairs(1, 1, turned_high[1])
        round_pairs(2, 0, turned_low[2])
        round_pairs(2, 1, turned_high[2])
        for n, (c, columns) in enumerate(((2, low), (3, low), (3, high))):
            group_pairs(y_grouped[c][:, columns, :], turn_pairs([y_pairs[n][:]], n), 2)
        interleave(0, whole)
        interleave(1, whole)
        for c in range(2):
            quantize_y(c, low)
            quantize_y(c, high)
        store_codes(0, 4)
        interleave(2, high)
        quantize_y(2, low)
        quantize_y(2, high)
        store_codes(4, 6)
        quantize_y(3, low)
        quantize_y(3, high)
        store_codes(6, 8)

        scale_rows = out_2[0].bitcast(I32).rearrange("r (c n) -> c r n", c=CHUNKS)
        for q in range(QUADRANTS):
            queue = nc.sync if q % 2 == 0 else nc.scalar
            queue.dma_start(scale_rows[:, 4 * q : 4 * q + 4, :], y_scales[32 * q : 32 * q + 16, :].bitcast(I32))
